import numpy as np
import ml_dtypes


def mxq(x, axis, fmt="e4m3"):
    dtype, down = {"e4m3": (ml_dtypes.float8_e4m3fn, 7), "e5m2": (ml_dtypes.float8_e5m2, 14)}[fmt]
    v = np.moveaxis(np.asarray(x, np.float32).astype(ml_dtypes.bfloat16).astype(np.float64), axis, -1)
    blocks = v.reshape(v.shape[:-1] + (-1, 32))
    amax = np.abs(blocks).max(-1, keepdims=True)
    byte = np.maximum(np.where(amax > 0, np.frexp(amax)[1] - 1 + 127, 0) - down, 1)
    scale = np.exp2(byte - 127.0)
    codes = (blocks / scale).astype(np.float32).astype(dtype).astype(np.float64)
    return np.moveaxis((codes * scale).reshape(v.shape), -1, axis)


WIDE = False


def mx_kscale(k):
    if not WIDE:
        return np.ones(k)
    levels = np.array([18, -18])
    if k % 512:
        return np.exp2(np.random.permutation(np.resize(levels, k // 32))).repeat(32)
    a = np.empty((k // 512, 16))
    for p in range(k // 512):
        a[p, :8] = np.random.permutation(np.resize(levels, 8))
        for g in range(8):
            far = levels[np.abs(levels - a[p, g]) >= 10]
            a[p, g + 8] = far[np.random.randint(len(far))]
    return np.exp2(a.ravel()).repeat(32)


def f64(x):
    return np.asarray(x).astype(np.float64)


def striped(idx):
    return np.tile(np.asarray(idx).reshape(-1, 16).T, (8, 1)).astype(np.uint16)


def unstriped(offs):
    return offs[:16].T.reshape(-1).astype(np.int64)

def planes(y):
    n, m = y.shape
    v = y.astype(np.float32).astype(ml_dtypes.bfloat16).astype(np.float64).reshape(n // 32, 32, m)
    top = np.abs(v).max(1)
    byte = np.clip(np.where(top > 0, np.frexp(top)[1] - 1 + 127 - 7, 1), 1, 254)
    codes = (v * np.exp2(127.0 - byte)[:, None, :]).reshape(n, m).astype(np.float32).astype(ml_dtypes.float8_e4m3fn).view(np.uint8)
    words = codes.reshape(n // 512, 128, 4, m).transpose(0, 1, 3, 2)
    return np.ascontiguousarray(words), np.ascontiguousarray(byte.astype(np.uint8).reshape(n // 512, 16, m))


def setup_inputs():
    n = np.random.standard_normal
    uni = np.random.uniform
    idx = np.random.permutation(2048)[:512]
    f_d = mx_kscale(512)
    f_r = mx_kscale(512)
    return {
        "x1": (n((512, 512)) * f_d[:, None] * f_r[None, :]).astype(np.float32),
        "x2": (n((512, 512)) * f_d[:, None] * f_r[None, :]).astype(np.float32),
        "wT": (n((512, 2048)) / np.sqrt(512) / f_d[:, None]).astype(np.float32),
        "y1": (n((512, 512))).astype(np.float32),
        "u1": (uni(0.75, 1.3, (512, 1)) / f_r[:, None]).astype(np.float32),
        "w1": (uni(0.75, 1.3, (512, 1)) / np.sqrt(512)).astype(np.float32),
        "y2": (n((512, 512))).astype(np.float32),
        "u2": (uni(0.75, 1.3, (512, 1)) / f_r[:, None]).astype(np.float32),
        "w2": (uni(0.75, 1.3, (512, 1)) / np.sqrt(512)).astype(np.float32),
        "ts": np.tile(uni(0.75, 1.3, 2048), (128, 1)).astype(np.float32),
        "offs": striped(idx),
    }


def reference(x1, x2, wT, y1, u1, w1, y2, u2, w2, ts, offs):
    idx = unstriped(offs)
    wT_i = f64(wT)[:, idx]
    ts_i = f64(ts)[:1][:, idx]
    q_wT_i = mxq(wT_i, 0, "e4m3")
    a1 = mxq(f64(x1), 0, "e4m3").T @ q_wT_i
    g1 = f64(w1) * f64(u1) * ts_i * (f64(u1) * ts_i * a1 - f64(y1))
    a2 = mxq(f64(x2), 0, "e4m3").T @ q_wT_i
    g2 = f64(w2) * f64(u2) * ts_i * (f64(u2) * ts_i * a2 - f64(y2))
    d1 = mxq(f64(x1), 1, "e4m3") @ mxq(g1, 0, "e5m2")
    d2 = mxq(f64(x2), 1, "e4m3") @ mxq(g2, 0, "e5m2")
    dw = d1 + d2
    out_0 = np.zeros((512, 2048))
    out_0[:, idx] = dw
    return (out_0,) + planes(out_0)

@@ -1,0 +1,242 @@
+from contextlib import ExitStack
+
+import concourse.mybir as mybir
+from concourse.masks import make_identity
+
+F32 = mybir.dt.float32
+BF16 = mybir.dt.bfloat16
+I32 = mybir.dt.int32
+U32 = mybir.dt.uint32
+U16 = mybir.dt.uint16
+U8 = mybir.dt.uint8
+E4M3 = mybir.dt.float8_e4m3fn_x4
+E5M2 = mybir.dt.float8_e5m2_x4
+MULT = mybir.AluOpType.mult
+SUB = mybir.AluOpType.subtract
+COPY = mybir.ActivationFunctionType.Copy
+SQUARE = mybir.ActivationFunctionType.Square
+
+P = 128
+PACK = 4
+D, R, SLOTS, TOKENS = 512, 512, 512, 2048
+HEADS = 2
+CHUNKS = (256, 512, 512, 512, 256)
+EARLY = 3
+FLOPS = 4 * 2 * 512 * 512 * 512
+
+
+def weave(engine_copy, out, in_):
+    engine_copy(
+        out=out.rearrange("p (c i) t -> p c t i", i=4),
+        in_=in_.rearrange("p t (c i) -> p c t i", i=4),
+    )
+
+
+def tile_attend_gheads_sg_pl_kernel(
+    tc, x1, x2, wT, y1, u1, w1, y2, u2, w2, ts, offs, out_0, out_1, out_2
+):
+    nc = tc.nc
+    xs, ys, us, ws = (x1, x2), (y1, y2), (u1, u2), (w1, w2)
+
+    with ExitStack() as ctx:
+        keep = ctx.enter_context(tc.tile_pool(name="keep", bufs=1))
+        ring = ctx.enter_context(tc.tile_pool(name="ring", bufs=2))
+        psum = ctx.enter_context(tc.psum_pool(name="psum", bufs=1))
+
+        def quantize(src, name, fmt):
+            width = src.shape[1]
+            codes = keep.tile([P, width], U32, name=name + "_codes", align_bytes=64)
+            scales = keep.tile([P, width], U8, name=name + "_scales", align_bytes=64)
+            nc.vector.quantize_mx(
+                out=codes[:].bitcast(fmt), scales=scales[:], in_=src.rearrange("p c t -> p (c t)")
+            )
+            return codes, scales
+
+        def bank():
+            return psum.tile([P, 512], F32, name="bank", tag="bank", bufs=8)
+
+        offsets = keep.tile([P, SLOTS // 16], U16, name="offsets")
+        ident = keep.tile([P, P], F32, name="ident")
+        make_identity(nc, ident[:])
+
+        ts_pool = keep.tile([P, TOKENS], F32, name="ts_pool")
+        nc.vector.memset(ts_pool[:], 0.0)
+        windows = [keep.tile([P, TOKENS], F32, name="window%d" % j) for j in range(PACK)]
+        for j in range(PACK):
+            nc.gpsimd.memset(windows[j][:], 0.0)
+
+        x_raw = [keep.tile([P, PACK, R], F32, name="x_raw%d" % h) for h in range(HEADS)]
+        table = [keep.tile([P, TOKENS], F32, name="table%d" % j) for j in range(PACK)]
+        w_planes = wT.rearrange("(p j) c -> p j c", j=PACK)
+        for h in range(HEADS):
+            nc.sync.dma_start(out=x_raw[h][:], in_=xs[h].rearrange("(p j) r -> p j r", j=PACK))
+        nc.sync.dma_start(offsets[:], offs)
+        nc.sync.dma_start(out=ts_pool[0:1, :], in_=ts[0:1, :])
+        for j in range(PACK):
+            nc.sync.dma_start(out=table[j][:], in_=w_planes[:, j, :])
+        u_col = [keep.tile([P, PACK], F32, name="u_col%d" % h) for h in range(HEADS)]
+        w_col = [keep.tile([P, PACK], F32, name="w_col%d" % h) for h in range(HEADS)]
+        for h in range(HEADS):
+            nc.sync.dma_start(out=u_col[h][:], in_=us[h].rearrange("(m t) o -> m (t o)", t=PACK))
+            nc.sync.dma_start(out=w_col[h][:], in_=ws[h].rearrange("(m t) o -> m (t o)", t=PACK))
+        y_sb = [
+            [keep.tile([P, SLOTS], F32, name="y%d_%d" % (h, t)) for t in range(PACK)]
+            for h in range(HEADS)
+        ]
+        for h in range(HEADS):
+            y_rows = ys[h].rearrange("(m t) i -> m t i", t=PACK)
+            for t in range(PACK):
+                nc.sync.dma_start(out=y_sb[h][t][:], in_=y_rows[:, t, :])
+
+        x_d = [keep.tile([P, R, PACK], BF16, name="x_d%d" % h, align_bytes=64) for h in range(HEADS)]
+        weave(nc.vector.tensor_copy, x_d[0][:], x_raw[0][:])
+        weave(nc.scalar.copy, x_d[1][:], x_raw[1][:])
+
+        xd_q = [quantize(x_d[h][:], "xd%d" % h, E4M3) for h in range(HEADS)]
+
+        xr_q = []
+        for h in range(HEADS):
+            words = x_d[h][:].rearrange("p r j -> p (r j)").bitcast(F32)
+            x_r = keep.tile([P, D, PACK], BF16, name="x_r%d" % h, align_bytes=64)
+            for jj in range(2):
+                turned = bank()
+                for t in range(PACK):
+                    nc.tensor.transpose(
+                        turned[:, t * P:(t + 1) * P], words[:, 2 * t + jj:2 * R:8], ident[:]
+                    )
+                nc.scalar.copy(
+                    out=x_r[:, jj * 256:(jj + 1) * 256, :].rearrange("s (e p) t -> s e p t", e=2),
+                    in_=turned[:].bitcast(BF16).rearrange("s (t p e) -> s e p t", t=PACK, e=2),
+                )
+            xr_q.append(quantize(x_r[:], "xr%d" % h, E4M3))
+
+        ts_listed = keep.tile([P, SLOTS], F32, name="ts_listed")
+        nc.vector.tensor_copy(ts_listed[:], ts_pool[:].indirect(offsets[:]))
+        ts_turned = bank()
+        for b in range(4):
+            nc.tensor.transpose(ts_turned[:, b * P:(b + 1) * P], ts_listed[:, b * P:(b + 1) * P], ident[:])
+        ts_col = keep.tile([P, 4], F32, name="ts_col")
+        ts2_col = keep.tile([P, 4], F32, name="ts2_col")
+        nc.scalar.activation(ts2_col[:], ts_turned[:, 0:512:P], SQUARE)
+        nc.scalar.copy(ts_col[:], ts_turned[:, 0:512:P])
+        ts_spread = bank()
+        for b in range(4):
+            nc.tensor.transpose(
+                ts_spread[:, b * P:(b + 1) * P], ts_col[:, b:b + 1].to_broadcast([P, P]), ident[:]
+            )
+        ts_row = keep.tile([P, SLOTS], F32, name="ts_row")
+        nc.scalar.copy(ts_row[:], ts_spread[:])
+
+        c1, c2 = [], []
+        for h in range(HEADS):
+            wu = keep.tile([P, PACK], F32, name="wu%d" % h)
+            wuu = keep.tile([P, PACK], F32, name="wuu%d" % h)
+            nc.vector.tensor_tensor(wu[:], w_col[h][:], u_col[h][:], MULT)
+            nc.vector.tensor_tensor(wuu[:], wu[:], u_col[h][:], MULT)
+            c2.append(wu)
+            c1.append(wuu)
+
+        w_d = keep.tile([P, SLOTS, PACK], BF16, name="w_d", align_bytes=64)
+        for j in range(PACK):
+            nc.vector.tensor_copy(w_d[:, :, j], table[j][:].indirect(offsets[:]))
+        w_codes, w_scales = quantize(w_d[:], "w", E4M3)
+
+        scaled = []
+        for h in range(HEADS):
+            for b in range(4):
+                a = bank()
+                cols = slice(b * P, (b + 1) * P)
+                nc.tensor.matmul_mx(
+                    out=a[:], lhsT=w_codes[:, cols].bitcast(E4M3), lhsT_scale=w_scales[:, cols],
+                    rhs=xd_q[h][0][:].bitcast(E4M3), rhs_scale=xd_q[h][1][:], start=True, stop=True,
+                )
+                s = ring.tile([P, PACK, P], F32, name="stage", tag="stage", bufs=8)
+                nc.scalar.activation(
+                    s[:], a[:].rearrange("i (m t) -> i t m", t=PACK), COPY, scale=ts2_col[:, b:b + 1]
+                )
+                scaled.append(s)
+        turned_back = []
+        for h in range(HEADS):
+            banks = [bank() for t in range(PACK)]
+            for t in range(PACK):
+                for b in range(4):
+                    nc.tensor.transpose(banks[t][:, b * P:(b + 1) * P], scaled[4 * h + b][:, t, :], ident[:])
+            for t in range(PACK):
+                nc.vector.scalar_tensor_tensor(
+                    y_sb[h][t][:], y_sb[h][t][:], c2[h][:, t:t + 1], ts_row[:], MULT, MULT
+                )
+            g_planes = keep.tile([P, PACK, SLOTS], BF16, name="g_planes%d" % h)
+            for t in range(PACK):
+                nc.vector.scalar_tensor_tensor(
+                    g_planes[:, t, :], banks[t][:], c1[h][:, t:t + 1], y_sb[h][t][:], MULT, SUB
+                )
+            turned_back.append(g_planes)
+
+        g_r = [keep.tile([P, SLOTS, PACK], BF16, name="g_r%d" % h, align_bytes=64) for h in range(HEADS)]
+        weave(nc.scalar.copy, g_r[0][:], turned_back[0][:])
+        weave(nc.vector.tensor_copy, g_r[1][:, 0:320, :], turned_back[1][:, :, 0:320])
+        weave(nc.scalar.copy, g_r[1][:, 320:, :], turned_back[1][:, :, 320:])
+        g_q = [quantize(g_r[h][:], "g%d" % h, E5M2) for h in range(HEADS)]
+
+        chunks = len(CHUNKS)
+        starts = [sum(CHUNKS[:k]) for k in range(chunks + 1)]
+        pairs = [keep.tile([P, 2, CHUNKS[k], 2], BF16, name="pairs%d" % k) for k in range(chunks)]
+        out_rows = out_0.rearrange("(p j) c -> p j c", j=PACK)
+        sums = []
+        accs = [bank() for j in range(PACK)]
+        for h in range(HEADS):
+            for j in range(PACK):
+                cols = slice(j * P, (j + 1) * P)
+                nc.tensor.matmul_mx(
+                    out=accs[j][:], lhsT=xr_q[h][0][:, cols].bitcast(E4M3), lhsT_scale=xr_q[h][1][:, cols],
+                    rhs=g_q[h][0][:].bitcast(E5M2), rhs_scale=g_q[h][1][:],
+                    start=(h == 0), stop=(h == HEADS - 1),
+                )
+        for j in range(PACK):
+            dw = ring.tile([P, SLOTS], F32, name="dw", tag="stage", bufs=8)
+            nc.scalar.copy(dw[:], accs[j][:])
+            sums.append(dw)
+        for j in range(PACK):
+            nc.vector.tensor_copy(windows[j][:].indirect(offsets[:]), sums[j][:])
+            nc.sync.dma_start(out=out_rows[:, j, :], in_=windows[j][:])
+            for k in range(chunks):
+                nc.scalar.copy(pairs[k][:, j // 2, :, j % 2], windows[j][:, starts[k]:starts[k + 1]])
+
+        out_words = out_1.rearrange("a p c l -> p (a c l)").bitcast(I32)
+        scale_rows = out_2.rearrange("a f c -> (a f) c").bitcast(I32)
+        split = starts[EARLY]
+        early_scales = keep.tile([P, split], U8, name="early_scales", align_bytes=64)
+        late_scales = keep.tile([P, TOKENS - split], U8, name="late_scales", align_bytes=64)
+        woven = [keep.tile([P, CHUNKS[k], PACK], BF16, name="woven%d" % k, align_bytes=64) for k in range(chunks)]
+
+        def weave_chunk(k):
+            copy, word = (nc.scalar.copy, U32) if k == chunks - 1 else (nc.vector.tensor_copy, I32)
+            weave(
+                copy,
+                woven[k][:].rearrange("p c t -> p (c t)").bitcast(word).rearrange("p (c u) -> p c u", u=2),
+                pairs[k][:].rearrange("p u c e -> p (u c e)").bitcast(word).rearrange("p (u c) -> p u c", u=2),
+            )
+
+        def store_scales(queue, scales, first, last):
+            for quad in range(4):
+                queue.dma_start(
+                    out=scale_rows[4 * quad:4 * quad + 4, first // 4:last // 4],
+                    in_=scales[32 * quad:32 * quad + 4, :].bitcast(I32),
+                )
+
+        weave_chunk(0)
+        for k in range(chunks):
+            if k + 1 < chunks:
+                weave_chunk(k + 1)
+            codes = keep.tile([P, CHUNKS[k]], U32, name="out_codes%d" % k, align_bytes=64)
+            if k < EARLY:
+                scales = early_scales[:, starts[k]:starts[k + 1]]
+            else:
+                scales = late_scales[:, starts[k] - split:starts[k + 1] - split]
+            nc.vector.quantize_mx(
+                out=codes[:].bitcast(E4M3), scales=scales, in_=woven[k][:].rearrange("p c t -> p (c t)")
+            )
+            nc.sync.dma_start(out=out_words[:, starts[k]:starts[k + 1]], in_=codes[:].bitcast(I32))
+            if k == EARLY - 1:
+                store_scales(nc.sync, early_scales, 0, split)
+        store_scales(nc.sync, late_scales, split, TOKENS)

@@ -21,7 +21,6 @@ PACK = 4
 D, R, SLOTS, TOKENS = 512, 512, 512, 2048
 HEADS = 2
 CHUNKS = (256, 512, 512, 512, 256)
-EARLY = 3
 FLOPS = 4 * 2 * 512 * 512 * 512
 
 
@@ -45,15 +44,18 @@ def tile_attend_gheads_sg_pl_kernel(
 
         def quantize(src, name, fmt):
             width = src.shape[1]
-            codes = keep.tile([P, width], U32, name=name + "_codes", align_bytes=64)
-            scales = keep.tile([P, width], U8, name=name + "_scales", align_bytes=64)
+            codes = keep.tile([P, width], U32, name=name + "_codes", tag=name + "_codes", align_bytes=64)
+            scales = keep.tile([P, width], U8, name=name + "_scales", tag=name + "_scales", align_bytes=64)
             nc.vector.quantize_mx(
                 out=codes[:].bitcast(fmt), scales=scales[:], in_=src.rearrange("p c t -> p (c t)")
             )
             return codes, scales
 
         def bank():
-            return psum.tile([P, 512], F32, name="bank", tag="bank", bufs=8)
+            return psum.tile([P, 512], F32, name="bank", tag="bank", bufs=7)
+
+        def ts_bank():
+            return psum.tile([P, 512], F32, name="ts_bank", tag="ts_bank", bufs=1)
 
         offsets = keep.tile([P, SLOTS // 16], U16, name="offsets")
         ident = keep.tile([P, P], F32, name="ident")
@@ -62,31 +64,32 @@ def tile_attend_gheads_sg_pl_kernel(
         ts_pool = keep.tile([P, TOKENS], F32, name="ts_pool")
         nc.vector.memset(ts_pool[:], 0.0)
         windows = [keep.tile([P, TOKENS], F32, name="window%d" % j) for j in range(PACK)]
-        for j in range(PACK):
-            nc.gpsimd.memset(windows[j][:], 0.0)
+        nc.vector.memset(windows[0][:], 0.0)
+        for j in range(1, PACK):
+            for c in range(0, TOKENS, 512):
+                nc.gpsimd.memset(windows[j][:, c:c + 512], 0.0)
 
         x_raw = [keep.tile([P, PACK, R], F32, name="x_raw%d" % h) for h in range(HEADS)]
         table = [keep.tile([P, TOKENS], F32, name="table%d" % j) for j in range(PACK)]
         w_planes = wT.rearrange("(p j) c -> p j c", j=PACK)
-        for h in range(HEADS):
-            nc.sync.dma_start(out=x_raw[h][:], in_=xs[h].rearrange("(p j) r -> p j r", j=PACK))
-        nc.sync.dma_start(offsets[:], offs)
-        nc.sync.dma_start(out=ts_pool[0:1, :], in_=ts[0:1, :])
-        for j in range(PACK):
-            nc.sync.dma_start(out=table[j][:], in_=w_planes[:, j, :])
         u_col = [keep.tile([P, PACK], F32, name="u_col%d" % h) for h in range(HEADS)]
         w_col = [keep.tile([P, PACK], F32, name="w_col%d" % h) for h in range(HEADS)]
+        nc.sync.dma_start(out=x_raw[0][:], in_=xs[0].rearrange("(p j) r -> p j r", j=PACK))
+        nc.sync.dma_start(offsets[:], offs)
         for h in range(HEADS):
             nc.sync.dma_start(out=u_col[h][:], in_=us[h].rearrange("(m t) o -> m (t o)", t=PACK))
             nc.sync.dma_start(out=w_col[h][:], in_=ws[h].rearrange("(m t) o -> m (t o)", t=PACK))
-        y_sb = [
-            [keep.tile([P, SLOTS], F32, name="y%d_%d" % (h, t)) for t in range(PACK)]
-            for h in range(HEADS)
-        ]
+        nc.sync.dma_start(out=x_raw[1][:], in_=xs[1].rearrange("(p j) r -> p j r", j=PACK))
+        nc.sync.dma_start(out=ts_pool[0:1, :], in_=ts[0:1, :])
+        for j in range(PACK):
+            nc.sync.dma_start(out=table[j][:], in_=w_planes[:, j, :])
+        y_sb = []
         for h in range(HEADS):
             y_rows = ys[h].rearrange("(m t) i -> m t i", t=PACK)
-            for t in range(PACK):
-                nc.sync.dma_start(out=y_sb[h][t][:], in_=y_rows[:, t, :])
+            halves = [keep.tile([P, 2, SLOTS], F32, name="y%d_%d" % (h, v)) for v in range(2)]
+            for v in range(2):
+                nc.sync.dma_start(out=halves[v][:], in_=y_rows[:, 2 * v:2 * v + 2, :])
+            y_sb.append([halves[t // 2][:, t % 2, :] for t in range(PACK)])
 
         x_d = [keep.tile([P, R, PACK], BF16, name="x_d%d" % h, align_bytes=64) for h in range(HEADS)]
         weave(nc.vector.tensor_copy, x_d[0][:], x_raw[0][:])
@@ -119,13 +122,11 @@ def tile_attend_gheads_sg_pl_kernel(
         ts2_col = keep.tile([P, 4], F32, name="ts2_col")
         nc.scalar.activation(ts2_col[:], ts_turned[:, 0:512:P], SQUARE)
         nc.scalar.copy(ts_col[:], ts_turned[:, 0:512:P])
-        ts_spread = bank()
+        ts_spread = ts_bank()
         for b in range(4):
             nc.tensor.transpose(
                 ts_spread[:, b * P:(b + 1) * P], ts_col[:, b:b + 1].to_broadcast([P, P]), ident[:]
             )
-        ts_row = keep.tile([P, SLOTS], F32, name="ts_row")
-        nc.scalar.copy(ts_row[:], ts_spread[:])
 
         c1, c2 = [], []
         for h in range(HEADS):
@@ -136,16 +137,31 @@ def tile_attend_gheads_sg_pl_kernel(
             c2.append(wu)
             c1.append(wuu)
 
-        w_d = keep.tile([P, SLOTS, PACK], BF16, name="w_d", align_bytes=64)
-        for j in range(PACK):
-            nc.vector.tensor_copy(w_d[:, :, j], table[j][:].indirect(offsets[:]))
-        w_codes, w_scales = quantize(w_d[:], "w", E4M3)
+        on_vector = [(0, 0), (0, 1), (0, 2)]
+        on_gpsimd = [(0, 3), (1, 0), (1, 1), (1, 2), (1, 3)]
+        factor = {}
+        for h, t in on_gpsimd:
+            factor[h, t] = keep.tile([P, SLOTS], F32, name="factor%d_%d" % (h, t))
+            nc.scalar.activation(factor[h, t][:], ts_spread[:], COPY, scale=c2[h][:, t:t + 1])
+
+        w_d = [
+            keep.tile([P, SLOTS // 2, PACK], BF16, name="w_d", tag="w_d%d" % v, align_bytes=64)
+            for v in range(2)
+        ]
+        for j in range(PACK - 1):
+            for v in range(2):
+                nc.vector.tensor_copy(w_d[v][:, :, j], table[j][:].indirect(offsets[:, 16 * v:16 * v + 16]))
+        w_q = []
+        for v in range(2):
+            nc.vector.tensor_copy(w_d[v][:, :, 3], table[3][:].indirect(offsets[:, 16 * v:16 * v + 16]))
+            w_q.append(quantize(w_d[v][:], "w%d" % v, E4M3))
 
         scaled = []
         for h in range(HEADS):
             for b in range(4):
                 a = bank()
-                cols = slice(b * P, (b + 1) * P)
+                cols = slice(b % 2 * P, (b % 2 + 1) * P)
+                w_codes, w_scales = w_q[b // 2]
                 nc.tensor.matmul_mx(
                     out=a[:], lhsT=w_codes[:, cols].bitcast(E4M3), lhsT_scale=w_scales[:, cols],
                     rhs=xd_q[h][0][:].bitcast(E4M3), rhs_scale=xd_q[h][1][:], start=True, stop=True,
@@ -155,24 +171,28 @@ def tile_attend_gheads_sg_pl_kernel(
                     s[:], a[:].rearrange("i (m t) -> i t m", t=PACK), COPY, scale=ts2_col[:, b:b + 1]
                 )
                 scaled.append(s)
+        for h, t in on_vector:
+            nc.vector.scalar_tensor_tensor(y_sb[h][t], y_sb[h][t], c2[h][:, t:t + 1], ts_spread[:], MULT, MULT)
+        for n, (h, t) in enumerate(on_gpsimd):
+            target = keep.tile(
+                [P, SLOTS], F32, name="target", tag="w_d1" if n == 0 else "target%d" % n, align_bytes=64
+            )
+            nc.gpsimd.tensor_tensor(target[:], y_sb[h][t], factor[h, t][:], MULT)
+            y_sb[h][t] = target[:]
         turned_back = []
         for h in range(HEADS):
-            banks = [bank() for t in range(PACK)]
+            banks = [ts_bank() if (h, t) == (1, 0) else bank() for t in range(PACK)]
             for t in range(PACK):
                 for b in range(4):
                     nc.tensor.transpose(banks[t][:, b * P:(b + 1) * P], scaled[4 * h + b][:, t, :], ident[:])
+            g_planes = keep.tile([P, PACK, SLOTS], BF16, name="g_planes%d" % h, tag="g_planes%d" % h)
             for t in range(PACK):
                 nc.vector.scalar_tensor_tensor(
-                    y_sb[h][t][:], y_sb[h][t][:], c2[h][:, t:t + 1], ts_row[:], MULT, MULT
-                )
-            g_planes = keep.tile([P, PACK, SLOTS], BF16, name="g_planes%d" % h)
-            for t in range(PACK):
-                nc.vector.scalar_tensor_tensor(
-                    g_planes[:, t, :], banks[t][:], c1[h][:, t:t + 1], y_sb[h][t][:], MULT, SUB
+                    g_planes[:, t, :], banks[t][:], c1[h][:, t:t + 1], y_sb[h][t], MULT, SUB
                 )
             turned_back.append(g_planes)
 
-        g_r = [keep.tile([P, SLOTS, PACK], BF16, name="g_r%d" % h, align_bytes=64) for h in range(HEADS)]
+        g_r = [keep.tile([P, SLOTS, PACK], BF16, name="g_r%d" % h, tag="g_r%d" % h, align_bytes=64) for h in range(HEADS)]
         weave(nc.scalar.copy, g_r[0][:], turned_back[0][:])
         weave(nc.vector.tensor_copy, g_r[1][:, 0:320, :], turned_back[1][:, :, 0:320])
         weave(nc.scalar.copy, g_r[1][:, 320:, :], turned_back[1][:, :, 320:])
@@ -180,12 +200,11 @@ def tile_attend_gheads_sg_pl_kernel(
 
         chunks = len(CHUNKS)
         starts = [sum(CHUNKS[:k]) for k in range(chunks + 1)]
-        pairs = [keep.tile([P, 2, CHUNKS[k], 2], BF16, name="pairs%d" % k) for k in range(chunks)]
         out_rows = out_0.rearrange("(p j) c -> p j c", j=PACK)
         sums = []
         accs = [bank() for j in range(PACK)]
-        for h in range(HEADS):
-            for j in range(PACK):
+        for j in range(PACK):
+            for h in range(HEADS):
                 cols = slice(j * P, (j + 1) * P)
                 nc.tensor.matmul_mx(
                     out=accs[j][:], lhsT=xr_q[h][0][:, cols].bitcast(E4M3), lhsT_scale=xr_q[h][1][:, cols],
@@ -196,6 +215,11 @@ def tile_attend_gheads_sg_pl_kernel(
             dw = ring.tile([P, SLOTS], F32, name="dw", tag="stage", bufs=8)
             nc.scalar.copy(dw[:], accs[j][:])
             sums.append(dw)
+        freed = ("xr1_codes", "xr1_scales", "g1_scales", "xr0_codes", "xr0_scales")
+        pairs = [
+            keep.tile([P, 2, CHUNKS[k], 2], BF16, name="pairs", tag=freed[k], align_bytes=64)
+            for k in range(chunks)
+        ]
         for j in range(PACK):
             nc.vector.tensor_copy(windows[j][:].indirect(offsets[:]), sums[j][:])
             nc.sync.dma_start(out=out_rows[:, j, :], in_=windows[j][:])
@@ -204,9 +228,8 @@ def tile_attend_gheads_sg_pl_kernel(
 
         out_words = out_1.rearrange("a p c l -> p (a c l)").bitcast(I32)
         scale_rows = out_2.rearrange("a f c -> (a f) c").bitcast(I32)
-        split = starts[EARLY]
-        early_scales = keep.tile([P, split], U8, name="early_scales", align_bytes=64)
-        late_scales = keep.tile([P, TOKENS - split], U8, name="late_scales", align_bytes=64)
+        out_scales = keep.tile([P, TOKENS], U8, name="out_scales", align_bytes=64)
+        out_codes = keep.tile([P, TOKENS], U32, name="out_codes", align_bytes=64)
         woven = [keep.tile([P, CHUNKS[k], PACK], BF16, name="woven%d" % k, align_bytes=64) for k in range(chunks)]
 
         def weave_chunk(k):
@@ -217,26 +240,22 @@ def tile_attend_gheads_sg_pl_kernel(
                 pairs[k][:].rearrange("p u c e -> p (u c e)").bitcast(word).rearrange("p (u c) -> p u c", u=2),
             )
 
-        def store_scales(queue, scales, first, last):
-            for quad in range(4):
-                queue.dma_start(
-                    out=scale_rows[4 * quad:4 * quad + 4, first // 4:last // 4],
-                    in_=scales[32 * quad:32 * quad + 4, :].bitcast(I32),
-                )
-
         weave_chunk(0)
+        stored = 0
         for k in range(chunks):
             if k + 1 < chunks:
                 weave_chunk(k + 1)
-            codes = keep.tile([P, CHUNKS[k]], U32, name="out_codes%d" % k, align_bytes=64)
-            if k < EARLY:
-                scales = early_scales[:, starts[k]:starts[k + 1]]
-            else:
-                scales = late_scales[:, starts[k] - split:starts[k + 1] - split]
+            cols = slice(starts[k], starts[k + 1])
             nc.vector.quantize_mx(
-                out=codes[:].bitcast(E4M3), scales=scales, in_=woven[k][:].rearrange("p c t -> p (c t)")
+                out=out_codes[:, cols].bitcast(E4M3), scales=out_scales[:, cols],
+                in_=woven[k][:].rearrange("p c t -> p (c t)"),
             )
-            nc.sync.dma_start(out=out_words[:, starts[k]:starts[k + 1]], in_=codes[:].bitcast(I32))
-            if k == EARLY - 1:
-                store_scales(nc.sync, early_scales, 0, split)
-        store_scales(nc.sync, late_scales, split, TOKENS)
+            if k in (1, 3, 4):
+                cols = slice(stored, starts[k + 1])
+                nc.sync.dma_start(out=out_words[:, cols], in_=out_codes[:, cols].bitcast(I32))
+                stored = starts[k + 1]
+        for quad in range(4):
+            nc.sync.dma_start(
+                out=scale_rows[4 * quad:4 * quad + 4, :],
+                in_=out_scales[32 * quad:32 * quad + 4, :].bitcast(I32),
+            )

@@ -63,11 +63,9 @@ def tile_attend_gheads_sg_pl_kernel(
 
         ts_pool = keep.tile([P, TOKENS], F32, name="ts_pool")
         nc.vector.memset(ts_pool[:], 0.0)
-        windows = [keep.tile([P, TOKENS], F32, name="window%d" % j) for j in range(PACK)]
-        nc.vector.memset(windows[0][:], 0.0)
-        for j in range(1, PACK):
-            for c in range(0, TOKENS, 512):
-                nc.gpsimd.memset(windows[j][:, c:c + 512], 0.0)
+        windows = [keep.tile([P, TOKENS], F32, name="window%d" % j) for j in range(PACK - 1)]
+        for window in windows:
+            nc.vector.memset(window[:], 0.0)
 
         x_raw = [keep.tile([P, PACK, R], F32, name="x_raw%d" % h) for h in range(HEADS)]
         table = [keep.tile([P, TOKENS], F32, name="table%d" % j) for j in range(PACK)]
@@ -86,7 +84,7 @@ def tile_attend_gheads_sg_pl_kernel(
         y_sb = []
         for h in range(HEADS):
             y_rows = ys[h].rearrange("(m t) i -> m t i", t=PACK)
-            halves = [keep.tile([P, 2, SLOTS], F32, name="y%d_%d" % (h, v)) for v in range(2)]
+            halves = [keep.tile([P, 2, SLOTS], F32, name="y", tag="y%d_%d" % (h, v)) for v in range(2)]
             for v in range(2):
                 nc.sync.dma_start(out=halves[v][:], in_=y_rows[:, 2 * v:2 * v + 2, :])
             y_sb.append([halves[t // 2][:, t % 2, :] for t in range(PACK)])
@@ -137,8 +135,8 @@ def tile_attend_gheads_sg_pl_kernel(
             c2.append(wu)
             c1.append(wuu)
 
-        on_vector = [(0, 0), (0, 1), (0, 2)]
-        on_gpsimd = [(0, 3), (1, 0), (1, 1), (1, 2), (1, 3)]
+        on_vector = [(0, 0), (0, 1), (0, 2), (1, 0), (1, 1)]
+        on_gpsimd = [(0, 3), (1, 2), (1, 3)]
         factor = {}
         for h, t in on_gpsimd:
             factor[h, t] = keep.tile([P, SLOTS], F32, name="factor%d_%d" % (h, t))
@@ -171,24 +169,29 @@ def tile_attend_gheads_sg_pl_kernel(
                     s[:], a[:].rearrange("i (m t) -> i t m", t=PACK), COPY, scale=ts2_col[:, b:b + 1]
                 )
                 scaled.append(s)
+        last_window = keep.tile([P, TOKENS], F32, name="last_window", tag="w_d1", align_bytes=64)
+        nc.gpsimd.memset(last_window[:], 0.0)
+        windows.append(last_window)
+        targets = {}
+        for h in range(HEADS):
+            for t in range(PACK):
+                targets[h, t] = keep.tile([P, SLOTS], F32, name="target", tag="target%d_%d" % (h, t))
         for h, t in on_vector:
-            nc.vector.scalar_tensor_tensor(y_sb[h][t], y_sb[h][t], c2[h][:, t:t + 1], ts_spread[:], MULT, MULT)
-        for n, (h, t) in enumerate(on_gpsimd):
-            target = keep.tile(
-                [P, SLOTS], F32, name="target", tag="w_d1" if n == 0 else "target%d" % n, align_bytes=64
+            nc.vector.scalar_tensor_tensor(
+                targets[h, t][:], y_sb[h][t], c2[h][:, t:t + 1], ts_spread[:], MULT, MULT
             )
-            nc.gpsimd.tensor_tensor(target[:], y_sb[h][t], factor[h, t][:], MULT)
-            y_sb[h][t] = target[:]
+        for h, t in on_gpsimd:
+            nc.gpsimd.tensor_tensor(targets[h, t][:], y_sb[h][t], factor[h, t][:], MULT)
         turned_back = []
         for h in range(HEADS):
             banks = [ts_bank() if (h, t) == (1, 0) else bank() for t in range(PACK)]
             for t in range(PACK):
                 for b in range(4):
                     nc.tensor.transpose(banks[t][:, b * P:(b + 1) * P], scaled[4 * h + b][:, t, :], ident[:])
-            g_planes = keep.tile([P, PACK, SLOTS], BF16, name="g_planes%d" % h, tag="g_planes%d" % h)
+            g_planes = keep.tile([P, PACK, SLOTS], BF16, name="g_planes%d" % h, tag=("y1_0", "target0_3")[h])
             for t in range(PACK):
                 nc.vector.scalar_tensor_tensor(
-                    g_planes[:, t, :], banks[t][:], c1[h][:, t:t + 1], y_sb[h][t], MULT, SUB
+                    g_planes[:, t, :], banks[t][:], c1[h][:, t:t + 1], targets[h, t][:], MULT, SUB
                 )
             turned_back.append(g_planes)
 

@@ -20,7 +20,11 @@ P = 128
 PACK = 4
 D, R, SLOTS, TOKENS = 512, 512, 512, 2048
 HEADS = 2
-CHUNKS = (256, 512, 512, 512, 256)
+HALF = SLOTS // 2
+CHUNKS = (256, 512, 512, 256, 256, 256)
+RUN = 128
+ON_SCALAR = (5,)
+STORE_AFTER = (1, 3, 5)
 FLOPS = 4 * 2 * 512 * 512 * 512
 
 
@@ -51,8 +55,11 @@ def tile_attend_gheads_sg_pl_kernel(
             )
             return codes, scales
 
-        def bank():
-            return psum.tile([P, 512], F32, name="bank", tag="bank", bufs=7)
+        def score_bank():
+            return psum.tile([P, 512], F32, name="score", tag="score", bufs=3)
+
+        def turn_bank():
+            return psum.tile([P, 512], F32, name="turn", tag="turn", bufs=4)
 
         def ts_bank():
             return psum.tile([P, 512], F32, name="ts_bank", tag="ts_bank", bufs=1)
@@ -63,68 +70,52 @@ def tile_attend_gheads_sg_pl_kernel(
 
         ts_pool = keep.tile([P, TOKENS], F32, name="ts_pool")
         nc.vector.memset(ts_pool[:], 0.0)
+
         windows = [keep.tile([P, TOKENS], F32, name="window%d" % j) for j in range(PACK - 1)]
         for window in windows:
             nc.vector.memset(window[:], 0.0)
 
         x_raw = [keep.tile([P, PACK, R], F32, name="x_raw%d" % h) for h in range(HEADS)]
-        table = [keep.tile([P, TOKENS], F32, name="table%d" % j) for j in range(PACK)]
+        table = [keep.tile([P, TOKENS], F32, name="table", tag="table%d" % j, align_bytes=64) for j in range(PACK)]
         w_planes = wT.rearrange("(p j) c -> p j c", j=PACK)
         u_col = [keep.tile([P, PACK], F32, name="u_col%d" % h) for h in range(HEADS)]
         w_col = [keep.tile([P, PACK], F32, name="w_col%d" % h) for h in range(HEADS)]
         nc.sync.dma_start(out=x_raw[0][:], in_=xs[0].rearrange("(p j) r -> p j r", j=PACK))
         nc.sync.dma_start(offsets[:], offs)
+        nc.sync.dma_start(out=x_raw[1][:], in_=xs[1].rearrange("(p j) r -> p j r", j=PACK))
+        nc.sync.dma_start(out=ts_pool[0:1, :], in_=ts[0:1, :])
         for h in range(HEADS):
             nc.sync.dma_start(out=u_col[h][:], in_=us[h].rearrange("(m t) o -> m (t o)", t=PACK))
             nc.sync.dma_start(out=w_col[h][:], in_=ws[h].rearrange("(m t) o -> m (t o)", t=PACK))
-        nc.sync.dma_start(out=x_raw[1][:], in_=xs[1].rearrange("(p j) r -> p j r", j=PACK))
-        nc.sync.dma_start(out=ts_pool[0:1, :], in_=ts[0:1, :])
         for j in range(PACK):
             nc.sync.dma_start(out=table[j][:], in_=w_planes[:, j, :])
-        y_sb = []
+        y_sb = {}
         for h in range(HEADS):
             y_rows = ys[h].rearrange("(m t) i -> m t i", t=PACK)
-            halves = [keep.tile([P, 2, SLOTS], F32, name="y", tag="y%d_%d" % (h, v)) for v in range(2)]
-            for v in range(2):
-                nc.sync.dma_start(out=halves[v][:], in_=y_rows[:, 2 * v:2 * v + 2, :])
-            y_sb.append([halves[t // 2][:, t % 2, :] for t in range(PACK)])
+            for tp in range(2):
+                y_sb[h, tp] = keep.tile([P, 2, SLOTS], F32, name="y", tag="y%d_%d" % (h, tp))
+                nc.sync.dma_start(out=y_sb[h, tp][:], in_=y_rows[:, 2 * tp:2 * tp + 2, :])
 
         x_d = [keep.tile([P, R, PACK], BF16, name="x_d%d" % h, align_bytes=64) for h in range(HEADS)]
-        weave(nc.vector.tensor_copy, x_d[0][:], x_raw[0][:])
-        weave(nc.scalar.copy, x_d[1][:], x_raw[1][:])
-
-        xd_q = [quantize(x_d[h][:], "xd%d" % h, E4M3) for h in range(HEADS)]
-
-        xr_q = []
-        for h in range(HEADS):
-            words = x_d[h][:].rearrange("p r j -> p (r j)").bitcast(F32)
-            x_r = keep.tile([P, D, PACK], BF16, name="x_r%d" % h, align_bytes=64)
-            for jj in range(2):
-                turned = bank()
-                for t in range(PACK):
-                    nc.tensor.transpose(
-                        turned[:, t * P:(t + 1) * P], words[:, 2 * t + jj:2 * R:8], ident[:]
-                    )
-                nc.scalar.copy(
-                    out=x_r[:, jj * 256:(jj + 1) * 256, :].rearrange("s (e p) t -> s e p t", e=2),
-                    in_=turned[:].bitcast(BF16).rearrange("s (t p e) -> s e p t", t=PACK, e=2),
-                )
-            xr_q.append(quantize(x_r[:], "xr%d" % h, E4M3))
+        weave(nc.scalar.copy, x_d[0][:], x_raw[0][:])
 
         ts_listed = keep.tile([P, SLOTS], F32, name="ts_listed")
         nc.vector.tensor_copy(ts_listed[:], ts_pool[:].indirect(offsets[:]))
-        ts_turned = bank()
+        ts_turned = score_bank()
         for b in range(4):
             nc.tensor.transpose(ts_turned[:, b * P:(b + 1) * P], ts_listed[:, b * P:(b + 1) * P], ident[:])
         ts_col = keep.tile([P, 4], F32, name="ts_col")
         ts2_col = keep.tile([P, 4], F32, name="ts2_col")
-        nc.scalar.activation(ts2_col[:], ts_turned[:, 0:512:P], SQUARE)
         nc.scalar.copy(ts_col[:], ts_turned[:, 0:512:P])
+        nc.scalar.activation(ts2_col[:], ts_turned[:, 0:512:P], SQUARE)
         ts_spread = ts_bank()
         for b in range(4):
             nc.tensor.transpose(
                 ts_spread[:, b * P:(b + 1) * P], ts_col[:, b:b + 1].to_broadcast([P, P]), ident[:]
             )
+
+        weave(nc.vector.tensor_copy, x_d[1][:], x_raw[1][:])
+        xd_q = [quantize(x_d[h][:], "xd%d" % h, E4M3) for h in range(HEADS)]
 
         c1, c2 = [], []
         for h in range(HEADS):
@@ -135,79 +126,135 @@ def tile_attend_gheads_sg_pl_kernel(
             c2.append(wu)
             c1.append(wuu)
 
-        on_vector = [(0, 0), (0, 1), (0, 2), (1, 0), (1, 1)]
-        on_gpsimd = [(0, 3), (1, 2), (1, 3)]
-        factor = {}
-        for h, t in on_gpsimd:
-            factor[h, t] = keep.tile([P, SLOTS], F32, name="factor%d_%d" % (h, t))
-            nc.scalar.activation(factor[h, t][:], ts_spread[:], COPY, scale=c2[h][:, t:t + 1])
-
         w_d = [
-            keep.tile([P, SLOTS // 2, PACK], BF16, name="w_d", tag="w_d%d" % v, align_bytes=64)
+            keep.tile([P, HALF, PACK], BF16, name="w_d", tag="w_d%d" % v, align_bytes=64)
             for v in range(2)
         ]
-        for j in range(PACK - 1):
+        for j in range(2):
             for v in range(2):
                 nc.vector.tensor_copy(w_d[v][:, :, j], table[j][:].indirect(offsets[:, 16 * v:16 * v + 16]))
+
+        xr_q = []
+        for h in range(HEADS):
+            words = x_d[h][:].rearrange("p r j -> p (r j)").bitcast(F32)
+            x_r = keep.tile([P, D, PACK], BF16, name="x_r%d" % h, align_bytes=64)
+            for jj in range(2):
+                turned = turn_bank()
+                for t in range(PACK):
+                    nc.tensor.transpose(
+                        turned[:, t * P:(t + 1) * P], words[:, 2 * t + jj:2 * R:8], ident[:]
+                    )
+                nc.scalar.copy(
+                    out=x_r[:, jj * 256:(jj + 1) * 256, :].rearrange("s (e p) t -> s e p t", e=2),
+                    in_=turned[:].bitcast(BF16).rearrange("s (t p e) -> s e p t", t=PACK, e=2),
+                )
+            xr_q.append(quantize(x_r[:], "xr%d" % h, E4M3))
+
+        for v in range(2):
+            nc.vector.tensor_copy(w_d[v][:, :, 2], table[2][:].indirect(offsets[:, 16 * v:16 * v + 16]))
         w_q = []
         for v in range(2):
             nc.vector.tensor_copy(w_d[v][:, :, 3], table[3][:].indirect(offsets[:, 16 * v:16 * v + 16]))
             w_q.append(quantize(w_d[v][:], "w%d" % v, E4M3))
 
-        scaled = []
-        for h in range(HEADS):
-            for b in range(4):
-                a = bank()
-                cols = slice(b % 2 * P, (b % 2 + 1) * P)
-                w_codes, w_scales = w_q[b // 2]
-                nc.tensor.matmul_mx(
-                    out=a[:], lhsT=w_codes[:, cols].bitcast(E4M3), lhsT_scale=w_scales[:, cols],
-                    rhs=xd_q[h][0][:].bitcast(E4M3), rhs_scale=xd_q[h][1][:], start=True, stop=True,
-                )
-                s = ring.tile([P, PACK, P], F32, name="stage", tag="stage", bufs=8)
+        on_vector = [(0, 0, 0), (0, 0, 1), (1, 1, 1)]
+        on_gpsimd = [(0, 1, 0), (0, 1, 1), (1, 0, 0), (1, 0, 1), (1, 1, 0)]
+        factor = {}
+        for h, v, tp in on_gpsimd:
+            factor[h, v, tp] = keep.tile([P, 2, HALF], F32, name="factor%d%d%d" % (h, v, tp))
+            for e in range(2):
+                t = 2 * tp + e
                 nc.scalar.activation(
-                    s[:], a[:].rearrange("i (m t) -> i t m", t=PACK), COPY, scale=ts2_col[:, b:b + 1]
+                    factor[h, v, tp][:, e, :], ts_spread[:, v * HALF:(v + 1) * HALF], COPY, scale=c2[h][:, t:t + 1]
                 )
-                scaled.append(s)
-        last_window = keep.tile([P, TOKENS], F32, name="last_window", tag="w_d1", align_bytes=64)
-        nc.gpsimd.memset(last_window[:], 0.0)
-        windows.append(last_window)
         targets = {}
-        for h in range(HEADS):
-            for t in range(PACK):
-                targets[h, t] = keep.tile([P, SLOTS], F32, name="target", tag="target%d_%d" % (h, t))
-        for h, t in on_vector:
-            nc.vector.scalar_tensor_tensor(
-                targets[h, t][:], y_sb[h][t], c2[h][:, t:t + 1], ts_spread[:], MULT, MULT
-            )
-        for h, t in on_gpsimd:
-            nc.gpsimd.tensor_tensor(targets[h, t][:], y_sb[h][t], factor[h, t][:], MULT)
-        turned_back = []
-        for h in range(HEADS):
-            banks = [ts_bank() if (h, t) == (1, 0) else bank() for t in range(PACK)]
-            for t in range(PACK):
-                for b in range(4):
-                    nc.tensor.transpose(banks[t][:, b * P:(b + 1) * P], scaled[4 * h + b][:, t, :], ident[:])
-            g_planes = keep.tile([P, PACK, SLOTS], BF16, name="g_planes%d" % h, tag=("y1_0", "target0_3")[h])
-            for t in range(PACK):
-                nc.vector.scalar_tensor_tensor(
-                    g_planes[:, t, :], banks[t][:], c1[h][:, t:t + 1], targets[h, t][:], MULT, SUB
-                )
-            turned_back.append(g_planes)
+        held = keep.tile([P, PACK, HALF], F32, name="held", tag="w_d1", align_bytes=64)
+        for h, v, tp in on_vector + on_gpsimd:
+            if (h, v) == (0, 1):
+                targets[h, v, tp] = held[:, 2 * tp:2 * tp + 2, :]
+            else:
+                targets[h, v, tp] = keep.tile([P, 2, HALF], F32, name="target%d%d%d" % (h, v, tp))[:]
 
-        g_r = [keep.tile([P, SLOTS, PACK], BF16, name="g_r%d" % h, tag="g_r%d" % h, align_bytes=64) for h in range(HEADS)]
-        weave(nc.scalar.copy, g_r[0][:], turned_back[0][:])
-        weave(nc.vector.tensor_copy, g_r[1][:, 0:320, :], turned_back[1][:, :, 0:320])
-        weave(nc.scalar.copy, g_r[1][:, 320:, :], turned_back[1][:, :, 320:])
-        g_q = [quantize(g_r[h][:], "g%d" % h, E5M2) for h in range(HEADS)]
+        def vector_target(h, v, tp):
+            for e in range(2):
+                t = 2 * tp + e
+                nc.vector.scalar_tensor_tensor(
+                    targets[h, v, tp][:, e, :], y_sb[h, tp][:, e, v * HALF:(v + 1) * HALF], c2[h][:, t:t + 1],
+                    ts_spread[:, v * HALF:(v + 1) * HALF], MULT, MULT,
+                )
+
+        for h, v, tp in on_gpsimd:
+            nc.gpsimd.tensor_tensor(
+                targets[h, v, tp], y_sb[h, tp][:, :, v * HALF:(v + 1) * HALF], factor[h, v, tp][:], MULT
+            )
+        for unit in on_vector[:2]:
+            vector_target(*unit)
+
+        scaled = {}
+
+        def score(n):
+            h, b = divmod(n, 4)
+            a = score_bank()
+            cols = slice(b % 2 * P, (b % 2 + 1) * P)
+            w_codes, w_scales = w_q[b // 2]
+            nc.tensor.matmul_mx(
+                out=a[:], lhsT=w_codes[:, cols].bitcast(E4M3), lhsT_scale=w_scales[:, cols],
+                rhs=xd_q[h][0][:].bitcast(E4M3), rhs_scale=xd_q[h][1][:], start=True, stop=True,
+            )
+            s = ring.tile([P, PACK, P], F32, name="stage", tag="stage", bufs=6)
+            nc.scalar.activation(
+                s[:], a[:].rearrange("i (m t) -> i t m", t=PACK), COPY, scale=ts2_col[:, b:b + 1]
+            )
+            scaled[n] = s
+
+        g_planes = {}
+
+        def gradient_unit(h, v):
+            banks = [turn_bank() for tp in range(2)]
+            for bb in range(2):
+                for t in range(PACK):
+                    at = t % 2 * HALF + bb * P
+                    nc.tensor.transpose(banks[t // 2][:, at:at + P], scaled[4 * h + 2 * v + bb][:, t, :], ident[:])
+            planes = keep.tile([P, PACK, HALF], BF16, name="g_planes%d%d" % (h, v))
+            for t in ((2, 3, 0, 1) if (h, v) == (1, 1) else range(PACK)):
+                if (h, v, t) == (1, 1, 2):
+                    vector_target(*on_vector[2])
+                nc.vector.scalar_tensor_tensor(
+                    planes[:, t, :], banks[t // 2][:, t % 2 * HALF:(t % 2 + 1) * HALF], c1[h][:, t:t + 1],
+                    targets[h, v, t // 2][:, t % 2, :], MULT, SUB,
+                )
+            g_planes[h, v] = planes
+
+        for n in range(3):
+            score(n)
+        for u in range(4):
+            gradient_unit(*divmod(u, 2))
+            for n in range(2 * u + 3, min(2 * u + 5, 8)):
+                score(n)
+
+        g_q = []
+        for h in range(HEADS):
+            codes = keep.tile([P, SLOTS], U32, name="g_codes", tag="g%d_codes" % h, align_bytes=64)
+            scales = keep.tile([P, SLOTS], U8, name="g_scales", tag="g%d_scales" % h, align_bytes=64)
+            for v in range(2):
+                g_r = keep.tile([P, HALF, PACK], BF16, name="g_r", tag="g_r%d%d" % (h, v), align_bytes=64)
+                weave(nc.vector.tensor_copy if (h, v) == (1, 1) else nc.scalar.copy, g_r[:], g_planes[h, v][:])
+                cols = slice(v * HALF, (v + 1) * HALF)
+                nc.vector.quantize_mx(
+                    out=codes[:, cols].bitcast(E5M2), scales=scales[:, cols], in_=g_r[:].rearrange("p c t -> p (c t)")
+                )
+            g_q.append((codes, scales))
+        last_window = keep.tile([P, TOKENS], F32, name="last_window", tag="g_r11", align_bytes=64)
+        nc.vector.memset(last_window[:], 0.0)
+        windows.append(last_window)
 
         chunks = len(CHUNKS)
         starts = [sum(CHUNKS[:k]) for k in range(chunks + 1)]
         out_rows = out_0.rearrange("(p j) c -> p j c", j=PACK)
         sums = []
-        accs = [bank() for j in range(PACK)]
-        for j in range(PACK):
-            for h in range(HEADS):
+        accs = [score_bank() for j in range(PACK - 1)] + [ts_bank()]
+        for h in range(HEADS):
+            for j in range(PACK):
                 cols = slice(j * P, (j + 1) * P)
                 nc.tensor.matmul_mx(
                     out=accs[j][:], lhsT=xr_q[h][0][:, cols].bitcast(E4M3), lhsT_scale=xr_q[h][1][:, cols],
@@ -215,32 +262,32 @@ def tile_attend_gheads_sg_pl_kernel(
                     start=(h == 0), stop=(h == HEADS - 1),
                 )
         for j in range(PACK):
-            dw = ring.tile([P, SLOTS], F32, name="dw", tag="stage", bufs=8)
+            dw = ring.tile([P, SLOTS], F32, name="dw", tag="stage", bufs=6)
             nc.scalar.copy(dw[:], accs[j][:])
             sums.append(dw)
-        freed = ("xr1_codes", "xr1_scales", "g1_scales", "xr0_codes", "xr0_scales")
-        pairs = [
-            keep.tile([P, 2, CHUNKS[k], 2], BF16, name="pairs", tag=freed[k], align_bytes=64)
-            for k in range(chunks)
-        ]
+        pairs = keep.tile([P, TOKENS // RUN, 2, RUN, 2], BF16, name="pairs", tag="xr1_codes", align_bytes=64)
         for j in range(PACK):
             nc.vector.tensor_copy(windows[j][:].indirect(offsets[:]), sums[j][:])
             nc.sync.dma_start(out=out_rows[:, j, :], in_=windows[j][:])
-            for k in range(chunks):
-                nc.scalar.copy(pairs[k][:, j // 2, :, j % 2], windows[j][:, starts[k]:starts[k + 1]])
+            cuts = starts if j == PACK - 1 else (0, TOKENS)
+            for lo, hi in zip(cuts[:-1], cuts[1:]):
+                nc.scalar.copy(
+                    pairs[:, lo // RUN:hi // RUN, j // 2, :, j % 2],
+                    windows[j][:, lo:hi].rearrange("p (k c) -> p k c", c=RUN),
+                )
 
         out_words = out_1.rearrange("a p c l -> p (a c l)").bitcast(I32)
         scale_rows = out_2.rearrange("a f c -> (a f) c").bitcast(I32)
         out_scales = keep.tile([P, TOKENS], U8, name="out_scales", align_bytes=64)
         out_codes = keep.tile([P, TOKENS], U32, name="out_codes", align_bytes=64)
-        woven = [keep.tile([P, CHUNKS[k], PACK], BF16, name="woven%d" % k, align_bytes=64) for k in range(chunks)]
+        woven = [keep.tile([P, CHUNKS[k], PACK], BF16, name="woven", tag="table%d" % k, align_bytes=64) for k in range(chunks)]
 
         def weave_chunk(k):
-            copy, word = (nc.scalar.copy, U32) if k == chunks - 1 else (nc.vector.tensor_copy, I32)
-            weave(
-                copy,
-                woven[k][:].rearrange("p c t -> p (c t)").bitcast(word).rearrange("p (c u) -> p c u", u=2),
-                pairs[k][:].rearrange("p u c e -> p (u c e)").bitcast(word).rearrange("p (u c) -> p u c", u=2),
+            copy, word = (nc.scalar.copy, U32) if k in ON_SCALAR else (nc.vector.tensor_copy, I32)
+            words = pairs[:].rearrange("p k u c e -> p (k u c e)").bitcast(word)[:, 2 * starts[k]:2 * starts[k + 1]]
+            copy(
+                out=woven[k][:].rearrange("p c t -> p (c t)").bitcast(word).rearrange("p (k c i u) -> p k c u i", c=RUN // 4, i=4, u=2),
+                in_=words.rearrange("p (k u c i) -> p k c u i", u=2, c=RUN // 4, i=4),
             )
 
         weave_chunk(0)
@@ -253,7 +300,7 @@ def tile_attend_gheads_sg_pl_kernel(
                 out=out_codes[:, cols].bitcast(E4M3), scales=out_scales[:, cols],
                 in_=woven[k][:].rearrange("p c t -> p (c t)"),
             )
-            if k in (1, 3, 4):
+            if k in STORE_AFTER:
                 cols = slice(stored, starts[k + 1])
                 nc.sync.dma_start(out=out_words[:, cols], in_=out_codes[:, cols].bitcast(I32))
                 stored = starts[k + 1]

@@ -55,11 +55,8 @@ def tile_attend_gheads_sg_pl_kernel(
             )
             return codes, scales
 
-        def score_bank():
-            return psum.tile([P, 512], F32, name="score", tag="score", bufs=3)
-
-        def turn_bank():
-            return psum.tile([P, 512], F32, name="turn", tag="turn", bufs=4)
+        def bank():
+            return psum.tile([P, 512], F32, name="bank", tag="bank", bufs=7)
 
         def ts_bank():
             return psum.tile([P, 512], F32, name="ts_bank", tag="ts_bank", bufs=1)
@@ -68,40 +65,45 @@ def tile_attend_gheads_sg_pl_kernel(
         ident = keep.tile([P, P], F32, name="ident")
         make_identity(nc, ident[:])
 
-        ts_pool = keep.tile([P, TOKENS], F32, name="ts_pool")
-        nc.vector.memset(ts_pool[:], 0.0)
+        ts_pool = keep.tile([P, TOKENS], F32, name="ts_pool", tag="x_d1", align_bytes=64)
+        ts_runs = keep.tile([P, TOKENS // P], F32, name="ts_runs", tag="x_d0", align_bytes=64)
 
-        windows = [keep.tile([P, TOKENS], F32, name="window%d" % j) for j in range(PACK - 1)]
+        windows = [keep.tile([P, TOKENS], F32, name="window%d" % j) for j in range(2)]
         for window in windows:
             nc.vector.memset(window[:], 0.0)
 
-        x_raw = [keep.tile([P, PACK, R], F32, name="x_raw%d" % h) for h in range(HEADS)]
+        x_raw = [keep.tile([P, PACK, R], F32, name="x_raw", tag="x_raw%d" % h) for h in range(HEADS)]
         table = [keep.tile([P, TOKENS], F32, name="table", tag="table%d" % j, align_bytes=64) for j in range(PACK)]
         w_planes = wT.rearrange("(p j) c -> p j c", j=PACK)
         u_col = [keep.tile([P, PACK], F32, name="u_col%d" % h) for h in range(HEADS)]
         w_col = [keep.tile([P, PACK], F32, name="w_col%d" % h) for h in range(HEADS)]
-        nc.sync.dma_start(out=x_raw[0][:], in_=xs[0].rearrange("(p j) r -> p j r", j=PACK))
+        nc.sync.dma_start(out=ts_runs[:], in_=ts[0:1, :].rearrange("o (p k) -> (o p) k", p=P))
         nc.sync.dma_start(offsets[:], offs)
+        nc.sync.dma_start(out=x_raw[0][:], in_=xs[0].rearrange("(p j) r -> p j r", j=PACK))
         nc.sync.dma_start(out=x_raw[1][:], in_=xs[1].rearrange("(p j) r -> p j r", j=PACK))
-        nc.sync.dma_start(out=ts_pool[0:1, :], in_=ts[0:1, :])
         for h in range(HEADS):
             nc.sync.dma_start(out=u_col[h][:], in_=us[h].rearrange("(m t) o -> m (t o)", t=PACK))
             nc.sync.dma_start(out=w_col[h][:], in_=ws[h].rearrange("(m t) o -> m (t o)", t=PACK))
         for j in range(PACK):
             nc.sync.dma_start(out=table[j][:], in_=w_planes[:, j, :])
-        y_sb = {}
-        for h in range(HEADS):
-            y_rows = ys[h].rearrange("(m t) i -> m t i", t=PACK)
-            for tp in range(2):
-                y_sb[h, tp] = keep.tile([P, 2, SLOTS], F32, name="y", tag="y%d_%d" % (h, tp))
-                nc.sync.dma_start(out=y_sb[h, tp][:], in_=y_rows[:, 2 * tp:2 * tp + 2, :])
 
-        x_d = [keep.tile([P, R, PACK], BF16, name="x_d%d" % h, align_bytes=64) for h in range(HEADS)]
+        for b in range(4):
+            spread = bank()
+            for k in range(4):
+                nc.tensor.transpose(
+                    spread[:, k * P:(k + 1) * P], ts_runs[:, 4 * b + k:4 * b + k + 1].to_broadcast([P, P]), ident[:]
+                )
+            nc.scalar.copy(
+                out=ts_pool[:].rearrange("q (p b k) -> q p b k", b=4, k=4)[:, :, b, :],
+                in_=spread[:].rearrange("q (k p) -> q p k", k=4),
+            )
+
+        x_d = [keep.tile([P, R, PACK], BF16, name="x_d", tag="x_d0", align_bytes=64)]
         weave(nc.scalar.copy, x_d[0][:], x_raw[0][:])
 
         ts_listed = keep.tile([P, SLOTS], F32, name="ts_listed")
         nc.vector.tensor_copy(ts_listed[:], ts_pool[:].indirect(offsets[:]))
-        ts_turned = score_bank()
+        ts_turned = bank()
         for b in range(4):
             nc.tensor.transpose(ts_turned[:, b * P:(b + 1) * P], ts_listed[:, b * P:(b + 1) * P], ident[:])
         ts_col = keep.tile([P, 4], F32, name="ts_col")
@@ -114,32 +116,33 @@ def tile_attend_gheads_sg_pl_kernel(
                 ts_spread[:, b * P:(b + 1) * P], ts_col[:, b:b + 1].to_broadcast([P, P]), ident[:]
             )
 
+        x_d.append(keep.tile([P, R, PACK], BF16, name="x_d", tag="x_d1", align_bytes=64))
         weave(nc.vector.tensor_copy, x_d[1][:], x_raw[1][:])
         xd_q = [quantize(x_d[h][:], "xd%d" % h, E4M3) for h in range(HEADS)]
+
+        y_sb = {}
+        for h in range(HEADS):
+            y_rows = ys[h].rearrange("(m t) i -> m t i", t=PACK)
+            y_all = keep.tile([P, PACK, SLOTS], F32, name="y_all", tag="x_raw%d" % h)
+            for tp in range(2):
+                y_sb[h, tp] = y_all[:, 2 * tp:2 * tp + 2, :]
+                nc.sync.dma_start(out=y_sb[h, tp], in_=y_rows[:, 2 * tp:2 * tp + 2, :])
 
         c1, c2 = [], []
         for h in range(HEADS):
             wu = keep.tile([P, PACK], F32, name="wu%d" % h)
             wuu = keep.tile([P, PACK], F32, name="wuu%d" % h)
-            nc.vector.tensor_tensor(wu[:], w_col[h][:], u_col[h][:], MULT)
-            nc.vector.tensor_tensor(wuu[:], wu[:], u_col[h][:], MULT)
+            nc.gpsimd.tensor_tensor(wu[:], w_col[h][:], u_col[h][:], MULT)
+            nc.gpsimd.tensor_tensor(wuu[:], wu[:], u_col[h][:], MULT)
             c2.append(wu)
             c1.append(wuu)
-
-        w_d = [
-            keep.tile([P, HALF, PACK], BF16, name="w_d", tag="w_d%d" % v, align_bytes=64)
-            for v in range(2)
-        ]
-        for j in range(2):
-            for v in range(2):
-                nc.vector.tensor_copy(w_d[v][:, :, j], table[j][:].indirect(offsets[:, 16 * v:16 * v + 16]))
 
         xr_q = []
         for h in range(HEADS):
             words = x_d[h][:].rearrange("p r j -> p (r j)").bitcast(F32)
             x_r = keep.tile([P, D, PACK], BF16, name="x_r%d" % h, align_bytes=64)
             for jj in range(2):
-                turned = turn_bank()
+                turned = bank()
                 for t in range(PACK):
                     nc.tensor.transpose(
                         turned[:, t * P:(t + 1) * P], words[:, 2 * t + jj:2 * R:8], ident[:]
@@ -150,111 +153,81 @@ def tile_attend_gheads_sg_pl_kernel(
                 )
             xr_q.append(quantize(x_r[:], "xr%d" % h, E4M3))
 
+        w_all = keep.tile([P, SLOTS, PACK], BF16, name="w_all", tag="x_d0", align_bytes=64)
+        w_d = [w_all[:, v * HALF:(v + 1) * HALF, :] for v in range(2)]
+        for j in range(2):
+            for v in range(2):
+                nc.vector.tensor_copy(w_d[v][:, :, j], table[j][:].indirect(offsets[:, 16 * v:16 * v + 16]))
+
         for v in range(2):
             nc.vector.tensor_copy(w_d[v][:, :, 2], table[2][:].indirect(offsets[:, 16 * v:16 * v + 16]))
         w_q = []
         for v in range(2):
             nc.vector.tensor_copy(w_d[v][:, :, 3], table[3][:].indirect(offsets[:, 16 * v:16 * v + 16]))
-            w_q.append(quantize(w_d[v][:], "w%d" % v, E4M3))
+            w_q.append(quantize(w_d[v], "w%d" % v, E4M3))
 
-        on_vector = [(0, 0, 0), (0, 0, 1), (1, 1, 1)]
-        on_gpsimd = [(0, 1, 0), (0, 1, 1), (1, 0, 0), (1, 0, 1), (1, 1, 0)]
+        on_vector = [(0, 0), (0, 1), (0, 2)]
+        on_gpsimd = [(0, 3), (1, 0), (1, 1), (1, 2), (1, 3)]
         factor = {}
-        for h, v, tp in on_gpsimd:
-            factor[h, v, tp] = keep.tile([P, 2, HALF], F32, name="factor%d%d%d" % (h, v, tp))
-            for e in range(2):
-                t = 2 * tp + e
-                nc.scalar.activation(
-                    factor[h, v, tp][:, e, :], ts_spread[:, v * HALF:(v + 1) * HALF], COPY, scale=c2[h][:, t:t + 1]
-                )
+        factors = keep.tile([P, len(on_gpsimd), SLOTS], F32, name="factors", tag="x_d1", align_bytes=64)
+        for n, (h, t) in enumerate(on_gpsimd):
+            factor[h, t] = factors[:, n, :]
+            nc.scalar.activation(factor[h, t], ts_spread[:], COPY, scale=c2[h][:, t:t + 1])
         targets = {}
-        held = keep.tile([P, PACK, HALF], F32, name="held", tag="w_d1", align_bytes=64)
-        for h, v, tp in on_vector + on_gpsimd:
-            if (h, v) == (0, 1):
-                targets[h, v, tp] = held[:, 2 * tp:2 * tp + 2, :]
-            else:
-                targets[h, v, tp] = keep.tile([P, 2, HALF], F32, name="target%d%d%d" % (h, v, tp))[:]
-
-        def vector_target(h, v, tp):
-            for e in range(2):
-                t = 2 * tp + e
-                nc.vector.scalar_tensor_tensor(
-                    targets[h, v, tp][:, e, :], y_sb[h, tp][:, e, v * HALF:(v + 1) * HALF], c2[h][:, t:t + 1],
-                    ts_spread[:, v * HALF:(v + 1) * HALF], MULT, MULT,
-                )
-
-        for h, v, tp in on_gpsimd:
-            nc.gpsimd.tensor_tensor(
-                targets[h, v, tp], y_sb[h, tp][:, :, v * HALF:(v + 1) * HALF], factor[h, v, tp][:], MULT
+        held = keep.tile([P, HEADS, PACK, SLOTS], F32, name="held", tag="x_d0", align_bytes=64)
+        for h, t in on_vector + on_gpsimd:
+            targets[h, t] = held[:, h, t, :]
+        for h, t in on_gpsimd:
+            nc.gpsimd.tensor_tensor(targets[h, t], y_sb[h, t // 2][:, t % 2, :], factor[h, t], MULT)
+        for h, t in on_vector:
+            nc.vector.scalar_tensor_tensor(
+                targets[h, t], y_sb[h, t // 2][:, t % 2, :], c2[h][:, t:t + 1], ts_spread[:], MULT, MULT
             )
-        for unit in on_vector[:2]:
-            vector_target(*unit)
 
-        scaled = {}
-
-        def score(n):
-            h, b = divmod(n, 4)
-            a = score_bank()
-            cols = slice(b % 2 * P, (b % 2 + 1) * P)
-            w_codes, w_scales = w_q[b // 2]
-            nc.tensor.matmul_mx(
-                out=a[:], lhsT=w_codes[:, cols].bitcast(E4M3), lhsT_scale=w_scales[:, cols],
-                rhs=xd_q[h][0][:].bitcast(E4M3), rhs_scale=xd_q[h][1][:], start=True, stop=True,
-            )
-            s = ring.tile([P, PACK, P], F32, name="stage", tag="stage", bufs=6)
-            nc.scalar.activation(
-                s[:], a[:].rearrange("i (m t) -> i t m", t=PACK), COPY, scale=ts2_col[:, b:b + 1]
-            )
-            scaled[n] = s
-
-        g_planes = {}
-
-        def gradient_unit(h, v):
-            banks = [turn_bank() for tp in range(2)]
-            for bb in range(2):
-                for t in range(PACK):
-                    at = t % 2 * HALF + bb * P
-                    nc.tensor.transpose(banks[t // 2][:, at:at + P], scaled[4 * h + 2 * v + bb][:, t, :], ident[:])
-            planes = keep.tile([P, PACK, HALF], BF16, name="g_planes%d%d" % (h, v))
-            for t in ((2, 3, 0, 1) if (h, v) == (1, 1) else range(PACK)):
-                if (h, v, t) == (1, 1, 2):
-                    vector_target(*on_vector[2])
-                nc.vector.scalar_tensor_tensor(
-                    planes[:, t, :], banks[t // 2][:, t % 2 * HALF:(t % 2 + 1) * HALF], c1[h][:, t:t + 1],
-                    targets[h, v, t // 2][:, t % 2, :], MULT, SUB,
-                )
-            g_planes[h, v] = planes
-
-        for n in range(3):
-            score(n)
-        for u in range(4):
-            gradient_unit(*divmod(u, 2))
-            for n in range(2 * u + 3, min(2 * u + 5, 8)):
-                score(n)
-
-        g_q = []
+        scaled = []
         for h in range(HEADS):
-            codes = keep.tile([P, SLOTS], U32, name="g_codes", tag="g%d_codes" % h, align_bytes=64)
-            scales = keep.tile([P, SLOTS], U8, name="g_scales", tag="g%d_scales" % h, align_bytes=64)
-            for v in range(2):
-                g_r = keep.tile([P, HALF, PACK], BF16, name="g_r", tag="g_r%d%d" % (h, v), align_bytes=64)
-                weave(nc.vector.tensor_copy if (h, v) == (1, 1) else nc.scalar.copy, g_r[:], g_planes[h, v][:])
-                cols = slice(v * HALF, (v + 1) * HALF)
-                nc.vector.quantize_mx(
-                    out=codes[:, cols].bitcast(E5M2), scales=scales[:, cols], in_=g_r[:].rearrange("p c t -> p (c t)")
+            for b in range(4):
+                a = bank()
+                cols = slice(b % 2 * P, (b % 2 + 1) * P)
+                w_codes, w_scales = w_q[b // 2]
+                nc.tensor.matmul_mx(
+                    out=a[:], lhsT=w_codes[:, cols].bitcast(E4M3), lhsT_scale=w_scales[:, cols],
+                    rhs=xd_q[h][0][:].bitcast(E4M3), rhs_scale=xd_q[h][1][:], start=True, stop=True,
                 )
-            g_q.append((codes, scales))
-        last_window = keep.tile([P, TOKENS], F32, name="last_window", tag="g_r11", align_bytes=64)
-        nc.vector.memset(last_window[:], 0.0)
-        windows.append(last_window)
+                s = ring.tile([P, PACK, P], F32, name="stage", tag="stage", bufs=8)
+                nc.scalar.activation(
+                    s[:], a[:].rearrange("i (m t) -> i t m", t=PACK), COPY, scale=ts2_col[:, b:b + 1]
+                )
+                scaled.append(s)
+        g_planes = []
+        for h in range(HEADS):
+            banks = [ts_bank() if (h, t) == (1, 0) else bank() for t in range(PACK)]
+            for t in range(PACK):
+                for b in range(4):
+                    nc.tensor.transpose(banks[t][:, b * P:(b + 1) * P], scaled[4 * h + b][:, t, :], ident[:])
+            planes = keep.tile([P, PACK, SLOTS], BF16, name="g_planes%d" % h)
+            for t in range(PACK):
+                nc.vector.scalar_tensor_tensor(
+                    planes[:, t, :], banks[t][:], c1[h][:, t:t + 1], targets[h, t], MULT, SUB
+                )
+            g_planes.append(planes)
+
+        g_r = [keep.tile([P, SLOTS, PACK], BF16, name="g_r", tag="g_r%d" % h, align_bytes=64) for h in range(HEADS)]
+        weave(nc.scalar.copy, g_r[0][:], g_planes[0][:])
+        weave(nc.vector.tensor_copy, g_r[1][:, 0:320, :], g_planes[1][:, :, 0:320])
+        weave(nc.scalar.copy, g_r[1][:, 320:, :], g_planes[1][:, :, 320:])
+        g_q = [quantize(g_r[h][:], "g%d" % h, E5M2) for h in range(HEADS)]
+        for freed in ("g_r1", "g1_scales"):
+            late_window = keep.tile([P, TOKENS], F32, name="late_window", tag=freed, align_bytes=64)
+            windows.append(late_window)
 
         chunks = len(CHUNKS)
         starts = [sum(CHUNKS[:k]) for k in range(chunks + 1)]
         out_rows = out_0.rearrange("(p j) c -> p j c", j=PACK)
         sums = []
-        accs = [score_bank() for j in range(PACK - 1)] + [ts_bank()]
-        for h in range(HEADS):
-            for j in range(PACK):
+        accs = [bank() for j in range(PACK)]
+        for pair in range(2):
+            for h, j in ((h, j) for h in range(HEADS) for j in (2 * pair, 2 * pair + 1)):
                 cols = slice(j * P, (j + 1) * P)
                 nc.tensor.matmul_mx(
                     out=accs[j][:], lhsT=xr_q[h][0][:, cols].bitcast(E4M3), lhsT_scale=xr_q[h][1][:, cols],
@@ -262,9 +235,11 @@ def tile_attend_gheads_sg_pl_kernel(
                     start=(h == 0), stop=(h == HEADS - 1),
                 )
         for j in range(PACK):
-            dw = ring.tile([P, SLOTS], F32, name="dw", tag="stage", bufs=6)
+            dw = ring.tile([P, SLOTS], F32, name="dw", tag="stage", bufs=8)
             nc.scalar.copy(dw[:], accs[j][:])
             sums.append(dw)
+        for window in windows[2:]:
+            nc.gpsimd.memset(window[:], 0.0)
         pairs = keep.tile([P, TOKENS // RUN, 2, RUN, 2], BF16, name="pairs", tag="xr1_codes", align_bytes=64)
         for j in range(PACK):
             nc.vector.tensor_copy(windows[j][:].indirect(offsets[:]), sums[j][:])

@@ -23,7 +23,7 @@ HEADS = 2
 HALF = SLOTS // 2
 CHUNKS = (256, 512, 512, 256, 256, 256)
 RUN = 128
-ON_SCALAR = (5,)
+ON_SCALAR = (4, 5)
 STORE_AFTER = (1, 3, 5)
 FLOPS = 4 * 2 * 512 * 512 * 512
 
@@ -46,9 +46,9 @@ def tile_attend_gheads_sg_pl_kernel(
         ring = ctx.enter_context(tc.tile_pool(name="ring", bufs=2))
         psum = ctx.enter_context(tc.psum_pool(name="psum", bufs=1))
 
-        def quantize(src, name, fmt):
+        def quantize(src, name, fmt, codes_tag=None):
             width = src.shape[1]
-            codes = keep.tile([P, width], U32, name=name + "_codes", tag=name + "_codes", align_bytes=64)
+            codes = keep.tile([P, width], U32, name=name + "_codes", tag=codes_tag or name + "_codes", align_bytes=64)
             scales = keep.tile([P, width], U8, name=name + "_scales", tag=name + "_scales", align_bytes=64)
             nc.vector.quantize_mx(
                 out=codes[:].bitcast(fmt), scales=scales[:], in_=src.rearrange("p c t -> p (c t)")
@@ -68,7 +68,7 @@ def tile_attend_gheads_sg_pl_kernel(
         ts_pool = keep.tile([P, TOKENS], F32, name="ts_pool", tag="x_d1", align_bytes=64)
         ts_runs = keep.tile([P, TOKENS // P], F32, name="ts_runs", tag="x_d0", align_bytes=64)
 
-        windows = [keep.tile([P, TOKENS], F32, name="window%d" % j) for j in range(2)]
+        windows = [keep.tile([P, TOKENS], F32, name="window%d" % j) for j in range(3)]
         for window in windows:
             nc.vector.memset(window[:], 0.0)
 
@@ -137,10 +137,10 @@ def tile_attend_gheads_sg_pl_kernel(
             c2.append(wu)
             c1.append(wuu)
 
-        xr_q = []
+        x_rs = []
         for h in range(HEADS):
             words = x_d[h][:].rearrange("p r j -> p (r j)").bitcast(F32)
-            x_r = keep.tile([P, D, PACK], BF16, name="x_r%d" % h, align_bytes=64)
+            x_r = keep.tile([P, D, PACK], BF16, name="x_r", tag="x_r%d" % h, align_bytes=64)
             for jj in range(2):
                 turned = bank()
                 for t in range(PACK):
@@ -151,8 +151,9 @@ def tile_attend_gheads_sg_pl_kernel(
                     out=x_r[:, jj * 256:(jj + 1) * 256, :].rearrange("s (e p) t -> s e p t", e=2),
                     in_=turned[:].bitcast(BF16).rearrange("s (t p e) -> s e p t", t=PACK, e=2),
                 )
-            xr_q.append(quantize(x_r[:], "xr%d" % h, E4M3))
+            x_rs.append(x_r)
 
+        xr_q = [quantize(x_rs[0][:], "xr0", E4M3)]
         w_all = keep.tile([P, SLOTS, PACK], BF16, name="w_all", tag="x_d0", align_bytes=64)
         w_d = [w_all[:, v * HALF:(v + 1) * HALF, :] for v in range(2)]
         for j in range(2):
@@ -166,6 +167,7 @@ def tile_attend_gheads_sg_pl_kernel(
             nc.vector.tensor_copy(w_d[v][:, :, 3], table[3][:].indirect(offsets[:, 16 * v:16 * v + 16]))
             w_q.append(quantize(w_d[v], "w%d" % v, E4M3))
 
+        xr_q.append(quantize(x_rs[1][:], "xr1", E4M3, "x_d0"))
         on_vector = [(0, 0), (0, 1), (0, 2)]
         on_gpsimd = [(0, 3), (1, 0), (1, 1), (1, 2), (1, 3)]
         factor = {}
@@ -174,15 +176,11 @@ def tile_attend_gheads_sg_pl_kernel(
             factor[h, t] = factors[:, n, :]
             nc.scalar.activation(factor[h, t], ts_spread[:], COPY, scale=c2[h][:, t:t + 1])
         targets = {}
-        held = keep.tile([P, HEADS, PACK, SLOTS], F32, name="held", tag="x_d0", align_bytes=64)
+        held = keep.tile([P, HEADS, PACK, SLOTS], F32, name="held", tag="x_r1", align_bytes=64)
         for h, t in on_vector + on_gpsimd:
             targets[h, t] = held[:, h, t, :]
         for h, t in on_gpsimd:
             nc.gpsimd.tensor_tensor(targets[h, t], y_sb[h, t // 2][:, t % 2, :], factor[h, t], MULT)
-        for h, t in on_vector:
-            nc.vector.scalar_tensor_tensor(
-                targets[h, t], y_sb[h, t // 2][:, t % 2, :], c2[h][:, t:t + 1], ts_spread[:], MULT, MULT
-            )
 
         scaled = []
         for h in range(HEADS):
@@ -195,10 +193,17 @@ def tile_attend_gheads_sg_pl_kernel(
                     rhs=xd_q[h][0][:].bitcast(E4M3), rhs_scale=xd_q[h][1][:], start=True, stop=True,
                 )
                 s = ring.tile([P, PACK, P], F32, name="stage", tag="stage", bufs=8)
-                nc.scalar.activation(
-                    s[:], a[:].rearrange("i (m t) -> i t m", t=PACK), COPY, scale=ts2_col[:, b:b + 1]
-                )
+                if (h, b) == (0, 3):
+                    nc.vector.tensor_scalar_mul(s[:], a[:].rearrange("i (m t) -> i t m", t=PACK), ts2_col[:, b:b + 1])
+                else:
+                    nc.scalar.activation(
+                        s[:], a[:].rearrange("i (m t) -> i t m", t=PACK), COPY, scale=ts2_col[:, b:b + 1]
+                    )
                 scaled.append(s)
+        for h, t in on_vector:
+            nc.vector.scalar_tensor_tensor(
+                targets[h, t], y_sb[h, t // 2][:, t % 2, :], c2[h][:, t:t + 1], ts_spread[:], MULT, MULT
+            )
         g_planes = []
         for h in range(HEADS):
             banks = [ts_bank() if (h, t) == (1, 0) else bank() for t in range(PACK)]
@@ -217,8 +222,9 @@ def tile_attend_gheads_sg_pl_kernel(
         weave(nc.vector.tensor_copy, g_r[1][:, 0:320, :], g_planes[1][:, :, 0:320])
         weave(nc.scalar.copy, g_r[1][:, 320:, :], g_planes[1][:, :, 320:])
         g_q = [quantize(g_r[h][:], "g%d" % h, E5M2) for h in range(HEADS)]
-        for freed in ("g_r1", "g1_scales"):
+        for freed in ("g_r1",):
             late_window = keep.tile([P, TOKENS], F32, name="late_window", tag=freed, align_bytes=64)
+            nc.vector.memset(late_window[:], 0.0)
             windows.append(late_window)
 
         chunks = len(CHUNKS)
@@ -226,8 +232,8 @@ def tile_attend_gheads_sg_pl_kernel(
         out_rows = out_0.rearrange("(p j) c -> p j c", j=PACK)
         sums = []
         accs = [bank() for j in range(PACK)]
-        for pair in range(2):
-            for h, j in ((h, j) for h in range(HEADS) for j in (2 * pair, 2 * pair + 1)):
+        for j in range(PACK):
+            for h in range(HEADS):
                 cols = slice(j * P, (j + 1) * P)
                 nc.tensor.matmul_mx(
                     out=accs[j][:], lhsT=xr_q[h][0][:, cols].bitcast(E4M3), lhsT_scale=xr_q[h][1][:, cols],
@@ -238,18 +244,22 @@ def tile_attend_gheads_sg_pl_kernel(
             dw = ring.tile([P, SLOTS], F32, name="dw", tag="stage", bufs=8)
             nc.scalar.copy(dw[:], accs[j][:])
             sums.append(dw)
-        for window in windows[2:]:
-            nc.gpsimd.memset(window[:], 0.0)
-        pairs = keep.tile([P, TOKENS // RUN, 2, RUN, 2], BF16, name="pairs", tag="xr1_codes", align_bytes=64)
+        pairs = keep.tile([P, TOKENS // RUN, 2, RUN, 2], BF16, name="pairs", tag="x_d0", align_bytes=64)
+
+        def cast(copy, j, lo, hi):
+            copy(
+                pairs[:, lo // RUN:hi // RUN, j // 2, :, j % 2],
+                windows[j][:, lo:hi].rearrange("p (k c) -> p k c", c=RUN),
+            )
+
         for j in range(PACK):
             nc.vector.tensor_copy(windows[j][:].indirect(offsets[:]), sums[j][:])
             nc.sync.dma_start(out=out_rows[:, j, :], in_=windows[j][:])
-            cuts = starts if j == PACK - 1 else (0, TOKENS)
+            cuts = ((0, TOKENS), (0, TOKENS), (starts[1], TOKENS), starts[1:])[j]
             for lo, hi in zip(cuts[:-1], cuts[1:]):
-                nc.scalar.copy(
-                    pairs[:, lo // RUN:hi // RUN, j // 2, :, j % 2],
-                    windows[j][:, lo:hi].rearrange("p (k c) -> p k c", c=RUN),
-                )
+                cast(nc.scalar.copy, j, lo, hi)
+        for j in (2, 3):
+            cast(nc.vector.tensor_copy, j, 0, starts[1])
 
         out_words = out_1.rearrange("a p c l -> p (a c l)").bitcast(I32)
         scale_rows = out_2.rearrange("a f c -> (a f) c").bitcast(I32)

@@ -154,20 +154,20 @@ def tile_attend_gheads_sg_pl_kernel(
             x_rs.append(x_r)
 
         xr_q = [quantize(x_rs[0][:], "xr0", E4M3)]
-        w_all = keep.tile([P, SLOTS, PACK], BF16, name="w_all", tag="x_d0", align_bytes=64)
-        w_d = [w_all[:, v * HALF:(v + 1) * HALF, :] for v in range(2)]
-        for j in range(2):
-            for v in range(2):
-                nc.vector.tensor_copy(w_d[v][:, :, j], table[j][:].indirect(offsets[:, 16 * v:16 * v + 16]))
-
+        w_listed = keep.tile([P, PACK, SLOTS], BF16, name="w_listed", tag="x_d0", align_bytes=64)
+        for j in range(PACK - 1):
+            nc.vector.tensor_copy(w_listed[:, j, :], table[j][:].indirect(offsets[:]))
         for v in range(2):
-            nc.vector.tensor_copy(w_d[v][:, :, 2], table[2][:].indirect(offsets[:, 16 * v:16 * v + 16]))
-        w_q = []
-        for v in range(2):
-            nc.vector.tensor_copy(w_d[v][:, :, 3], table[3][:].indirect(offsets[:, 16 * v:16 * v + 16]))
-            w_q.append(quantize(w_d[v], "w%d" % v, E4M3))
+            cols = slice(v * HALF, (v + 1) * HALF)
+            nc.vector.tensor_copy(w_listed[:, 3, cols], table[3][:].indirect(offsets[:, 16 * v:16 * v + 16]))
+        w_d = [keep.tile([P, HALF, PACK], BF16, name="w_d", tag="w_d%d" % v, align_bytes=64) for v in range(2)]
+        weave(nc.scalar.copy, w_d[0][:], w_listed[:, :, 0:HALF])
+        weave(nc.vector.tensor_copy, w_d[1][:], w_listed[:, :, HALF:])
+        w_q = [None, None]
+        for v in (1, 0):
+            w_q[v] = quantize(w_d[v][:], "w%d" % v, E4M3)
 
-        xr_q.append(quantize(x_rs[1][:], "xr1", E4M3, "x_d0"))
+        xr_q.append(quantize(x_rs[1][:], "xr1", E4M3, "w_d0"))
         on_vector = [(0, 0), (0, 1), (0, 2)]
         on_gpsimd = [(0, 3), (1, 0), (1, 1), (1, 2), (1, 3)]
         factor = {}
@@ -182,9 +182,9 @@ def tile_attend_gheads_sg_pl_kernel(
         for h, t in on_gpsimd:
             nc.gpsimd.tensor_tensor(targets[h, t], y_sb[h, t // 2][:, t % 2, :], factor[h, t], MULT)
 
-        scaled = []
+        scaled = {}
         for h in range(HEADS):
-            for b in range(4):
+            for b in (2, 3, 0, 1):
                 a = bank()
                 cols = slice(b % 2 * P, (b % 2 + 1) * P)
                 w_codes, w_scales = w_q[b // 2]
@@ -193,13 +193,13 @@ def tile_attend_gheads_sg_pl_kernel(
                     rhs=xd_q[h][0][:].bitcast(E4M3), rhs_scale=xd_q[h][1][:], start=True, stop=True,
                 )
                 s = ring.tile([P, PACK, P], F32, name="stage", tag="stage", bufs=8)
-                if (h, b) == (0, 3):
+                if (h, b) == (0, 1):
                     nc.vector.tensor_scalar_mul(s[:], a[:].rearrange("i (m t) -> i t m", t=PACK), ts2_col[:, b:b + 1])
                 else:
                     nc.scalar.activation(
                         s[:], a[:].rearrange("i (m t) -> i t m", t=PACK), COPY, scale=ts2_col[:, b:b + 1]
                     )
-                scaled.append(s)
+                scaled[4 * h + b] = s
         for h, t in on_vector:
             nc.vector.scalar_tensor_tensor(
                 targets[h, t], y_sb[h, t // 2][:, t % 2, :], c2[h][:, t:t + 1], ts_spread[:], MULT, MULT
@@ -208,7 +208,7 @@ def tile_attend_gheads_sg_pl_kernel(
         for h in range(HEADS):
             banks = [ts_bank() if (h, t) == (1, 0) else bank() for t in range(PACK)]
             for t in range(PACK):
-                for b in range(4):
+                for b in (2, 3, 0, 1):
                     nc.tensor.transpose(banks[t][:, b * P:(b + 1) * P], scaled[4 * h + b][:, t, :], ident[:])
             planes = keep.tile([P, PACK, SLOTS], BF16, name="g_planes%d" % h)
             for t in range(PACK):
@@ -244,7 +244,7 @@ def tile_attend_gheads_sg_pl_kernel(
             dw = ring.tile([P, SLOTS], F32, name="dw", tag="stage", bufs=8)
             nc.scalar.copy(dw[:], accs[j][:])
             sums.append(dw)
-        pairs = keep.tile([P, TOKENS // RUN, 2, RUN, 2], BF16, name="pairs", tag="x_d0", align_bytes=64)
+        pairs = keep.tile([P, TOKENS // RUN, 2, RUN, 2], BF16, name="pairs", tag="w_d0", align_bytes=64)
 
         def cast(copy, j, lo, hi):
             copy(

@@ -12,6 +12,7 @@ U8 = mybir.dt.uint8
 E4M3 = mybir.dt.float8_e4m3fn_x4
 E5M2 = mybir.dt.float8_e5m2_x4
 MULT = mybir.AluOpType.mult
+ADD = mybir.AluOpType.add
 SUB = mybir.AluOpType.subtract
 COPY = mybir.ActivationFunctionType.Copy
 SQUARE = mybir.ActivationFunctionType.Square
@@ -21,10 +22,10 @@ PACK = 4
 D, R, SLOTS, TOKENS = 512, 512, 512, 2048
 HEADS = 2
 HALF = SLOTS // 2
-CHUNKS = (256, 512, 512, 256, 256, 256)
+CHUNKS = (256, 512, 256, 512, 256, 256)
 RUN = 128
 ON_SCALAR = (4, 5)
-STORE_AFTER = (1, 3, 5)
+STORE_AFTER = (2, 4, 5)
 FLOPS = 4 * 2 * 512 * 512 * 512
 
 
@@ -46,9 +47,9 @@ def tile_attend_gheads_sg_pl_kernel(
         ring = ctx.enter_context(tc.tile_pool(name="ring", bufs=2))
         psum = ctx.enter_context(tc.psum_pool(name="psum", bufs=1))
 
-        def quantize(src, name, fmt, codes_tag=None):
+        def quantize(src, name, fmt):
             width = src.shape[1]
-            codes = keep.tile([P, width], U32, name=name + "_codes", tag=codes_tag or name + "_codes", align_bytes=64)
+            codes = keep.tile([P, width], U32, name=name + "_codes", tag=name + "_codes", align_bytes=64)
             scales = keep.tile([P, width], U8, name=name + "_scales", tag=name + "_scales", align_bytes=64)
             nc.vector.quantize_mx(
                 out=codes[:].bitcast(fmt), scales=scales[:], in_=src.rearrange("p c t -> p (c t)")
@@ -68,7 +69,7 @@ def tile_attend_gheads_sg_pl_kernel(
         ts_pool = keep.tile([P, TOKENS], F32, name="ts_pool", tag="x_d1", align_bytes=64)
         ts_runs = keep.tile([P, TOKENS // P], F32, name="ts_runs", tag="x_d0", align_bytes=64)
 
-        windows = [keep.tile([P, TOKENS], F32, name="window%d" % j) for j in range(3)]
+        windows = [keep.tile([P, TOKENS], F32, name="window%d" % j) for j in range(2)]
         for window in windows:
             nc.vector.memset(window[:], 0.0)
 
@@ -153,7 +154,7 @@ def tile_attend_gheads_sg_pl_kernel(
                 )
             x_rs.append(x_r)
 
-        xr_q = [quantize(x_rs[0][:], "xr0", E4M3)]
+        xr_first = [quantize(x_rs[h][:, 0:P, :], "xr%d" % h, E4M3) for h in range(HEADS)]
         w_listed = keep.tile([P, PACK, SLOTS], BF16, name="w_listed", tag="x_d0", align_bytes=64)
         for j in range(PACK - 1):
             nc.vector.tensor_copy(w_listed[:, j, :], table[j][:].indirect(offsets[:]))
@@ -167,20 +168,27 @@ def tile_attend_gheads_sg_pl_kernel(
         for v in (1, 0):
             w_q[v] = quantize(w_d[v][:], "w%d" % v, E4M3)
 
-        xr_q.append(quantize(x_rs[1][:], "xr1", E4M3, "w_d0"))
         on_vector = [(0, 0), (0, 1), (0, 2)]
         on_gpsimd = [(0, 3), (1, 0), (1, 1), (1, 2), (1, 3)]
         factor = {}
         factors = keep.tile([P, len(on_gpsimd), SLOTS], F32, name="factors", tag="x_d1", align_bytes=64)
         for n, (h, t) in enumerate(on_gpsimd):
             factor[h, t] = factors[:, n, :]
-            nc.scalar.activation(factor[h, t], ts_spread[:], COPY, scale=c2[h][:, t:t + 1])
+            nc.gpsimd.tensor_scalar(factor[h, t], ts_listed[:], c2[h][:, t:t + 1], 0.0, MULT, ADD)
         targets = {}
-        held = keep.tile([P, HEADS, PACK, SLOTS], F32, name="held", tag="x_r1", align_bytes=64)
+        held = keep.tile([P, HEADS, PACK, SLOTS], F32, name="held", tag="w_d0", align_bytes=64)
         for h, t in on_vector + on_gpsimd:
             targets[h, t] = held[:, h, t, :]
         for h, t in on_gpsimd:
             nc.gpsimd.tensor_tensor(targets[h, t], y_sb[h, t // 2][:, t % 2, :], factor[h, t], MULT)
+
+        warm = bank()
+        nc.tensor.transpose(warm[:, 0:P], table[3][:, 0:P], ident[:])
+        for n in range(4):
+            nc.tensor.matmul_mx(
+                out=warm[:], lhsT=xd_q[0][0][:, 0:P].bitcast(E4M3), lhsT_scale=xd_q[0][1][:, 0:P],
+                rhs=xd_q[1][0][:].bitcast(E4M3), rhs_scale=xd_q[1][1][:], start=True, stop=True,
+            )
 
         scaled = {}
         for h in range(HEADS):
@@ -210,7 +218,7 @@ def tile_attend_gheads_sg_pl_kernel(
             for t in range(PACK):
                 for b in (2, 3, 0, 1):
                     nc.tensor.transpose(banks[t][:, b * P:(b + 1) * P], scaled[4 * h + b][:, t, :], ident[:])
-            planes = keep.tile([P, PACK, SLOTS], BF16, name="g_planes%d" % h)
+            planes = keep.tile([P, PACK, SLOTS], BF16, name="g_planes", tag="g_planes%d" % h, align_bytes=64)
             for t in range(PACK):
                 nc.vector.scalar_tensor_tensor(
                     planes[:, t, :], banks[t][:], c1[h][:, t:t + 1], targets[h, t], MULT, SUB
@@ -219,12 +227,20 @@ def tile_attend_gheads_sg_pl_kernel(
 
         g_r = [keep.tile([P, SLOTS, PACK], BF16, name="g_r", tag="g_r%d" % h, align_bytes=64) for h in range(HEADS)]
         weave(nc.scalar.copy, g_r[0][:], g_planes[0][:])
+        g_q = [quantize(g_r[0][:], "g0", E5M2)]
         weave(nc.vector.tensor_copy, g_r[1][:, 0:320, :], g_planes[1][:, :, 0:320])
         weave(nc.scalar.copy, g_r[1][:, 320:, :], g_planes[1][:, :, 320:])
-        g_q = [quantize(g_r[h][:], "g%d" % h, E5M2) for h in range(HEADS)]
-        for freed in ("g_r1",):
+        g_q.append(quantize(g_r[1][:], "g1", E5M2))
+        rest_codes = keep.tile([P, HEADS, D - P], U32, name="rest_codes", tag="g_planes1", align_bytes=64)
+        rest_scales = keep.tile([P, HEADS, D - P], U8, name="rest_scales", align_bytes=64)
+        for lo, hi in ((P, 2 * P), (2 * P, D)):
+            for h in range(HEADS):
+                nc.vector.quantize_mx(
+                    out=rest_codes[:, h, lo - P:hi - P].bitcast(E4M3), scales=rest_scales[:, h, lo - P:hi - P],
+                    in_=x_rs[h][:, lo:hi, :].rearrange("p c t -> p (c t)"),
+                )
+        for freed in ("x_r1", "g1_scales"):
             late_window = keep.tile([P, TOKENS], F32, name="late_window", tag=freed, align_bytes=64)
-            nc.vector.memset(late_window[:], 0.0)
             windows.append(late_window)
 
         chunks = len(CHUNKS)
@@ -233,18 +249,21 @@ def tile_attend_gheads_sg_pl_kernel(
         sums = []
         accs = [bank() for j in range(PACK)]
         for j in range(PACK):
-            for h in range(HEADS):
-                cols = slice(j * P, (j + 1) * P)
+            for n, h in enumerate((0, 1) if j == 0 else (1, 0)):
+                cols = slice((j - 1) * P, j * P)
+                codes, scales = (t[:] for t in xr_first[h]) if j == 0 else (rest_codes[:, h, cols], rest_scales[:, h, cols])
                 nc.tensor.matmul_mx(
-                    out=accs[j][:], lhsT=xr_q[h][0][:, cols].bitcast(E4M3), lhsT_scale=xr_q[h][1][:, cols],
+                    out=accs[j][:], lhsT=codes.bitcast(E4M3), lhsT_scale=scales,
                     rhs=g_q[h][0][:].bitcast(E5M2), rhs_scale=g_q[h][1][:],
-                    start=(h == 0), stop=(h == HEADS - 1),
+                    start=(n == 0), stop=(n == 1),
                 )
         for j in range(PACK):
             dw = ring.tile([P, SLOTS], F32, name="dw", tag="stage", bufs=8)
             nc.scalar.copy(dw[:], accs[j][:])
             sums.append(dw)
-        pairs = keep.tile([P, TOKENS // RUN, 2, RUN, 2], BF16, name="pairs", tag="w_d0", align_bytes=64)
+        for window in windows[2:]:
+            nc.gpsimd.memset(window[:], 0.0)
+        pairs = keep.tile([P, TOKENS // RUN, 2, RUN, 2], BF16, name="pairs", tag="g_planes1", align_bytes=64)
 
         def cast(copy, j, lo, hi):
             copy(
@@ -263,7 +282,7 @@ def tile_attend_gheads_sg_pl_kernel(
 
         out_words = out_1.rearrange("a p c l -> p (a c l)").bitcast(I32)
         scale_rows = out_2.rearrange("a f c -> (a f) c").bitcast(I32)
-        out_scales = keep.tile([P, TOKENS], U8, name="out_scales", align_bytes=64)
+        out_scales = keep.tile([P, TOKENS // 2], U8, name="out_scales", align_bytes=64)
         out_codes = keep.tile([P, TOKENS], U32, name="out_codes", align_bytes=64)
         woven = [keep.tile([P, CHUNKS[k], PACK], BF16, name="woven", tag="table%d" % k, align_bytes=64) for k in range(chunks)]
 
@@ -281,8 +300,9 @@ def tile_attend_gheads_sg_pl_kernel(
             if k + 1 < chunks:
                 weave_chunk(k + 1)
             cols = slice(starts[k], starts[k + 1])
+            side, at = divmod(starts[k], TOKENS // 2)
             nc.vector.quantize_mx(
-                out=out_codes[:, cols].bitcast(E4M3), scales=out_scales[:, cols],
+                out=out_codes[:, cols].bitcast(E4M3), scales=out_scales[4 * side:, at:at + CHUNKS[k]],
                 in_=woven[k][:].rearrange("p c t -> p (c t)"),
             )
             if k in STORE_AFTER:
@@ -290,7 +310,7 @@ def tile_attend_gheads_sg_pl_kernel(
                 nc.sync.dma_start(out=out_words[:, cols], in_=out_codes[:, cols].bitcast(I32))
                 stored = starts[k + 1]
         for quad in range(4):
-            nc.sync.dma_start(
-                out=scale_rows[4 * quad:4 * quad + 4, :],
-                in_=out_scales[32 * quad:32 * quad + 4, :].bitcast(I32),
+            (nc.sync, nc.scalar)[quad % 2].dma_start(
+                out=scale_rows[4 * quad:4 * quad + 4, :].rearrange("f (a c) -> a f c", a=2),
+                in_=out_scales[32 * quad:32 * quad + 8, :].bitcast(I32),
             )

@@ -22,10 +22,9 @@ PACK = 4
 D, R, SLOTS, TOKENS = 512, 512, 512, 2048
 HEADS = 2
 HALF = SLOTS // 2
-CHUNKS = (256, 512, 256, 512, 256, 256)
-RUN = 128
-ON_SCALAR = (4, 5)
-STORE_AFTER = (2, 4, 5)
+CHUNKS = (512, 256, 128, 128, 512, 256, 256)
+ON_VECTOR = 3
+STORE_AFTER = (3, 5, 6)
 FLOPS = 4 * 2 * 512 * 512 * 512
 
 
@@ -263,47 +262,37 @@ def tile_attend_gheads_sg_pl_kernel(
             sums.append(dw)
         for window in windows[2:]:
             nc.gpsimd.memset(window[:], 0.0)
-        pairs = keep.tile([P, TOKENS // RUN, 2, RUN, 2], BF16, name="pairs", tag="g_planes1", align_bytes=64)
+        woven = keep.tile([P, TOKENS, PACK], BF16, name="woven", tag="g_planes1", align_bytes=64)
 
         def cast(copy, j, lo, hi):
-            copy(
-                pairs[:, lo // RUN:hi // RUN, j // 2, :, j % 2],
-                windows[j][:, lo:hi].rearrange("p (k c) -> p k c", c=RUN),
-            )
+            copy(woven[:, lo:hi, j], windows[j][:, lo:hi])
 
         for j in range(PACK):
             nc.vector.tensor_copy(windows[j][:].indirect(offsets[:]), sums[j][:])
             nc.sync.dma_start(out=out_rows[:, j, :], in_=windows[j][:])
-            cuts = ((0, TOKENS), (0, TOKENS), (starts[1], TOKENS), starts[1:])[j]
-            for lo, hi in zip(cuts[:-1], cuts[1:]):
-                cast(nc.scalar.copy, j, lo, hi)
-        for j in (2, 3):
-            cast(nc.vector.tensor_copy, j, 0, starts[1])
+            if j < PACK - 1:
+                split = (TOKENS // 2, TOKENS // 2, starts[ON_VECTOR])[j]
+                if j < 2:
+                    cast(nc.gpsimd.tensor_copy, j, 0, split)
+                else:
+                    nc.gpsimd.tensor_copy(
+                        woven[:, 0:split, 2:4], windows[j][:, 0:split].unsqueeze(2).to_broadcast([P, split, 2])
+                    )
+                cast(nc.scalar.copy, j, split, TOKENS)
 
         out_words = out_1.rearrange("a p c l -> p (a c l)").bitcast(I32)
         scale_rows = out_2.rearrange("a f c -> (a f) c").bitcast(I32)
         out_scales = keep.tile([P, TOKENS // 2], U8, name="out_scales", align_bytes=64)
-        out_codes = keep.tile([P, TOKENS], U32, name="out_codes", align_bytes=64)
-        woven = [keep.tile([P, CHUNKS[k], PACK], BF16, name="woven", tag="table%d" % k, align_bytes=64) for k in range(chunks)]
-
-        def weave_chunk(k):
-            copy, word = (nc.scalar.copy, U32) if k in ON_SCALAR else (nc.vector.tensor_copy, I32)
-            words = pairs[:].rearrange("p k u c e -> p (k u c e)").bitcast(word)[:, 2 * starts[k]:2 * starts[k + 1]]
-            copy(
-                out=woven[k][:].rearrange("p c t -> p (c t)").bitcast(word).rearrange("p (k c i u) -> p k c u i", c=RUN // 4, i=4, u=2),
-                in_=words.rearrange("p (k u c i) -> p k c u i", u=2, c=RUN // 4, i=4),
-            )
-
-        weave_chunk(0)
+        out_codes = keep.tile([P, TOKENS], U32, name="out_codes", tag="x_r1", align_bytes=64)
+        for k in range(chunks):
+            cast(nc.vector.tensor_copy if k < ON_VECTOR else nc.scalar.copy, PACK - 1, starts[k], starts[k + 1])
         stored = 0
         for k in range(chunks):
-            if k + 1 < chunks:
-                weave_chunk(k + 1)
             cols = slice(starts[k], starts[k + 1])
             side, at = divmod(starts[k], TOKENS // 2)
             nc.vector.quantize_mx(
                 out=out_codes[:, cols].bitcast(E4M3), scales=out_scales[4 * side:, at:at + CHUNKS[k]],
-                in_=woven[k][:].rearrange("p c t -> p (c t)"),
+                in_=woven[:, cols, :].rearrange("p c t -> p (c t)"),
             )
             if k in STORE_AFTER:
                 cols = slice(stored, starts[k + 1])

@@ -66,11 +66,11 @@ def tile_attend_gheads_sg_pl_kernel(
         make_identity(nc, ident[:])
 
         ts_pool = keep.tile([P, TOKENS], F32, name="ts_pool", tag="x_d1", align_bytes=64)
-        ts_runs = keep.tile([P, TOKENS // P], F32, name="ts_runs", tag="x_d0", align_bytes=64)
+        ts_runs = keep.tile([P, TOKENS // P], F32, name="ts_runs")
 
         windows = [keep.tile([P, TOKENS], F32, name="window%d" % j) for j in range(2)]
         for window in windows:
-            nc.vector.memset(window[:], 0.0)
+            nc.gpsimd.memset(window[:], 0.0)
 
         x_raw = [keep.tile([P, PACK, R], F32, name="x_raw", tag="x_raw%d" % h) for h in range(HEADS)]
         table = [keep.tile([P, TOKENS], F32, name="table", tag="table%d" % j, align_bytes=64) for j in range(PACK)]
@@ -99,7 +99,7 @@ def tile_attend_gheads_sg_pl_kernel(
             )
 
         x_d = [keep.tile([P, R, PACK], BF16, name="x_d", tag="x_d0", align_bytes=64)]
-        weave(nc.scalar.copy, x_d[0][:], x_raw[0][:])
+        weave(nc.vector.tensor_copy, x_d[0][:], x_raw[0][:])
 
         ts_listed = keep.tile([P, SLOTS], F32, name="ts_listed")
         nc.vector.tensor_copy(ts_listed[:], ts_pool[:].indirect(offsets[:]))

@@ -12,7 +12,6 @@ U8 = mybir.dt.uint8
 E4M3 = mybir.dt.float8_e4m3fn_x4
 E5M2 = mybir.dt.float8_e5m2_x4
 MULT = mybir.AluOpType.mult
-ADD = mybir.AluOpType.add
 SUB = mybir.AluOpType.subtract
 COPY = mybir.ActivationFunctionType.Copy
 SQUARE = mybir.ActivationFunctionType.Square
@@ -22,9 +21,11 @@ PACK = 4
 D, R, SLOTS, TOKENS = 512, 512, 512, 2048
 HEADS = 2
 HALF = SLOTS // 2
-CHUNKS = (512, 256, 128, 128, 512, 256, 256)
-ON_VECTOR = 3
-STORE_AFTER = (3, 5, 6)
+CHUNKS = (512, 256, 256, 512, 256, 256)
+VECTOR_COLUMNS = 896
+VECTOR_SLOTS = 304
+PIECES = ((0, 128), (128, 256), (256, 512))
+STORE_AFTER = (2, 4, 5)
 FLOPS = 4 * 2 * 512 * 512 * 512
 
 
@@ -137,10 +138,11 @@ def tile_attend_gheads_sg_pl_kernel(
             c2.append(wu)
             c1.append(wuu)
 
-        x_rs = []
+        shared = keep.tile([P, (PACK - 1) * SLOTS + HEADS * D * PACK], BF16, name="shared", tag="x_d0", align_bytes=64)
+        w_listed = shared[:, 0:PACK * SLOTS].rearrange("p (j i) -> p j i", j=PACK)
+        x_r = shared[:, (PACK - 1) * SLOTS:].rearrange("s (j h p t) -> s j h p t", j=PACK, h=HEADS, t=PACK)
         for h in range(HEADS):
             words = x_d[h][:].rearrange("p r j -> p (r j)").bitcast(F32)
-            x_r = keep.tile([P, D, PACK], BF16, name="x_r", tag="x_r%d" % h, align_bytes=64)
             for jj in range(2):
                 turned = bank()
                 for t in range(PACK):
@@ -148,41 +150,54 @@ def tile_attend_gheads_sg_pl_kernel(
                         turned[:, t * P:(t + 1) * P], words[:, 2 * t + jj:2 * R:8], ident[:]
                     )
                 nc.scalar.copy(
-                    out=x_r[:, jj * 256:(jj + 1) * 256, :].rearrange("s (e p) t -> s e p t", e=2),
+                    out=x_r[:, 2 * jj:2 * jj + 2, h, :, :],
                     in_=turned[:].bitcast(BF16).rearrange("s (t p e) -> s e p t", t=PACK, e=2),
                 )
-            x_rs.append(x_r)
 
-        xr_first = [quantize(x_rs[h][:, 0:P, :], "xr%d" % h, E4M3) for h in range(HEADS)]
-        w_listed = keep.tile([P, PACK, SLOTS], BF16, name="w_listed", tag="x_d0", align_bytes=64)
+        def x_planes(lo, hi):
+            return x_r[:, lo:hi, :, :, :].rearrange("s j h p t -> s (j h p) t")
+
         for j in range(PACK - 1):
             nc.vector.tensor_copy(w_listed[:, j, :], table[j][:].indirect(offsets[:]))
-        for v in range(2):
-            cols = slice(v * HALF, (v + 1) * HALF)
-            nc.vector.tensor_copy(w_listed[:, 3, cols], table[3][:].indirect(offsets[:, 16 * v:16 * v + 16]))
-        w_d = [keep.tile([P, HALF, PACK], BF16, name="w_d", tag="w_d%d" % v, align_bytes=64) for v in range(2)]
-        weave(nc.scalar.copy, w_d[0][:], w_listed[:, :, 0:HALF])
-        weave(nc.vector.tensor_copy, w_d[1][:], w_listed[:, :, HALF:])
-        w_q = [None, None]
-        for v in (1, 0):
-            w_q[v] = quantize(w_d[v][:], "w%d" % v, E4M3)
+        xr_first = quantize(x_planes(0, 1), "xr", E4M3)
+        for lo, hi in PIECES:
+            nc.vector.tensor_copy(w_listed[:, 3, lo:hi], table[3][:].indirect(offsets[:, lo // 16:hi // 16]))
+        w_q = []
+        for n, (lo, hi) in enumerate(PIECES):
+            w_d = keep.tile([P, hi - lo, PACK], BF16, name="w_d", tag="w_d%d" % (n % 2), align_bytes=64)
+            weave(nc.scalar.copy if n < 2 else nc.vector.tensor_copy, w_d[:], w_listed[:, :, lo:hi])
+            if n < 2:
+                early = w_d
+            if n == 0:
+                w_q.append(quantize(w_d[:], "w0", E4M3))
+                continue
+            if n == 2:
+                w_q.append(quantize(early[:], "w1", E4M3))
+                w_q.append(quantize(w_d[:], "w2", E4M3))
 
-        on_vector = [(0, 0), (0, 1), (0, 2)]
-        on_gpsimd = [(0, 3), (1, 0), (1, 1), (1, 2), (1, 3)]
-        factor = {}
-        factors = keep.tile([P, len(on_gpsimd), SLOTS], F32, name="factors", tag="x_d1", align_bytes=64)
-        for n, (h, t) in enumerate(on_gpsimd):
-            factor[h, t] = factors[:, n, :]
-            nc.gpsimd.tensor_scalar(factor[h, t], ts_listed[:], c2[h][:, t:t + 1], 0.0, MULT, ADD)
-        targets = {}
-        held = keep.tile([P, HEADS, PACK, SLOTS], F32, name="held", tag="w_d0", align_bytes=64)
-        for h, t in on_vector + on_gpsimd:
-            targets[h, t] = held[:, h, t, :]
-        for h, t in on_gpsimd:
-            nc.gpsimd.tensor_tensor(targets[h, t], y_sb[h, t // 2][:, t % 2, :], factor[h, t], MULT)
+        third_window = keep.tile([P, TOKENS], F32, name="third_window", tag="x_d1", align_bytes=64)
+        nc.gpsimd.memset(third_window[:], 0.0)
+        windows.append(third_window)
+
+        factors = keep.tile([P, PACK * SLOTS + HALF], F32, name="factors", align_bytes=64)
+        nc.scalar.activation(factors[:, 0:HALF], ts_listed[:, HALF:], COPY, scale=c2[0][:, 3:4])
+        for t in range(PACK):
+            first = HALF + t * SLOTS
+            nc.scalar.activation(factors[:, first:first + SLOTS], ts_listed[:], COPY, scale=c2[1][:, t:t + 1])
+        held = keep.tile([P, HEADS * PACK * SLOTS], F32, name="held", tag="w_d0", align_bytes=64)
+        targets = {
+            (h, t): held[:, (h * PACK + t) * SLOTS:(h * PACK + t + 1) * SLOTS] for h in range(HEADS) for t in range(PACK)
+        }
+        nc.gpsimd.tensor_tensor(targets[0, 3][:, HALF:], y_sb[0, 1][:, 1, HALF:], factors[:, 0:HALF], MULT)
+        for tp in range(2):
+            first = 2 * tp * SLOTS
+            nc.gpsimd.tensor_tensor(
+                held[:, PACK * SLOTS + first:PACK * SLOTS + first + 2 * SLOTS],
+                y_sb[1, tp].rearrange("p t i -> p (t i)"), factors[:, HALF + first:HALF + first + 2 * SLOTS], MULT,
+            )
 
         warm = bank()
-        nc.tensor.transpose(warm[:, 0:P], table[3][:, 0:P], ident[:])
+        nc.tensor.transpose(warm[:, 0:P], w_listed[:, 2, 0:2 * P].bitcast(F32), ident[:])
         for n in range(4):
             nc.tensor.matmul_mx(
                 out=warm[:], lhsT=xd_q[0][0][:, 0:P].bitcast(E4M3), lhsT_scale=xd_q[0][1][:, 0:P],
@@ -191,31 +206,30 @@ def tile_attend_gheads_sg_pl_kernel(
 
         scaled = {}
         for h in range(HEADS):
-            for b in (2, 3, 0, 1):
+            for b in range(4):
                 a = bank()
-                cols = slice(b % 2 * P, (b % 2 + 1) * P)
-                w_codes, w_scales = w_q[b // 2]
+                cols = slice(P, 2 * P) if b == 3 else slice(0, P)
+                w_codes, w_scales = w_q[min(b, 2)]
                 nc.tensor.matmul_mx(
                     out=a[:], lhsT=w_codes[:, cols].bitcast(E4M3), lhsT_scale=w_scales[:, cols],
                     rhs=xd_q[h][0][:].bitcast(E4M3), rhs_scale=xd_q[h][1][:], start=True, stop=True,
                 )
                 s = ring.tile([P, PACK, P], F32, name="stage", tag="stage", bufs=8)
-                if (h, b) == (0, 1):
-                    nc.vector.tensor_scalar_mul(s[:], a[:].rearrange("i (m t) -> i t m", t=PACK), ts2_col[:, b:b + 1])
-                else:
-                    nc.scalar.activation(
-                        s[:], a[:].rearrange("i (m t) -> i t m", t=PACK), COPY, scale=ts2_col[:, b:b + 1]
-                    )
+                nc.scalar.activation(
+                    s[:], a[:].rearrange("i (m t) -> i t m", t=PACK), COPY, scale=ts2_col[:, b:b + 1]
+                )
                 scaled[4 * h + b] = s
-        for h, t in on_vector:
+        for t in range(PACK):
+            width = SLOTS if t < PACK - 1 else HALF
             nc.vector.scalar_tensor_tensor(
-                targets[h, t], y_sb[h, t // 2][:, t % 2, :], c2[h][:, t:t + 1], ts_spread[:], MULT, MULT
+                targets[0, t][:, 0:width], y_sb[0, t // 2][:, t % 2, 0:width], c2[0][:, t:t + 1],
+                ts_spread[:, 0:width], MULT, MULT,
             )
         g_planes = []
         for h in range(HEADS):
             banks = [ts_bank() if (h, t) == (1, 0) else bank() for t in range(PACK)]
             for t in range(PACK):
-                for b in (2, 3, 0, 1):
+                for b in range(4):
                     nc.tensor.transpose(banks[t][:, b * P:(b + 1) * P], scaled[4 * h + b][:, t, :], ident[:])
             planes = keep.tile([P, PACK, SLOTS], BF16, name="g_planes", tag="g_planes%d" % h, align_bytes=64)
             for t in range(PACK):
@@ -226,21 +240,20 @@ def tile_attend_gheads_sg_pl_kernel(
 
         g_r = [keep.tile([P, SLOTS, PACK], BF16, name="g_r", tag="g_r%d" % h, align_bytes=64) for h in range(HEADS)]
         weave(nc.scalar.copy, g_r[0][:], g_planes[0][:])
+        weave(nc.vector.tensor_copy, g_r[1][:, 0:VECTOR_SLOTS, :], g_planes[1][:, :, 0:VECTOR_SLOTS])
         g_q = [quantize(g_r[0][:], "g0", E5M2)]
-        weave(nc.vector.tensor_copy, g_r[1][:, 0:320, :], g_planes[1][:, :, 0:320])
-        weave(nc.scalar.copy, g_r[1][:, 320:, :], g_planes[1][:, :, 320:])
+        weave(nc.scalar.copy, g_r[1][:, VECTOR_SLOTS:, :], g_planes[1][:, :, VECTOR_SLOTS:])
         g_q.append(quantize(g_r[1][:], "g1", E5M2))
-        rest_codes = keep.tile([P, HEADS, D - P], U32, name="rest_codes", tag="g_planes1", align_bytes=64)
-        rest_scales = keep.tile([P, HEADS, D - P], U8, name="rest_scales", align_bytes=64)
-        for lo, hi in ((P, 2 * P), (2 * P, D)):
-            for h in range(HEADS):
-                nc.vector.quantize_mx(
-                    out=rest_codes[:, h, lo - P:hi - P].bitcast(E4M3), scales=rest_scales[:, h, lo - P:hi - P],
-                    in_=x_rs[h][:, lo:hi, :].rearrange("p c t -> p (c t)"),
-                )
-        for freed in ("x_r1", "g1_scales"):
-            late_window = keep.tile([P, TOKENS], F32, name="late_window", tag=freed, align_bytes=64)
-            windows.append(late_window)
+        rest_codes = keep.tile([P, HEADS * (D - P)], U32, name="rest_codes", tag="g_r1", align_bytes=64)
+        rest_scales = keep.tile([P, HEADS * (D - P)], U8, name="rest_scales", align_bytes=64)
+        for lo, hi in ((1, 2), (2, PACK)):
+            cols = slice((lo - 1) * HEADS * P, (hi - 1) * HEADS * P)
+            nc.vector.quantize_mx(
+                out=rest_codes[:, cols].bitcast(E4M3), scales=rest_scales[:, cols],
+                in_=x_planes(lo, hi).rearrange("p c t -> p (c t)"),
+            )
+        late_window = keep.tile([P, TOKENS], F32, name="late_window", tag="x_d0", align_bytes=64)
+        windows.append(late_window)
 
         chunks = len(CHUNKS)
         starts = [sum(CHUNKS[:k]) for k in range(chunks + 1)]
@@ -249,8 +262,8 @@ def tile_attend_gheads_sg_pl_kernel(
         accs = [bank() for j in range(PACK)]
         for j in range(PACK):
             for n, h in enumerate((0, 1) if j == 0 else (1, 0)):
-                cols = slice((j - 1) * P, j * P)
-                codes, scales = (t[:] for t in xr_first[h]) if j == 0 else (rest_codes[:, h, cols], rest_scales[:, h, cols])
+                first = (max(j - 1, 0) * HEADS + h) * P
+                codes, scales = (t[:, first:first + P] for t in (xr_first if j == 0 else (rest_codes, rest_scales)))
                 nc.tensor.matmul_mx(
                     out=accs[j][:], lhsT=codes.bitcast(E4M3), lhsT_scale=scales,
                     rhs=g_q[h][0][:].bitcast(E5M2), rhs_scale=g_q[h][1][:],
@@ -260,9 +273,8 @@ def tile_attend_gheads_sg_pl_kernel(
             dw = ring.tile([P, SLOTS], F32, name="dw", tag="stage", bufs=8)
             nc.scalar.copy(dw[:], accs[j][:])
             sums.append(dw)
-        for window in windows[2:]:
-            nc.gpsimd.memset(window[:], 0.0)
-        woven = keep.tile([P, TOKENS, PACK], BF16, name="woven", tag="g_planes1", align_bytes=64)
+        nc.gpsimd.memset(late_window[:], 0.0)
+        woven = keep.tile([P, TOKENS, PACK], BF16, name="woven", tag="g_r1", align_bytes=64)
 
         def cast(copy, j, lo, hi):
             copy(woven[:, lo:hi, j], windows[j][:, lo:hi])
@@ -271,7 +283,7 @@ def tile_attend_gheads_sg_pl_kernel(
             nc.vector.tensor_copy(windows[j][:].indirect(offsets[:]), sums[j][:])
             nc.sync.dma_start(out=out_rows[:, j, :], in_=windows[j][:])
             if j < PACK - 1:
-                split = (TOKENS // 2, TOKENS // 2, starts[ON_VECTOR])[j]
+                split = (TOKENS // 2, TOKENS // 2, VECTOR_COLUMNS)[j]
                 if j < 2:
                     cast(nc.gpsimd.tensor_copy, j, 0, split)
                 else:
@@ -283,9 +295,10 @@ def tile_attend_gheads_sg_pl_kernel(
         out_words = out_1.rearrange("a p c l -> p (a c l)").bitcast(I32)
         scale_rows = out_2.rearrange("a f c -> (a f) c").bitcast(I32)
         out_scales = keep.tile([P, TOKENS // 2], U8, name="out_scales", align_bytes=64)
-        out_codes = keep.tile([P, TOKENS], U32, name="out_codes", tag="x_r1", align_bytes=64)
-        for k in range(chunks):
-            cast(nc.vector.tensor_copy if k < ON_VECTOR else nc.scalar.copy, PACK - 1, starts[k], starts[k + 1])
+        out_codes = keep.tile([P, TOKENS], U32, name="out_codes", align_bytes=64)
+        cuts = sorted(starts + [VECTOR_COLUMNS])
+        for lo, hi in zip(cuts, cuts[1:]):
+            cast(nc.vector.tensor_copy if lo < VECTOR_COLUMNS else nc.scalar.copy, PACK - 1, lo, hi)
         stored = 0
         for k in range(chunks):
             cols = slice(starts[k], starts[k + 1])

@@ -36,6 +36,10 @@ def weave(engine_copy, out, in_):
     )
 
 
+def deal(out, in_):
+    return out.rearrange("p (t s) j -> p s j t", t=4), in_.rearrange("p j (s t) -> p s j t", t=4)
+
+
 def tile_attend_gheads_sg_pl_kernel(
     tc, x1, x2, wT, y1, u1, w1, y2, u2, w2, ts, offs, out_0, out_1, out_2
 ):
@@ -100,7 +104,7 @@ def tile_attend_gheads_sg_pl_kernel(
             )
 
         x_d = [keep.tile([P, R, PACK], BF16, name="x_d", tag="x_d0", align_bytes=64)]
-        weave(nc.vector.tensor_copy, x_d[0][:], x_raw[0][:])
+        nc.vector.tensor_copy(*deal(x_d[0][:], x_raw[0][:]))
 
         ts_listed = keep.tile([P, SLOTS], F32, name="ts_listed")
         nc.vector.tensor_copy(ts_listed[:], ts_pool[:].indirect(offsets[:]))
@@ -118,7 +122,7 @@ def tile_attend_gheads_sg_pl_kernel(
             )
 
         x_d.append(keep.tile([P, R, PACK], BF16, name="x_d", tag="x_d1", align_bytes=64))
-        weave(nc.vector.tensor_copy, x_d[1][:], x_raw[1][:])
+        nc.vector.tensor_copy(*deal(x_d[1][:], x_raw[1][:]))
         xd_q = [quantize(x_d[h][:], "xd%d" % h, E4M3) for h in range(HEADS)]
 
         y_sb = {}
@@ -147,7 +151,7 @@ def tile_attend_gheads_sg_pl_kernel(
                 turned = bank()
                 for t in range(PACK):
                     nc.tensor.transpose(
-                        turned[:, t * P:(t + 1) * P], words[:, 2 * t + jj:2 * R:8], ident[:]
+                        turned[:, t * P:(t + 1) * P], words[:, 2 * t * P + jj:2 * (t + 1) * P:2], ident[:]
                     )
                 nc.scalar.copy(
                     out=x_r[:, 2 * jj:2 * jj + 2, h, :, :],
@@ -216,7 +220,7 @@ def tile_attend_gheads_sg_pl_kernel(
                 )
                 s = ring.tile([P, PACK, P], F32, name="stage", tag="stage", bufs=8)
                 nc.scalar.activation(
-                    s[:], a[:].rearrange("i (m t) -> i t m", t=PACK), COPY, scale=ts2_col[:, b:b + 1]
+                    s[:], a[:].rearrange("i (t m) -> i t m", t=PACK), COPY, scale=ts2_col[:, b:b + 1]
                 )
                 scaled[4 * h + b] = s
         for t in range(PACK):

@@ -22,7 +22,9 @@ D, R, SLOTS, TOKENS = 512, 512, 512, 2048
 HEADS = 2
 HALF = SLOTS // 2
 CHUNKS = (512, 256, 256, 512, 256, 256)
-VECTOR_COLUMNS = 896
+VECTOR_COLUMNS = 960
+GPSIMD_COLUMNS = 1008
+TIE = 16
 VECTOR_SLOTS = 304
 PIECES = ((0, 128), (128, 256), (256, 512))
 STORE_AFTER = (2, 4, 5)
@@ -261,6 +263,8 @@ def tile_attend_gheads_sg_pl_kernel(
 
         chunks = len(CHUNKS)
         starts = [sum(CHUNKS[:k]) for k in range(chunks + 1)]
+        vector_casts = ((0, VECTOR_COLUMNS // 2), (VECTOR_COLUMNS // 2, VECTOR_COLUMNS))
+        scalar_casts = ((VECTOR_COLUMNS, starts[3]), (starts[3], starts[4]), (starts[4], starts[5]), (starts[5], TOKENS))
         out_rows = out_0.rearrange("(p j) c -> p j c", j=PACK)
         sums = []
         accs = [bank() for j in range(PACK)]
@@ -287,12 +291,15 @@ def tile_attend_gheads_sg_pl_kernel(
             nc.vector.tensor_copy(windows[j][:].indirect(offsets[:]), sums[j][:])
             nc.sync.dma_start(out=out_rows[:, j, :], in_=windows[j][:])
             if j < PACK - 1:
-                split = (TOKENS // 2, TOKENS // 2, VECTOR_COLUMNS)[j]
+                split = (GPSIMD_COLUMNS, GPSIMD_COLUMNS, VECTOR_COLUMNS)[j]
                 if j < 2:
                     cast(nc.gpsimd.tensor_copy, j, 0, split)
                 else:
+                    lanes = woven[:, 0:split, :].rearrange("p (h c) t -> p h c t", h=2)
+                    values = windows[j][:, 0:split].rearrange("p (h c) -> p h c", h=2)
+                    nc.gpsimd.tensor_copy(lanes[:, :, TIE:, 2], values[:, :, TIE:])
                     nc.gpsimd.tensor_copy(
-                        woven[:, 0:split, 2:4], windows[j][:, 0:split].unsqueeze(2).to_broadcast([P, split, 2])
+                        lanes[:, :, 0:TIE, 2:4], values[:, :, 0:TIE].unsqueeze(3).to_broadcast([P, 2, TIE, 2])
                     )
                 cast(nc.scalar.copy, j, split, TOKENS)
 
@@ -300,9 +307,10 @@ def tile_attend_gheads_sg_pl_kernel(
         scale_rows = out_2.rearrange("a f c -> (a f) c").bitcast(I32)
         out_scales = keep.tile([P, TOKENS // 2], U8, name="out_scales", align_bytes=64)
         out_codes = keep.tile([P, TOKENS], U32, name="out_codes", align_bytes=64)
-        cuts = sorted(starts + [VECTOR_COLUMNS])
-        for lo, hi in zip(cuts, cuts[1:]):
-            cast(nc.vector.tensor_copy if lo < VECTOR_COLUMNS else nc.scalar.copy, PACK - 1, lo, hi)
+        for lo, hi in vector_casts:
+            cast(nc.vector.tensor_copy, PACK - 1, lo, hi)
+        for lo, hi in scalar_casts:
+            cast(nc.scalar.copy, PACK - 1, lo, hi)
         stored = 0
         for k in range(chunks):
             cols = slice(starts[k], starts[k + 1])

@@ -27,7 +27,7 @@ GPSIMD_COLUMNS = 1008
 TIE = 16
 VECTOR_SLOTS = 304
 PIECES = ((0, 128), (128, 256), (256, 512))
-STORE_AFTER = (2, 4, 5)
+STORE_AFTER = (0, 2, 4, 5)
 FLOPS = 4 * 2 * 512 * 512 * 512
 
 
@@ -185,21 +185,23 @@ def tile_attend_gheads_sg_pl_kernel(
         nc.gpsimd.memset(third_window[:], 0.0)
         windows.append(third_window)
 
-        factors = keep.tile([P, PACK * SLOTS + HALF], F32, name="factors", align_bytes=64)
-        nc.scalar.activation(factors[:, 0:HALF], ts_listed[:, HALF:], COPY, scale=c2[0][:, 3:4])
+        factors = keep.tile([P, (PACK + 1) * SLOTS], F32, name="factors", align_bytes=64)
+        nc.scalar.activation(factors[:, 0:SLOTS], ts_listed[:], COPY, scale=c2[0][:, 3:4])
         for t in range(PACK):
-            first = HALF + t * SLOTS
+            first = (t + 1) * SLOTS
             nc.scalar.activation(factors[:, first:first + SLOTS], ts_listed[:], COPY, scale=c2[1][:, t:t + 1])
         held = keep.tile([P, HEADS * PACK * SLOTS], F32, name="held", tag="w_d0", align_bytes=64)
         targets = {
             (h, t): held[:, (h * PACK + t) * SLOTS:(h * PACK + t + 1) * SLOTS] for h in range(HEADS) for t in range(PACK)
         }
-        nc.gpsimd.tensor_tensor(targets[0, 3][:, HALF:], y_sb[0, 1][:, 1, HALF:], factors[:, 0:HALF], MULT)
-        for tp in range(2):
-            first = 2 * tp * SLOTS
+        nc.gpsimd.tensor_tensor(targets[0, 3], y_sb[0, 1][:, 1, :], factors[:, 0:SLOTS], MULT)
+        nc.gpsimd.tensor_tensor(
+            held[:, PACK * SLOTS:(PACK + 2) * SLOTS], y_sb[1, 0].rearrange("p t i -> p (t i)"),
+            factors[:, SLOTS:3 * SLOTS], MULT,
+        )
+        for t in (2, 3):
             nc.gpsimd.tensor_tensor(
-                held[:, PACK * SLOTS + first:PACK * SLOTS + first + 2 * SLOTS],
-                y_sb[1, tp].rearrange("p t i -> p (t i)"), factors[:, HALF + first:HALF + first + 2 * SLOTS], MULT,
+                targets[1, t], y_sb[1, 1][:, t - 2, :], factors[:, (t + 1) * SLOTS:(t + 2) * SLOTS], MULT
             )
 
         warm = bank()
@@ -221,15 +223,16 @@ def tile_attend_gheads_sg_pl_kernel(
                     rhs=xd_q[h][0][:].bitcast(E4M3), rhs_scale=xd_q[h][1][:], start=True, stop=True,
                 )
                 s = ring.tile([P, PACK, P], F32, name="stage", tag="stage", bufs=8)
-                nc.scalar.activation(
-                    s[:], a[:].rearrange("i (t m) -> i t m", t=PACK), COPY, scale=ts2_col[:, b:b + 1]
-                )
+                if (h, b) == (0, 3):
+                    nc.vector.tensor_scalar_mul(s[:], a[:].rearrange("i (t m) -> i t m", t=PACK), ts2_col[:, b:b + 1])
+                else:
+                    nc.scalar.activation(
+                        s[:], a[:].rearrange("i (t m) -> i t m", t=PACK), COPY, scale=ts2_col[:, b:b + 1]
+                    )
                 scaled[4 * h + b] = s
-        for t in range(PACK):
-            width = SLOTS if t < PACK - 1 else HALF
+        for t in range(PACK - 1):
             nc.vector.scalar_tensor_tensor(
-                targets[0, t][:, 0:width], y_sb[0, t // 2][:, t % 2, 0:width], c2[0][:, t:t + 1],
-                ts_spread[:, 0:width], MULT, MULT,
+                targets[0, t], y_sb[0, t // 2][:, t % 2, :], c2[0][:, t:t + 1], ts_spread[:], MULT, MULT
             )
         g_planes = []
         for h in range(HEADS):

@@ -21,13 +21,12 @@ PACK = 4
 D, R, SLOTS, TOKENS = 512, 512, 512, 2048
 HEADS = 2
 HALF = SLOTS // 2
-CHUNKS = (512, 256, 256, 512, 256, 256)
-VECTOR_COLUMNS = 960
-GPSIMD_COLUMNS = 1008
-TIE = 16
+CHUNKS = (512, 512, 512, 256, 128, 128)
+RUN = 128
+VECTOR_COLUMNS = 1024
 VECTOR_SLOTS = 304
 PIECES = ((0, 128), (128, 256), (256, 512))
-STORE_AFTER = (0, 2, 4, 5)
+STORE_AFTER = (0, 1, 2, 5)
 FLOPS = 4 * 2 * 512 * 512 * 512
 
 
@@ -266,10 +265,7 @@ def tile_attend_gheads_sg_pl_kernel(
 
         chunks = len(CHUNKS)
         starts = [sum(CHUNKS[:k]) for k in range(chunks + 1)]
-        vector_casts = ((0, VECTOR_COLUMNS // 2), (VECTOR_COLUMNS // 2, VECTOR_COLUMNS))
-        scalar_casts = ((VECTOR_COLUMNS, starts[3]), (starts[3], starts[4]), (starts[4], starts[5]), (starts[5], TOKENS))
         out_rows = out_0.rearrange("(p j) c -> p j c", j=PACK)
-        sums = []
         accs = [bank() for j in range(PACK)]
         for j in range(PACK):
             for n, h in enumerate((0, 1) if j == 0 else (1, 0)):
@@ -280,40 +276,46 @@ def tile_attend_gheads_sg_pl_kernel(
                     rhs=g_q[h][0][:].bitcast(E5M2), rhs_scale=g_q[h][1][:],
                     start=(n == 0), stop=(n == 1),
                 )
+        nc.gpsimd.memset(late_window[:], 0.0)
         for j in range(PACK):
             dw = ring.tile([P, SLOTS], F32, name="dw", tag="stage", bufs=8)
-            nc.scalar.copy(dw[:], accs[j][:])
-            sums.append(dw)
-        nc.gpsimd.memset(late_window[:], 0.0)
+            if j % 2 == 0:
+                nc.vector.tensor_copy(dw[:], accs[j][:])
+                nc.vector.tensor_copy(windows[j][:].indirect(offsets[:]), dw[:])
+            else:
+                nc.scalar.copy(dw[:], accs[j][:])
+                for lo in (0, HALF):
+                    nc.scalar.activation(
+                        windows[j][:].indirect(offsets[:, lo // 16:(lo + HALF) // 16]), dw[:, lo:lo + HALF], COPY
+                    )
+            nc.sync.dma_start(out=out_rows[:, j, :], in_=windows[j][:])
+
+        rounded = keep.tile([P, TOKENS * PACK], BF16, name="rounded", align_bytes=64)
+        runs = rounded[:].rearrange("p (k j c) -> p k j c", j=PACK, c=RUN)
         woven = keep.tile([P, TOKENS, PACK], BF16, name="woven", tag="g_r1", align_bytes=64)
 
         def cast(copy, j, lo, hi):
-            copy(woven[:, lo:hi, j], windows[j][:, lo:hi])
+            copy(runs[:, lo // RUN:hi // RUN, j, :], windows[j][:, lo:hi].rearrange("p (k c) -> p k c", c=RUN))
 
-        for j in range(PACK):
-            nc.vector.tensor_copy(windows[j][:].indirect(offsets[:]), sums[j][:])
-            nc.sync.dma_start(out=out_rows[:, j, :], in_=windows[j][:])
-            if j < PACK - 1:
-                split = (GPSIMD_COLUMNS, GPSIMD_COLUMNS, VECTOR_COLUMNS)[j]
-                if j < 2:
-                    cast(nc.gpsimd.tensor_copy, j, 0, split)
-                else:
-                    lanes = woven[:, 0:split, :].rearrange("p (h c) t -> p h c t", h=2)
-                    values = windows[j][:, 0:split].rearrange("p (h c) -> p h c", h=2)
-                    nc.gpsimd.tensor_copy(lanes[:, :, TIE:, 2], values[:, :, TIE:])
-                    nc.gpsimd.tensor_copy(
-                        lanes[:, :, 0:TIE, 2:4], values[:, :, 0:TIE].unsqueeze(3).to_broadcast([P, 2, TIE, 2])
-                    )
-                cast(nc.scalar.copy, j, split, TOKENS)
+        def weave_runs(copy, lo, hi):
+            copy(
+                out=woven[:, lo:hi, :].rearrange("p (k c i) t -> p k c t i", i=4, c=RUN // 4),
+                in_=runs[:, lo // RUN:hi // RUN, :, :].rearrange("p k t (c i) -> p k c t i", i=4),
+            )
+
+        cast(nc.gpsimd.tensor_copy, 0, 0, TOKENS)
+        cast(nc.gpsimd.tensor_copy, 1, 0, TOKENS)
+        cast(nc.vector.tensor_copy, 2, VECTOR_COLUMNS, TOKENS)
+        cast(nc.vector.tensor_copy, 2, 0, VECTOR_COLUMNS)
+        cast(nc.vector.tensor_copy, 3, 0, VECTOR_COLUMNS)
+        cast(nc.scalar.copy, 3, VECTOR_COLUMNS, TOKENS)
 
         out_words = out_1.rearrange("a p c l -> p (a c l)").bitcast(I32)
         scale_rows = out_2.rearrange("a f c -> (a f) c").bitcast(I32)
         out_scales = keep.tile([P, TOKENS // 2], U8, name="out_scales", align_bytes=64)
         out_codes = keep.tile([P, TOKENS], U32, name="out_codes", align_bytes=64)
-        for lo, hi in vector_casts:
-            cast(nc.vector.tensor_copy, PACK - 1, lo, hi)
-        for lo, hi in scalar_casts:
-            cast(nc.scalar.copy, PACK - 1, lo, hi)
+        for k in range(chunks):
+            weave_runs(nc.vector.tensor_copy if starts[k] < VECTOR_COLUMNS else nc.scalar.copy, starts[k], starts[k + 1])
         stored = 0
         for k in range(chunks):
             cols = slice(starts[k], starts[k + 1])

@@ -164,43 +164,35 @@ def tile_attend_gheads_sg_pl_kernel(
 
         for j in range(PACK - 1):
             nc.vector.tensor_copy(w_listed[:, j, :], table[j][:].indirect(offsets[:]))
-        xr_first = quantize(x_planes(0, 1), "xr", E4M3)
+        xr_first = quantize(x_planes(0, 2), "xr", E4M3)
         for lo, hi in PIECES:
-            nc.vector.tensor_copy(w_listed[:, 3, lo:hi], table[3][:].indirect(offsets[:, lo // 16:hi // 16]))
-        w_q = []
-        for n, (lo, hi) in enumerate(PIECES):
-            w_d = keep.tile([P, hi - lo, PACK], BF16, name="w_d", tag="w_d%d" % (n % 2), align_bytes=64)
+            listed = table[3][:].indirect(offsets[:, lo // 16:hi // 16])
+            if lo < HALF:
+                nc.vector.tensor_copy(w_listed[:, 3, lo:hi], listed)
+            else:
+                nc.scalar.activation(w_listed[:, 3, lo:hi], listed, COPY)
+        w_q = {}
+        for n in (2, 0, 1):
+            lo, hi = PIECES[n]
+            w_d = keep.tile([P, hi - lo, PACK], BF16, name="w_d", tag="w_d%d" % n, align_bytes=64)
             weave(nc.scalar.copy if n < 2 else nc.vector.tensor_copy, w_d[:], w_listed[:, :, lo:hi])
-            if n < 2:
-                early = w_d
-            if n == 0:
-                w_q.append(quantize(w_d[:], "w0", E4M3))
-                continue
-            if n == 2:
-                w_q.append(quantize(early[:], "w1", E4M3))
-                w_q.append(quantize(w_d[:], "w2", E4M3))
+            w_q[n] = quantize(w_d[:], "w%d" % n, E4M3)
 
         third_window = keep.tile([P, TOKENS], F32, name="third_window", tag="x_d1", align_bytes=64)
         nc.gpsimd.memset(third_window[:], 0.0)
         windows.append(third_window)
 
         factors = keep.tile([P, (PACK + 1) * SLOTS], F32, name="factors", align_bytes=64)
-        nc.scalar.activation(factors[:, 0:SLOTS], ts_listed[:], COPY, scale=c2[0][:, 3:4])
-        for t in range(PACK):
-            first = (t + 1) * SLOTS
-            nc.scalar.activation(factors[:, first:first + SLOTS], ts_listed[:], COPY, scale=c2[1][:, t:t + 1])
-        held = keep.tile([P, HEADS * PACK * SLOTS], F32, name="held", tag="w_d0", align_bytes=64)
+        shared_out = ((0, 3), (1, 0), (1, 1), (1, 2), (1, 3))
+        for n, (h, t) in enumerate(shared_out):
+            nc.scalar.activation(factors[:, n * SLOTS:(n + 1) * SLOTS], ts_listed[:], COPY, scale=c2[h][:, t:t + 1])
+        held = keep.tile([P, HEADS * PACK * SLOTS], F32, name="held", tag="w_d1", align_bytes=64)
         targets = {
             (h, t): held[:, (h * PACK + t) * SLOTS:(h * PACK + t + 1) * SLOTS] for h in range(HEADS) for t in range(PACK)
         }
-        nc.gpsimd.tensor_tensor(targets[0, 3], y_sb[0, 1][:, 1, :], factors[:, 0:SLOTS], MULT)
-        nc.gpsimd.tensor_tensor(
-            held[:, PACK * SLOTS:(PACK + 2) * SLOTS], y_sb[1, 0].rearrange("p t i -> p (t i)"),
-            factors[:, SLOTS:3 * SLOTS], MULT,
-        )
-        for t in (2, 3):
+        for n, (h, t) in enumerate(shared_out):
             nc.gpsimd.tensor_tensor(
-                targets[1, t], y_sb[1, 1][:, t - 2, :], factors[:, (t + 1) * SLOTS:(t + 2) * SLOTS], MULT
+                targets[h, t], y_sb[h, t // 2][:, t % 2, :], factors[:, n * SLOTS:(n + 1) * SLOTS], MULT
             )
 
         warm = bank()
@@ -213,7 +205,7 @@ def tile_attend_gheads_sg_pl_kernel(
 
         scaled = {}
         for h in range(HEADS):
-            for b in range(4):
+            for b in (2, 3, 0, 1):
                 a = bank()
                 cols = slice(P, 2 * P) if b == 3 else slice(0, P)
                 w_codes, w_scales = w_q[min(b, 2)]
@@ -233,7 +225,8 @@ def tile_attend_gheads_sg_pl_kernel(
             nc.vector.scalar_tensor_tensor(
                 targets[0, t], y_sb[0, t // 2][:, t % 2, :], c2[0][:, t:t + 1], ts_spread[:], MULT, MULT
             )
-        g_planes = []
+        g_r = [keep.tile([P, SLOTS, PACK], BF16, name="g_r", tag="g_r%d" % h, align_bytes=64) for h in range(HEADS)]
+        g_q = []
         for h in range(HEADS):
             banks = [ts_bank() if (h, t) == (1, 0) else bank() for t in range(PACK)]
             for t in range(PACK):
@@ -244,51 +237,70 @@ def tile_attend_gheads_sg_pl_kernel(
                 nc.vector.scalar_tensor_tensor(
                     planes[:, t, :], banks[t][:], c1[h][:, t:t + 1], targets[h, t], MULT, SUB
                 )
-            g_planes.append(planes)
-
-        g_r = [keep.tile([P, SLOTS, PACK], BF16, name="g_r", tag="g_r%d" % h, align_bytes=64) for h in range(HEADS)]
-        weave(nc.scalar.copy, g_r[0][:], g_planes[0][:])
-        weave(nc.vector.tensor_copy, g_r[1][:, 0:VECTOR_SLOTS, :], g_planes[1][:, :, 0:VECTOR_SLOTS])
-        g_q = [quantize(g_r[0][:], "g0", E5M2)]
-        weave(nc.scalar.copy, g_r[1][:, VECTOR_SLOTS:, :], g_planes[1][:, :, VECTOR_SLOTS:])
-        g_q.append(quantize(g_r[1][:], "g1", E5M2))
-        rest_codes = keep.tile([P, HEADS * (D - P)], U32, name="rest_codes", tag="g_r1", align_bytes=64)
-        rest_scales = keep.tile([P, HEADS * (D - P)], U8, name="rest_scales", align_bytes=64)
-        for lo, hi in ((1, 2), (2, PACK)):
-            cols = slice((lo - 1) * HEADS * P, (hi - 1) * HEADS * P)
-            nc.vector.quantize_mx(
-                out=rest_codes[:, cols].bitcast(E4M3), scales=rest_scales[:, cols],
-                in_=x_planes(lo, hi).rearrange("p c t -> p (c t)"),
-            )
+            if h == 0:
+                shares = ((nc.scalar.copy, 0, HALF), (nc.scalar.copy, HALF, SLOTS))
+            else:
+                shares = (
+                    (nc.vector.tensor_copy, 0, HALF),
+                    (nc.vector.tensor_copy, HALF, VECTOR_SLOTS),
+                    (nc.scalar.copy, VECTOR_SLOTS, SLOTS),
+                )
+            for copy, lo, hi in shares:
+                weave(copy, g_r[h][:, lo:hi, :], planes[:, :, lo:hi])
+            codes = keep.tile([P, SLOTS], U32, name="g_codes%d" % h, align_bytes=64)
+            scales = keep.tile([P, SLOTS], U8, name="g_scales%d" % h, align_bytes=64)
+            for lo in (0, HALF):
+                nc.vector.quantize_mx(
+                    out=codes[:, lo:lo + HALF].bitcast(E5M2), scales=scales[:, lo:lo + HALF],
+                    in_=g_r[h][:, lo:lo + HALF, :].rearrange("p c t -> p (c t)"),
+                )
+            g_q.append((codes, scales))
+        rest_codes = keep.tile([P, D], U32, name="rest_codes", tag="g_r1", align_bytes=64)
+        rest_scales = keep.tile([P, D], U8, name="rest_scales", align_bytes=64)
+        nc.vector.quantize_mx(
+            out=rest_codes[:].bitcast(E4M3), scales=rest_scales[:],
+            in_=x_planes(2, PACK).rearrange("p c t -> p (c t)"),
+        )
         late_window = keep.tile([P, TOKENS], F32, name="late_window", tag="x_d0", align_bytes=64)
         windows.append(late_window)
 
         chunks = len(CHUNKS)
         starts = [sum(CHUNKS[:k]) for k in range(chunks + 1)]
         out_rows = out_0.rearrange("(p j) c -> p j c", j=PACK)
-        accs = [bank() for j in range(PACK)]
-        for j in range(PACK):
-            for n, h in enumerate((0, 1) if j == 0 else (1, 0)):
-                first = (max(j - 1, 0) * HEADS + h) * P
-                codes, scales = (t[:, first:first + P] for t in (xr_first if j == 0 else (rest_codes, rest_scales)))
-                nc.tensor.matmul_mx(
-                    out=accs[j][:], lhsT=codes.bitcast(E4M3), lhsT_scale=scales,
-                    rhs=g_q[h][0][:].bitcast(E5M2), rhs_scale=g_q[h][1][:],
-                    start=(n == 0), stop=(n == 1),
-                )
+        units = ((1, 0, HALF), (0, 0, HALF), (1, HALF, SLOTS), (0, HALF, SLOTS), (2, 0, SLOTS), (3, 0, SLOTS))
+        accs = [bank() for unit in units]
+
+        def gradient_pass(u, h, start):
+            j, lo, hi = units[u]
+            first = (j % 2 * HEADS + h) * P
+            codes, scales = (t[:, first:first + P] for t in (xr_first if j < 2 else (rest_codes, rest_scales)))
+            nc.tensor.matmul_mx(
+                out=accs[u][:, 0:hi - lo], lhsT=codes.bitcast(E4M3), lhsT_scale=scales,
+                rhs=g_q[h][0][:, lo:hi].bitcast(E5M2), rhs_scale=g_q[h][1][:, lo:hi],
+                start=start, stop=not start,
+            )
+
+        for h in range(HEADS):
+            for u in range(4):
+                gradient_pass(u, h, h == 0)
+        for u in (4, 5):
+            for h in range(HEADS):
+                gradient_pass(u, h, h == 0)
         nc.gpsimd.memset(late_window[:], 0.0)
-        for j in range(PACK):
-            dw = ring.tile([P, SLOTS], F32, name="dw", tag="stage", bufs=8)
+        for u, (j, lo, hi) in enumerate(units):
+            dw = ring.tile([P, hi - lo], F32, name="dw", tag="stage", bufs=8)
             if j % 2 == 0:
-                nc.vector.tensor_copy(dw[:], accs[j][:])
-                nc.vector.tensor_copy(windows[j][:].indirect(offsets[:]), dw[:])
+                nc.vector.tensor_copy(dw[:], accs[u][:, 0:hi - lo])
+                nc.vector.tensor_copy(windows[j][:].indirect(offsets[:, lo // 16:hi // 16]), dw[:])
             else:
-                nc.scalar.copy(dw[:], accs[j][:])
-                for lo in (0, HALF):
+                nc.scalar.copy(dw[:], accs[u][:, 0:hi - lo])
+                for at in range(lo, hi, HALF):
                     nc.scalar.activation(
-                        windows[j][:].indirect(offsets[:, lo // 16:(lo + HALF) // 16]), dw[:, lo:lo + HALF], COPY
+                        windows[j][:].indirect(offsets[:, at // 16:(at + HALF) // 16]),
+                        dw[:, at - lo:at - lo + HALF], COPY,
                     )
-            nc.sync.dma_start(out=out_rows[:, j, :], in_=windows[j][:])
+            if hi == SLOTS:
+                nc.sync.dma_start(out=out_rows[:, j, :], in_=windows[j][:])
 
         rounded = keep.tile([P, TOKENS * PACK], BF16, name="rounded", align_bytes=64)
         runs = rounded[:].rearrange("p (k j c) -> p k j c", j=PACK, c=RUN)
@@ -303,8 +315,8 @@ def tile_attend_gheads_sg_pl_kernel(
                 in_=runs[:, lo // RUN:hi // RUN, :, :].rearrange("p k t (c i) -> p k c t i", i=4),
             )
 
-        cast(nc.gpsimd.tensor_copy, 0, 0, TOKENS)
         cast(nc.gpsimd.tensor_copy, 1, 0, TOKENS)
+        cast(nc.gpsimd.tensor_copy, 0, 0, TOKENS)
         cast(nc.vector.tensor_copy, 2, VECTOR_COLUMNS, TOKENS)
         cast(nc.vector.tensor_copy, 2, 0, VECTOR_COLUMNS)
         cast(nc.vector.tensor_copy, 3, 0, VECTOR_COLUMNS)

@@ -22,8 +22,7 @@ D, R, SLOTS, TOKENS = 512, 512, 512, 2048
 HEADS = 2
 HALF = SLOTS // 2
 CHUNKS = (512, 512, 512, 256, 128, 128)
-RUN = 128
-VECTOR_COLUMNS = 1024
+OWN_COLUMNS = 896
 VECTOR_SLOTS = 304
 PIECES = ((0, 128), (128, 256), (256, 512))
 STORE_AFTER = (0, 1, 2, 5)
@@ -287,8 +286,14 @@ def tile_attend_gheads_sg_pl_kernel(
             for h in range(HEADS):
                 gradient_pass(u, h, h == 0)
         nc.gpsimd.memset(late_window[:], 0.0)
+        split_pairs = keep.tile([P, PACK * (TOKENS - OWN_COLUMNS)], BF16, name="split_pairs", align_bytes=64)
         for u, (j, lo, hi) in enumerate(units):
-            dw = ring.tile([P, hi - lo], F32, name="dw", tag="stage", bufs=8)
+            if j == 2:
+                dw = keep.tile([P, hi - lo], F32, name="dw", tag="own_pairs", align_bytes=64)
+            elif j == 3:
+                dw = split_pairs[:, 2 * (TOKENS - OWN_COLUMNS):].bitcast(F32)[:, HALF:HALF + SLOTS]
+            else:
+                dw = ring.tile([P, hi - lo], F32, name="dw", tag="stage", bufs=8)
             if j % 2 == 0:
                 nc.vector.tensor_copy(dw[:], accs[u][:, 0:hi - lo])
                 nc.vector.tensor_copy(windows[j][:].indirect(offsets[:, lo // 16:hi // 16]), dw[:])
@@ -302,32 +307,44 @@ def tile_attend_gheads_sg_pl_kernel(
             if hi == SLOTS:
                 nc.sync.dma_start(out=out_rows[:, j, :], in_=windows[j][:])
 
-        rounded = keep.tile([P, TOKENS * PACK], BF16, name="rounded", align_bytes=64)
-        runs = rounded[:].rearrange("p (k j c) -> p k j c", j=PACK, c=RUN)
+        pairs = (
+            keep.tile([P, 2, OWN_COLUMNS, 2], BF16, name="own_pairs", tag="own_pairs", align_bytes=64),
+            split_pairs[:].rearrange("p (u c e) -> p u c e", u=2, e=2),
+        )
         woven = keep.tile([P, TOKENS, PACK], BF16, name="woven", tag="g_r1", align_bytes=64)
 
         def cast(copy, j, lo, hi):
-            copy(runs[:, lo // RUN:hi // RUN, j, :], windows[j][:, lo:hi].rearrange("p (k c) -> p k c", c=RUN))
+            side = int(lo >= OWN_COLUMNS)
+            at = side * OWN_COLUMNS
+            copy(pairs[side][:, j // 2, lo - at:hi - at, j % 2], windows[j][:, lo:hi])
 
-        def weave_runs(copy, lo, hi):
+        def weave_words(copy, dtype, lo, hi):
+            side = int(lo >= OWN_COLUMNS)
+            at = side * OWN_COLUMNS
+            words = pairs[side][:].rearrange("p u c e -> p (u c e)").bitcast(dtype).rearrange("p (u c) -> p c u", u=2)
             copy(
-                out=woven[:, lo:hi, :].rearrange("p (k c i) t -> p k c t i", i=4, c=RUN // 4),
-                in_=runs[:, lo // RUN:hi // RUN, :, :].rearrange("p k t (c i) -> p k c t i", i=4),
+                woven[:].rearrange("p c t -> p (c t)").bitcast(dtype).rearrange("p (c u) -> p c u", u=2)[:, lo:hi, :],
+                words[:, lo - at:hi - at, :],
             )
 
-        cast(nc.gpsimd.tensor_copy, 1, 0, TOKENS)
-        cast(nc.gpsimd.tensor_copy, 0, 0, TOKENS)
-        cast(nc.vector.tensor_copy, 2, VECTOR_COLUMNS, TOKENS)
-        cast(nc.vector.tensor_copy, 2, 0, VECTOR_COLUMNS)
-        cast(nc.vector.tensor_copy, 3, 0, VECTOR_COLUMNS)
-        cast(nc.scalar.copy, 3, VECTOR_COLUMNS, TOKENS)
+        for j in (1, 0):
+            cast(nc.gpsimd.tensor_copy, j, OWN_COLUMNS, TOKENS)
+        for j in range(PACK):
+            cast(nc.vector.tensor_copy, j, 0, OWN_COLUMNS)
+        weave_words(nc.vector.tensor_copy, I32, 0, starts[1])
+        weave_words(nc.vector.tensor_copy, I32, starts[1], OWN_COLUMNS)
+        for j in (3, 2):
+            cast(nc.scalar.copy, j, OWN_COLUMNS, starts[3])
+        weave_words(nc.scalar.copy, U32, OWN_COLUMNS, starts[3])
+        for j in (3, 2):
+            cast(nc.scalar.copy, j, starts[3], TOKENS)
+        for k in range(3, chunks):
+            weave_words(nc.scalar.copy, U32, starts[k], starts[k + 1])
 
         out_words = out_1.rearrange("a p c l -> p (a c l)").bitcast(I32)
         scale_rows = out_2.rearrange("a f c -> (a f) c").bitcast(I32)
         out_scales = keep.tile([P, TOKENS // 2], U8, name="out_scales", align_bytes=64)
         out_codes = keep.tile([P, TOKENS], U32, name="out_codes", align_bytes=64)
-        for k in range(chunks):
-            weave_runs(nc.vector.tensor_copy if starts[k] < VECTOR_COLUMNS else nc.scalar.copy, starts[k], starts[k + 1])
         stored = 0
         for k in range(chunks):
             cols = slice(starts[k], starts[k + 1])

@@ -22,10 +22,10 @@ D, R, SLOTS, TOKENS = 512, 512, 512, 2048
 HEADS = 2
 HALF = SLOTS // 2
 CHUNKS = (512, 512, 512, 256, 128, 128)
-OWN_COLUMNS = 896
-VECTOR_SLOTS = 304
+OWN_COLUMNS = 1024
+VECTOR_SLOTS = 400
 PIECES = ((0, 128), (128, 256), (256, 512))
-STORE_AFTER = (0, 1, 2, 5)
+STORE_AFTER = (1, 3, 5)
 FLOPS = 4 * 2 * 512 * 512 * 512
 
 
@@ -51,9 +51,9 @@ def tile_attend_gheads_sg_pl_kernel(
         ring = ctx.enter_context(tc.tile_pool(name="ring", bufs=2))
         psum = ctx.enter_context(tc.psum_pool(name="psum", bufs=1))
 
-        def quantize(src, name, fmt):
+        def quantize(src, name, fmt, place=None):
             width = src.shape[1]
-            codes = keep.tile([P, width], U32, name=name + "_codes", tag=name + "_codes", align_bytes=64)
+            codes = keep.tile([P, width], U32, name=name + "_codes", tag=place or name + "_codes", align_bytes=64)
             scales = keep.tile([P, width], U8, name=name + "_scales", tag=name + "_scales", align_bytes=64)
             nc.vector.quantize_mx(
                 out=codes[:].bitcast(fmt), scales=scales[:], in_=src.rearrange("p c t -> p (c t)")
@@ -77,7 +77,7 @@ def tile_attend_gheads_sg_pl_kernel(
         for window in windows:
             nc.gpsimd.memset(window[:], 0.0)
 
-        x_raw = [keep.tile([P, PACK, R], F32, name="x_raw", tag="x_raw%d" % h) for h in range(HEADS)]
+        x_raw = [keep.tile([P, PACK, R], F32, name="x_raw", tag="x_raw%d" % h, align_bytes=64) for h in range(HEADS)]
         table = [keep.tile([P, TOKENS], F32, name="table", tag="table%d" % j, align_bytes=64) for j in range(PACK)]
         w_planes = wT.rearrange("(p j) c -> p j c", j=PACK)
         u_col = [keep.tile([P, PACK], F32, name="u_col%d" % h) for h in range(HEADS)]
@@ -123,14 +123,15 @@ def tile_attend_gheads_sg_pl_kernel(
 
         x_d.append(keep.tile([P, R, PACK], BF16, name="x_d", tag="x_d1", align_bytes=64))
         nc.vector.tensor_copy(*deal(x_d[1][:], x_raw[1][:]))
-        xd_q = [quantize(x_d[h][:], "xd%d" % h, E4M3) for h in range(HEADS)]
+        xd_q = [quantize(x_d[0][:], "xd0", E4M3)]
 
         y_sb = {}
+        y_all = keep.tile([P, HEADS * PACK * SLOTS], F32, name="y_all", tag="x_raw0", align_bytes=64)
         for h in range(HEADS):
             y_rows = ys[h].rearrange("(m t) i -> m t i", t=PACK)
-            y_all = keep.tile([P, PACK, SLOTS], F32, name="y_all", tag="x_raw%d" % h)
             for tp in range(2):
-                y_sb[h, tp] = y_all[:, 2 * tp:2 * tp + 2, :]
+                first = (h * PACK + 2 * tp) * SLOTS
+                y_sb[h, tp] = y_all[:, first:first + 2 * SLOTS].rearrange("p (t i) -> p t i", t=2)
                 nc.sync.dma_start(out=y_sb[h, tp], in_=y_rows[:, 2 * tp:2 * tp + 2, :])
 
         c1, c2 = [], []
@@ -163,6 +164,8 @@ def tile_attend_gheads_sg_pl_kernel(
 
         for j in range(PACK - 1):
             nc.vector.tensor_copy(w_listed[:, j, :], table[j][:].indirect(offsets[:]))
+            if j == 1:
+                xd_q.append(quantize(x_d[1][:], "xd1", E4M3, place="table1"))
         xr_first = quantize(x_planes(0, 2), "xr", E4M3)
         for lo, hi in PIECES:
             listed = table[3][:].indirect(offsets[:, lo // 16:hi // 16])
@@ -171,13 +174,16 @@ def tile_attend_gheads_sg_pl_kernel(
             else:
                 nc.scalar.activation(w_listed[:, 3, lo:hi], listed, COPY)
         w_q = {}
-        for n in (2, 0, 1):
-            lo, hi = PIECES[n]
-            w_d = keep.tile([P, hi - lo, PACK], BF16, name="w_d", tag="w_d%d" % n, align_bytes=64)
-            weave(nc.scalar.copy if n < 2 else nc.vector.tensor_copy, w_d[:], w_listed[:, :, lo:hi])
-            w_q[n] = quantize(w_d[:], "w%d" % n, E4M3)
+        w_d = {}
+        for n, (lo, hi) in enumerate(PIECES):
+            w_d[n] = keep.tile([P, hi - lo, PACK], BF16, name="w_d", tag="w_d%d" % (n % 2), align_bytes=64)
+            weave(nc.scalar.copy if n == 1 else nc.vector.tensor_copy, w_d[n][:], w_listed[:, :, lo:hi])
+            if n == 0:
+                w_q[0] = quantize(w_d[0][:], "w0", E4M3)
+        for n in (1, 2):
+            w_q[n] = quantize(w_d[n][:], "w%d" % n, E4M3)
 
-        third_window = keep.tile([P, TOKENS], F32, name="third_window", tag="x_d1", align_bytes=64)
+        third_window = keep.tile([P, TOKENS], F32, name="third_window", tag="x_raw1", align_bytes=64)
         nc.gpsimd.memset(third_window[:], 0.0)
         windows.append(third_window)
 
@@ -185,7 +191,7 @@ def tile_attend_gheads_sg_pl_kernel(
         shared_out = ((0, 3), (1, 0), (1, 1), (1, 2), (1, 3))
         for n, (h, t) in enumerate(shared_out):
             nc.scalar.activation(factors[:, n * SLOTS:(n + 1) * SLOTS], ts_listed[:], COPY, scale=c2[h][:, t:t + 1])
-        held = keep.tile([P, HEADS * PACK * SLOTS], F32, name="held", tag="w_d1", align_bytes=64)
+        held = keep.tile([P, HEADS * PACK * SLOTS], F32, name="held", tag="w_d0", align_bytes=64)
         targets = {
             (h, t): held[:, (h * PACK + t) * SLOTS:(h * PACK + t + 1) * SLOTS] for h in range(HEADS) for t in range(PACK)
         }
@@ -195,31 +201,30 @@ def tile_attend_gheads_sg_pl_kernel(
             )
 
         warm = bank()
-        nc.tensor.transpose(warm[:, 0:P], w_listed[:, 2, 0:2 * P].bitcast(F32), ident[:])
-        for n in range(4):
+        nc.tensor.transpose(warm[:, 0:P], w_listed[:, 3, 0:2].bitcast(F32).to_broadcast([P, P]), ident[:])
+        for width in (SLOTS, HALF):
             nc.tensor.matmul_mx(
-                out=warm[:], lhsT=xd_q[0][0][:, 0:P].bitcast(E4M3), lhsT_scale=xd_q[0][1][:, 0:P],
-                rhs=xd_q[1][0][:].bitcast(E4M3), rhs_scale=xd_q[1][1][:], start=True, stop=True,
+                out=warm[:, 0:width], lhsT=xd_q[0][0][:, 0:P].bitcast(E4M3), lhsT_scale=xd_q[0][1][:, 0:P],
+                rhs=xd_q[1][0][:, 0:width].bitcast(E4M3), rhs_scale=xd_q[1][1][:, 0:width], start=True, stop=True,
             )
 
         scaled = {}
-        for h in range(HEADS):
-            for b in (2, 3, 0, 1):
-                a = bank()
-                cols = slice(P, 2 * P) if b == 3 else slice(0, P)
-                w_codes, w_scales = w_q[min(b, 2)]
-                nc.tensor.matmul_mx(
-                    out=a[:], lhsT=w_codes[:, cols].bitcast(E4M3), lhsT_scale=w_scales[:, cols],
-                    rhs=xd_q[h][0][:].bitcast(E4M3), rhs_scale=xd_q[h][1][:], start=True, stop=True,
+        for h, b in ((h, b) for h in range(HEADS) for b in range(4)):
+            a = bank()
+            cols = slice(P, 2 * P) if b == 3 else slice(0, P)
+            w_codes, w_scales = w_q[min(b, 2)]
+            nc.tensor.matmul_mx(
+                out=a[:], lhsT=w_codes[:, cols].bitcast(E4M3), lhsT_scale=w_scales[:, cols],
+                rhs=xd_q[h][0][:].bitcast(E4M3), rhs_scale=xd_q[h][1][:], start=True, stop=True,
+            )
+            s = ring.tile([P, PACK, P], F32, name="stage", tag="stage", bufs=8)
+            if (h, b) == (0, 2):
+                nc.vector.tensor_scalar_mul(s[:], a[:].rearrange("i (t m) -> i t m", t=PACK), ts2_col[:, b:b + 1])
+            else:
+                nc.scalar.activation(
+                    s[:], a[:].rearrange("i (t m) -> i t m", t=PACK), COPY, scale=ts2_col[:, b:b + 1]
                 )
-                s = ring.tile([P, PACK, P], F32, name="stage", tag="stage", bufs=8)
-                if (h, b) == (0, 3):
-                    nc.vector.tensor_scalar_mul(s[:], a[:].rearrange("i (t m) -> i t m", t=PACK), ts2_col[:, b:b + 1])
-                else:
-                    nc.scalar.activation(
-                        s[:], a[:].rearrange("i (t m) -> i t m", t=PACK), COPY, scale=ts2_col[:, b:b + 1]
-                    )
-                scaled[4 * h + b] = s
+            scaled[4 * h + b] = s
         for t in range(PACK - 1):
             nc.vector.scalar_tensor_tensor(
                 targets[0, t], y_sb[0, t // 2][:, t % 2, :], c2[0][:, t:t + 1], ts_spread[:], MULT, MULT
@@ -233,14 +238,16 @@ def tile_attend_gheads_sg_pl_kernel(
                     nc.tensor.transpose(banks[t][:, b * P:(b + 1) * P], scaled[4 * h + b][:, t, :], ident[:])
             planes = keep.tile([P, PACK, SLOTS], BF16, name="g_planes", tag="g_planes%d" % h, align_bytes=64)
             for t in range(PACK):
-                nc.vector.scalar_tensor_tensor(
-                    planes[:, t, :], banks[t][:], c1[h][:, t:t + 1], targets[h, t], MULT, SUB
-                )
+                for lo, hi in ((0, HALF), (HALF, SLOTS)) if (h, t) == (1, 3) else ((0, SLOTS),):
+                    nc.vector.scalar_tensor_tensor(
+                        planes[:, t, lo:hi], banks[t][:, lo:hi], c1[h][:, t:t + 1], targets[h, t][:, lo:hi], MULT, SUB
+                    )
             if h == 0:
                 shares = ((nc.scalar.copy, 0, HALF), (nc.scalar.copy, HALF, SLOTS))
             else:
                 shares = (
-                    (nc.vector.tensor_copy, 0, HALF),
+                    (nc.scalar.copy, 0, P),
+                    (nc.vector.tensor_copy, P, HALF),
                     (nc.vector.tensor_copy, HALF, VECTOR_SLOTS),
                     (nc.scalar.copy, VECTOR_SLOTS, SLOTS),
                 )

@@ -12,6 +12,7 @@ U8 = mybir.dt.uint8
 E4M3 = mybir.dt.float8_e4m3fn_x4
 E5M2 = mybir.dt.float8_e5m2_x4
 MULT = mybir.AluOpType.mult
+ADD = mybir.AluOpType.add
 SUB = mybir.AluOpType.subtract
 COPY = mybir.ActivationFunctionType.Copy
 SQUARE = mybir.ActivationFunctionType.Square
@@ -22,7 +23,9 @@ D, R, SLOTS, TOKENS = 512, 512, 512, 2048
 HEADS = 2
 HALF = SLOTS // 2
 CHUNKS = (512, 512, 512, 256, 128, 128)
-OWN_COLUMNS = 1024
+OWN_COLUMNS = 896
+VECTOR_COLUMNS = 1024
+SPAN = TOKENS + OWN_COLUMNS
 VECTOR_SLOTS = 400
 PIECES = ((0, 128), (128, 256), (256, 512))
 STORE_AFTER = (1, 3, 5)
@@ -115,11 +118,6 @@ def tile_attend_gheads_sg_pl_kernel(
         ts2_col = keep.tile([P, 4], F32, name="ts2_col")
         nc.scalar.copy(ts_col[:], ts_turned[:, 0:512:P])
         nc.scalar.activation(ts2_col[:], ts_turned[:, 0:512:P], SQUARE)
-        ts_spread = ts_bank()
-        for b in range(4):
-            nc.tensor.transpose(
-                ts_spread[:, b * P:(b + 1) * P], ts_col[:, b:b + 1].to_broadcast([P, P]), ident[:]
-            )
 
         x_d.append(keep.tile([P, R, PACK], BF16, name="x_d", tag="x_d1", align_bytes=64))
         nc.vector.tensor_copy(*deal(x_d[1][:], x_raw[1][:]))
@@ -143,30 +141,35 @@ def tile_attend_gheads_sg_pl_kernel(
             c2.append(wu)
             c1.append(wuu)
 
-        shared = keep.tile([P, (PACK - 1) * SLOTS + HEADS * D * PACK], BF16, name="shared", tag="x_d0", align_bytes=64)
+        half_r = HEADS * D * PACK // 2
+        shared = keep.tile([P, (PACK - 1) * SLOTS + half_r], BF16, name="shared", tag="x_d0", align_bytes=64)
         w_listed = shared[:, 0:PACK * SLOTS].rearrange("p (j i) -> p j i", j=PACK)
-        x_r = shared[:, (PACK - 1) * SLOTS:].rearrange("s (j h p t) -> s j h p t", j=PACK, h=HEADS, t=PACK)
-        for h in range(HEADS):
+        x_r = [
+            shared[:, (PACK - 1) * SLOTS:],
+            keep.tile([P, half_r], BF16, name="x_r1", tag="x_r1", align_bytes=64)[:],
+        ]
+        for h, jj in ((0, 1), (0, 0), (1, 0), (1, 1)):
             words = x_d[h][:].rearrange("p r j -> p (r j)").bitcast(F32)
-            for jj in range(2):
-                turned = bank()
-                for t in range(PACK):
-                    nc.tensor.transpose(
-                        turned[:, t * P:(t + 1) * P], words[:, 2 * t * P + jj:2 * (t + 1) * P:2], ident[:]
-                    )
-                nc.scalar.copy(
-                    out=x_r[:, 2 * jj:2 * jj + 2, h, :, :],
-                    in_=turned[:].bitcast(BF16).rearrange("s (t p e) -> s e p t", t=PACK, e=2),
+            turned = ts_bank() if (h, jj) == (1, 1) else bank()
+            for t in range(PACK):
+                nc.tensor.transpose(
+                    turned[:, t * P:(t + 1) * P], words[:, 2 * t * P + jj:2 * (t + 1) * P:2], ident[:]
                 )
-
-        def x_planes(lo, hi):
-            return x_r[:, lo:hi, :, :, :].rearrange("s j h p t -> s (j h p) t")
+            nc.scalar.copy(
+                out=x_r[jj].rearrange("s (e h p t) -> s e h p t", e=2, h=HEADS, t=PACK)[:, :, h, :, :],
+                in_=turned[:].bitcast(BF16).rearrange("s (t p e) -> s e p t", t=PACK, e=2),
+            )
+        ts_spread = ts_bank()
+        for b in range(4):
+            nc.tensor.transpose(
+                ts_spread[:, b * P:(b + 1) * P], ts_col[:, b:b + 1].to_broadcast([P, P]), ident[:]
+            )
 
         for j in range(PACK - 1):
             nc.vector.tensor_copy(w_listed[:, j, :], table[j][:].indirect(offsets[:]))
             if j == 1:
                 xd_q.append(quantize(x_d[1][:], "xd1", E4M3, place="table1"))
-        xr_first = quantize(x_planes(0, 2), "xr", E4M3)
+        xr_first = quantize(x_r[0].rearrange("p (c t) -> p c t", t=PACK), "xr", E4M3)
         for lo, hi in PIECES:
             listed = table[3][:].indirect(offsets[:, lo // 16:hi // 16])
             if lo < HALF:
@@ -175,29 +178,37 @@ def tile_attend_gheads_sg_pl_kernel(
                 nc.scalar.activation(w_listed[:, 3, lo:hi], listed, COPY)
         w_q = {}
         w_d = {}
-        for n, (lo, hi) in enumerate(PIECES):
-            w_d[n] = keep.tile([P, hi - lo, PACK], BF16, name="w_d", tag="w_d%d" % (n % 2), align_bytes=64)
-            weave(nc.scalar.copy if n == 1 else nc.vector.tensor_copy, w_d[n][:], w_listed[:, :, lo:hi])
-            if n == 0:
+        for b in range(4):
+            w_d[b] = keep.tile([P, P, PACK], BF16, name="w_d", tag="w_d%d" % (b if b % 2 else 0), align_bytes=64)
+            weave(nc.scalar.copy if b % 2 else nc.vector.tensor_copy, w_d[b][:], w_listed[:, :, b * P:(b + 1) * P])
+            if b == 0:
                 w_q[0] = quantize(w_d[0][:], "w0", E4M3)
-        for n in (1, 2):
-            w_q[n] = quantize(w_d[n][:], "w%d" % n, E4M3)
+        for b in (1, 2, 3):
+            w_q[b] = quantize(w_d[b][:], "w%d" % b, E4M3)
 
         third_window = keep.tile([P, TOKENS], F32, name="third_window", tag="x_raw1", align_bytes=64)
         nc.gpsimd.memset(third_window[:], 0.0)
         windows.append(third_window)
 
-        factors = keep.tile([P, (PACK + 1) * SLOTS], F32, name="factors", align_bytes=64)
         shared_out = ((0, 3), (1, 0), (1, 1), (1, 2), (1, 3))
+        first_rows = keep.tile([P, 2 * SLOTS], F32, name="first_rows", align_bytes=64)
+        last_rows = keep.tile([P, 3 * SLOTS], F32, name="last_rows", tag="table0", align_bytes=64)
+        factors = []
         for n, (h, t) in enumerate(shared_out):
-            nc.scalar.activation(factors[:, n * SLOTS:(n + 1) * SLOTS], ts_listed[:], COPY, scale=c2[h][:, t:t + 1])
-        held = keep.tile([P, HEADS * PACK * SLOTS], F32, name="held", tag="w_d0", align_bytes=64)
+            if n < 2:
+                row = first_rows[:, n * SLOTS:(n + 1) * SLOTS]
+                nc.scalar.activation(row, ts_listed[:], COPY, scale=c2[h][:, t:t + 1])
+            else:
+                row = last_rows[:, (n - 2) * SLOTS:(n - 1) * SLOTS]
+                nc.gpsimd.tensor_scalar(row, ts_listed[:], c2[h][:, t:t + 1], 0.0, MULT, ADD)
+            factors.append(row)
+        held = keep.tile([P, HEADS * PACK * SLOTS], F32, name="held", tag="w_d3", align_bytes=64)
         targets = {
             (h, t): held[:, (h * PACK + t) * SLOTS:(h * PACK + t + 1) * SLOTS] for h in range(HEADS) for t in range(PACK)
         }
         for n, (h, t) in enumerate(shared_out):
             nc.gpsimd.tensor_tensor(
-                targets[h, t], y_sb[h, t // 2][:, t % 2, :], factors[:, n * SLOTS:(n + 1) * SLOTS], MULT
+                targets[h, t], y_sb[h, t // 2][:, t % 2, :], factors[n], MULT
             )
 
         warm = bank()
@@ -211,10 +222,9 @@ def tile_attend_gheads_sg_pl_kernel(
         scaled = {}
         for h, b in ((h, b) for h in range(HEADS) for b in range(4)):
             a = bank()
-            cols = slice(P, 2 * P) if b == 3 else slice(0, P)
-            w_codes, w_scales = w_q[min(b, 2)]
+            w_codes, w_scales = w_q[b]
             nc.tensor.matmul_mx(
-                out=a[:], lhsT=w_codes[:, cols].bitcast(E4M3), lhsT_scale=w_scales[:, cols],
+                out=a[:], lhsT=w_codes[:].bitcast(E4M3), lhsT_scale=w_scales[:],
                 rhs=xd_q[h][0][:].bitcast(E4M3), rhs_scale=xd_q[h][1][:], start=True, stop=True,
             )
             s = ring.tile([P, PACK, P], F32, name="stage", tag="stage", bufs=8)
@@ -265,9 +275,9 @@ def tile_attend_gheads_sg_pl_kernel(
         rest_scales = keep.tile([P, D], U8, name="rest_scales", align_bytes=64)
         nc.vector.quantize_mx(
             out=rest_codes[:].bitcast(E4M3), scales=rest_scales[:],
-            in_=x_planes(2, PACK).rearrange("p c t -> p (c t)"),
+            in_=x_r[1],
         )
-        late_window = keep.tile([P, TOKENS], F32, name="late_window", tag="x_d0", align_bytes=64)
+        late_window = keep.tile([P, TOKENS], F32, name="late_window", tag="x_r1", align_bytes=64)
         windows.append(late_window)
 
         chunks = len(CHUNKS)
@@ -293,12 +303,13 @@ def tile_attend_gheads_sg_pl_kernel(
             for h in range(HEADS):
                 gradient_pass(u, h, h == 0)
         nc.gpsimd.memset(late_window[:], 0.0)
-        split_pairs = keep.tile([P, PACK * (TOKENS - OWN_COLUMNS)], BF16, name="split_pairs", align_bytes=64)
+        pairs = keep.tile([P, 2 * SPAN * 2], BF16, name="pairs", align_bytes=64)
+        shared_first, own_first = 0, TOKENS - OWN_COLUMNS
         for u, (j, lo, hi) in enumerate(units):
             if j == 2:
-                dw = keep.tile([P, hi - lo], F32, name="dw", tag="own_pairs", align_bytes=64)
+                dw = pairs[:].bitcast(F32)[:, TOKENS - HALF:TOKENS + HALF]
             elif j == 3:
-                dw = split_pairs[:, 2 * (TOKENS - OWN_COLUMNS):].bitcast(F32)[:, HALF:HALF + SLOTS]
+                dw = pairs[:].bitcast(F32)[:, 2 * TOKENS - 3 * HALF:2 * TOKENS - HALF]
             else:
                 dw = ring.tile([P, hi - lo], F32, name="dw", tag="stage", bufs=8)
             if j % 2 == 0:
@@ -314,35 +325,37 @@ def tile_attend_gheads_sg_pl_kernel(
             if hi == SLOTS:
                 nc.sync.dma_start(out=out_rows[:, j, :], in_=windows[j][:])
 
-        pairs = (
-            keep.tile([P, 2, OWN_COLUMNS, 2], BF16, name="own_pairs", tag="own_pairs", align_bytes=64),
-            split_pairs[:].rearrange("p (u c e) -> p u c e", u=2, e=2),
-        )
         woven = keep.tile([P, TOKENS, PACK], BF16, name="woven", tag="g_r1", align_bytes=64)
 
         def cast(copy, j, lo, hi):
-            side = int(lo >= OWN_COLUMNS)
-            at = side * OWN_COLUMNS
-            copy(pairs[side][:, j // 2, lo - at:hi - at, j % 2], windows[j][:, lo:hi])
+            if j >= 2:
+                first = TOKENS + lo
+            elif lo < OWN_COLUMNS:
+                first = own_first + lo
+            else:
+                first = shared_first + lo - OWN_COLUMNS
+            copy(pairs[:].rearrange("p (w e) -> p w e", e=2)[:, first:first + hi - lo, j % 2], windows[j][:, lo:hi])
 
         def weave_words(copy, dtype, lo, hi):
-            side = int(lo >= OWN_COLUMNS)
-            at = side * OWN_COLUMNS
-            words = pairs[side][:].rearrange("p u c e -> p (u c e)").bitcast(dtype).rearrange("p (u c) -> p c u", u=2)
+            words = pairs[:].bitcast(dtype)
+            if lo < OWN_COLUMNS:
+                both = words[:, own_first:own_first + 2 * OWN_COLUMNS].rearrange("p (u c) -> p c u", u=2)[:, lo:hi, :]
+            else:
+                both = words.rearrange("p (u c) -> p c u", u=2)[:, lo - OWN_COLUMNS:hi - OWN_COLUMNS, :]
             copy(
                 woven[:].rearrange("p c t -> p (c t)").bitcast(dtype).rearrange("p (c u) -> p c u", u=2)[:, lo:hi, :],
-                words[:, lo - at:hi - at, :],
+                both,
             )
 
         for j in (1, 0):
             cast(nc.gpsimd.tensor_copy, j, OWN_COLUMNS, TOKENS)
         for j in range(PACK):
-            cast(nc.vector.tensor_copy, j, 0, OWN_COLUMNS)
-        weave_words(nc.vector.tensor_copy, I32, 0, starts[1])
-        weave_words(nc.vector.tensor_copy, I32, starts[1], OWN_COLUMNS)
+            cast(nc.vector.tensor_copy, j, 0, OWN_COLUMNS if j < 2 else VECTOR_COLUMNS)
+        for lo, hi in ((0, starts[1]), (starts[1], OWN_COLUMNS), (OWN_COLUMNS, VECTOR_COLUMNS)):
+            weave_words(nc.vector.tensor_copy, I32, lo, hi)
         for j in (3, 2):
-            cast(nc.scalar.copy, j, OWN_COLUMNS, starts[3])
-        weave_words(nc.scalar.copy, U32, OWN_COLUMNS, starts[3])
+            cast(nc.scalar.copy, j, VECTOR_COLUMNS, starts[3])
+        weave_words(nc.scalar.copy, U32, VECTOR_COLUMNS, starts[3])
         for j in (3, 2):
             cast(nc.scalar.copy, j, starts[3], TOKENS)
         for k in range(3, chunks):

@@ -26,9 +26,9 @@ CHUNKS = (512, 512, 512, 256, 128, 128)
 OWN_COLUMNS = 896
 VECTOR_COLUMNS = 1024
 SPAN = TOKENS + OWN_COLUMNS
-VECTOR_SLOTS = 400
+VECTOR_SLOTS = 448
 PIECES = ((0, 128), (128, 256), (256, 512))
-STORE_AFTER = (1, 3, 5)
+STORE_AFTER = (0, 1, 2, 3, 5)
 FLOPS = 4 * 2 * 512 * 512 * 512
 
 
@@ -378,7 +378,7 @@ def tile_attend_gheads_sg_pl_kernel(
                 nc.sync.dma_start(out=out_words[:, cols], in_=out_codes[:, cols].bitcast(I32))
                 stored = starts[k + 1]
         for quad in range(4):
-            (nc.sync, nc.scalar)[quad % 2].dma_start(
+            nc.sync.dma_start(
                 out=scale_rows[4 * quad:4 * quad + 4, :].rearrange("f (a c) -> a f c", a=2),
                 in_=out_scales[32 * quad:32 * quad + 8, :].bitcast(I32),
             )

@@ -27,7 +27,6 @@ OWN_COLUMNS = 896
 VECTOR_COLUMNS = 1024
 SPAN = TOKENS + OWN_COLUMNS
 VECTOR_SLOTS = 448
-PIECES = ((0, 128), (128, 256), (256, 512))
 STORE_AFTER = (0, 1, 2, 3, 5)
 FLOPS = 4 * 2 * 512 * 512 * 512
 
@@ -77,8 +76,13 @@ def tile_attend_gheads_sg_pl_kernel(
         ts_runs = keep.tile([P, TOKENS // P], F32, name="ts_runs")
 
         windows = [keep.tile([P, TOKENS], F32, name="window%d" % j) for j in range(2)]
-        for window in windows:
-            nc.gpsimd.memset(window[:], 0.0)
+        nc.gpsimd.memset(windows[0][:, 0:P], 0.0)
+        nc.gpsimd.memset(windows[0][:, P:], 0.0)
+        nc.gpsimd.memset(windows[1][:], 0.0)
+        third_window = keep.tile([P, TOKENS], F32, name="third_window")
+        for lo, hi in ((0, TOKENS // 2 - 1), (TOKENS // 2 - 1, TOKENS)):
+            nc.vector.memset(third_window[:, lo:hi], 0.0)
+        windows.append(third_window)
 
         x_raw = [keep.tile([P, PACK, R], F32, name="x_raw", tag="x_raw%d" % h, align_bytes=64) for h in range(HEADS)]
         table = [keep.tile([P, TOKENS], F32, name="table", tag="table%d" % j, align_bytes=64) for j in range(PACK)]
@@ -109,6 +113,26 @@ def tile_attend_gheads_sg_pl_kernel(
         x_d = [keep.tile([P, R, PACK], BF16, name="x_d", tag="x_d0", align_bytes=64)]
         nc.vector.tensor_copy(*deal(x_d[0][:], x_raw[0][:]))
 
+        half_r = HEADS * D * PACK // 2
+        shared = keep.tile([P, 2 * half_r], BF16, name="shared", tag="shared", align_bytes=64)
+        x_r = [shared[:, jj * half_r:(jj + 1) * half_r] for jj in range(2)]
+        late_planes = shared[:].rearrange("p (j i) -> p j i", j=2)[:, :, 0:SLOTS]
+
+        def lay_along_r(h):
+            words = x_d[h][:].rearrange("p r j -> p (r j)").bitcast(F32)
+            for jj in range(2):
+                turned = ts_bank() if (h, jj) == (1, 1) else bank()
+                for t in range(PACK):
+                    nc.tensor.transpose(
+                        turned[:, t * P:(t + 1) * P], words[:, 2 * t * P + jj:2 * (t + 1) * P:2], ident[:]
+                    )
+                nc.scalar.copy(
+                    out=x_r[jj].rearrange("s (e h p t) -> s e h p t", e=2, h=HEADS, t=PACK)[:, :, h, :, :],
+                    in_=turned[:].bitcast(BF16).rearrange("s (t p e) -> s e p t", t=PACK, e=2),
+                )
+
+        lay_along_r(0)
+
         ts_listed = keep.tile([P, SLOTS], F32, name="ts_listed")
         nc.vector.tensor_copy(ts_listed[:], ts_pool[:].indirect(offsets[:]))
         ts_turned = bank()
@@ -121,7 +145,8 @@ def tile_attend_gheads_sg_pl_kernel(
 
         x_d.append(keep.tile([P, R, PACK], BF16, name="x_d", tag="x_d1", align_bytes=64))
         nc.vector.tensor_copy(*deal(x_d[1][:], x_raw[1][:]))
-        xd_q = [quantize(x_d[0][:], "xd0", E4M3)]
+        xd_q = [quantize(x_d[h][:], "xd%d" % h, E4M3) for h in range(HEADS)]
+        lay_along_r(1)
 
         y_sb = {}
         y_all = keep.tile([P, HEADS * PACK * SLOTS], F32, name="y_all", tag="x_raw0", align_bytes=64)
@@ -141,58 +166,22 @@ def tile_attend_gheads_sg_pl_kernel(
             c2.append(wu)
             c1.append(wuu)
 
-        half_r = HEADS * D * PACK // 2
-        shared = keep.tile([P, (PACK - 1) * SLOTS + half_r], BF16, name="shared", tag="x_d0", align_bytes=64)
-        w_listed = shared[:, 0:PACK * SLOTS].rearrange("p (j i) -> p j i", j=PACK)
-        x_r = [
-            shared[:, (PACK - 1) * SLOTS:],
-            keep.tile([P, half_r], BF16, name="x_r1", tag="x_r1", align_bytes=64)[:],
-        ]
-        for h, jj in ((0, 1), (0, 0), (1, 0), (1, 1)):
-            words = x_d[h][:].rearrange("p r j -> p (r j)").bitcast(F32)
-            turned = ts_bank() if (h, jj) == (1, 1) else bank()
-            for t in range(PACK):
-                nc.tensor.transpose(
-                    turned[:, t * P:(t + 1) * P], words[:, 2 * t * P + jj:2 * (t + 1) * P:2], ident[:]
-                )
-            nc.scalar.copy(
-                out=x_r[jj].rearrange("s (e h p t) -> s e h p t", e=2, h=HEADS, t=PACK)[:, :, h, :, :],
-                in_=turned[:].bitcast(BF16).rearrange("s (t p e) -> s e p t", t=PACK, e=2),
-            )
         ts_spread = ts_bank()
         for b in range(4):
             nc.tensor.transpose(
                 ts_spread[:, b * P:(b + 1) * P], ts_col[:, b:b + 1].to_broadcast([P, P]), ident[:]
             )
 
-        for j in range(PACK - 1):
-            nc.vector.tensor_copy(w_listed[:, j, :], table[j][:].indirect(offsets[:]))
-            if j == 1:
-                xd_q.append(quantize(x_d[1][:], "xd1", E4M3, place="table1"))
+        early_planes = keep.tile([P, 2, SLOTS], BF16, name="early_planes", tag="x_raw1", align_bytes=64)
+        for j in range(2):
+            nc.vector.tensor_copy(early_planes[:, j, :], table[j][:].indirect(offsets[:]))
         xr_first = quantize(x_r[0].rearrange("p (c t) -> p c t", t=PACK), "xr", E4M3)
-        for lo, hi in PIECES:
-            listed = table[3][:].indirect(offsets[:, lo // 16:hi // 16])
-            if lo < HALF:
-                nc.vector.tensor_copy(w_listed[:, 3, lo:hi], listed)
-            else:
-                nc.scalar.activation(w_listed[:, 3, lo:hi], listed, COPY)
-        w_q = {}
-        w_d = {}
-        for b in range(4):
-            w_d[b] = keep.tile([P, P, PACK], BF16, name="w_d", tag="w_d%d" % (b if b % 2 else 0), align_bytes=64)
-            weave(nc.scalar.copy if b % 2 else nc.vector.tensor_copy, w_d[b][:], w_listed[:, :, b * P:(b + 1) * P])
-            if b == 0:
-                w_q[0] = quantize(w_d[0][:], "w0", E4M3)
-        for b in (1, 2, 3):
-            w_q[b] = quantize(w_d[b][:], "w%d" % b, E4M3)
-
-        third_window = keep.tile([P, TOKENS], F32, name="third_window", tag="x_raw1", align_bytes=64)
-        nc.gpsimd.memset(third_window[:], 0.0)
-        windows.append(third_window)
+        nc.vector.tensor_copy(late_planes[:, 0, :], table[2][:].indirect(offsets[:]))
+        xr_rest = quantize(x_r[1].rearrange("p (c t) -> p c t", t=PACK), "rest", E4M3, place="table2")
 
         shared_out = ((0, 3), (1, 0), (1, 1), (1, 2), (1, 3))
         first_rows = keep.tile([P, 2 * SLOTS], F32, name="first_rows", align_bytes=64)
-        last_rows = keep.tile([P, 3 * SLOTS], F32, name="last_rows", tag="table0", align_bytes=64)
+        last_rows = keep.tile([P, 3 * SLOTS], F32, name="last_rows", tag="x_d0", align_bytes=64)
         factors = []
         for n, (h, t) in enumerate(shared_out):
             if n < 2:
@@ -202,7 +191,26 @@ def tile_attend_gheads_sg_pl_kernel(
                 row = last_rows[:, (n - 2) * SLOTS:(n - 1) * SLOTS]
                 nc.gpsimd.tensor_scalar(row, ts_listed[:], c2[h][:, t:t + 1], 0.0, MULT, ADD)
             factors.append(row)
-        held = keep.tile([P, HEADS * PACK * SLOTS], F32, name="held", tag="w_d3", align_bytes=64)
+
+        w_d = keep.tile([P, SLOTS, PACK], BF16, name="w_d", tag="x_d1", align_bytes=64)
+        weave(nc.scalar.copy, w_d[:, :, 0:2], early_planes[:])
+        for lo in range(0, SLOTS, P):
+            hi = lo + P
+            listed = table[3][:].indirect(offsets[:, lo // 16:hi // 16])
+            if lo == 0:
+                nc.vector.tensor_copy(late_planes[:, 1, lo:hi], listed)
+            else:
+                nc.scalar.activation(late_planes[:, 1, lo:hi], listed, COPY)
+        w_q = {}
+        for step in range(5):
+            if step < 4:
+                cols = slice(step * P, (step + 1) * P)
+                weave(nc.vector.tensor_copy, w_d[:, cols, 2:4], late_planes[:, :, cols])
+            if step > 0:
+                b = step - 1
+                w_q[b] = quantize(w_d[:, b * P:(b + 1) * P, :], "w%d" % b, E4M3)
+
+        held = keep.tile([P, HEADS * PACK * SLOTS], F32, name="held", tag="x_d1", align_bytes=64)
         targets = {
             (h, t): held[:, (h * PACK + t) * SLOTS:(h * PACK + t + 1) * SLOTS] for h in range(HEADS) for t in range(PACK)
         }
@@ -212,12 +220,18 @@ def tile_attend_gheads_sg_pl_kernel(
             )
 
         warm = bank()
-        nc.tensor.transpose(warm[:, 0:P], w_listed[:, 3, 0:2].bitcast(F32).to_broadcast([P, P]), ident[:])
         for width in (SLOTS, HALF):
             nc.tensor.matmul_mx(
-                out=warm[:, 0:width], lhsT=xd_q[0][0][:, 0:P].bitcast(E4M3), lhsT_scale=xd_q[0][1][:, 0:P],
+                out=warm[:, 0:width], lhsT=xr_rest[0][:, 0:P].bitcast(E4M3), lhsT_scale=xr_rest[1][:, 0:P],
                 rhs=xd_q[1][0][:, 0:width].bitcast(E4M3), rhs_scale=xd_q[1][1][:, 0:width], start=True, stop=True,
             )
+
+        def own_target(t):
+            nc.vector.scalar_tensor_tensor(
+                targets[0, t], y_sb[0, t // 2][:, t % 2, :], c2[0][:, t:t + 1], ts_spread[:], MULT, MULT
+            )
+
+        own_target(0)
 
         scaled = {}
         for h, b in ((h, b) for h in range(HEADS) for b in range(4)):
@@ -235,10 +249,8 @@ def tile_attend_gheads_sg_pl_kernel(
                     s[:], a[:].rearrange("i (t m) -> i t m", t=PACK), COPY, scale=ts2_col[:, b:b + 1]
                 )
             scaled[4 * h + b] = s
-        for t in range(PACK - 1):
-            nc.vector.scalar_tensor_tensor(
-                targets[0, t], y_sb[0, t // 2][:, t % 2, :], c2[0][:, t:t + 1], ts_spread[:], MULT, MULT
-            )
+        for t in range(1, PACK - 1):
+            own_target(t)
         g_r = [keep.tile([P, SLOTS, PACK], BF16, name="g_r", tag="g_r%d" % h, align_bytes=64) for h in range(HEADS)]
         g_q = []
         for h in range(HEADS):
@@ -271,13 +283,7 @@ def tile_attend_gheads_sg_pl_kernel(
                     in_=g_r[h][:, lo:lo + HALF, :].rearrange("p c t -> p (c t)"),
                 )
             g_q.append((codes, scales))
-        rest_codes = keep.tile([P, D], U32, name="rest_codes", tag="g_r1", align_bytes=64)
-        rest_scales = keep.tile([P, D], U8, name="rest_scales", align_bytes=64)
-        nc.vector.quantize_mx(
-            out=rest_codes[:].bitcast(E4M3), scales=rest_scales[:],
-            in_=x_r[1],
-        )
-        late_window = keep.tile([P, TOKENS], F32, name="late_window", tag="x_r1", align_bytes=64)
+        late_window = keep.tile([P, TOKENS], F32, name="late_window", tag="g_r1", align_bytes=64)
         windows.append(late_window)
 
         chunks = len(CHUNKS)
@@ -289,7 +295,7 @@ def tile_attend_gheads_sg_pl_kernel(
         def gradient_pass(u, h, start):
             j, lo, hi = units[u]
             first = (j % 2 * HEADS + h) * P
-            codes, scales = (t[:, first:first + P] for t in (xr_first if j < 2 else (rest_codes, rest_scales)))
+            codes, scales = (t[:, first:first + P] for t in (xr_first if j < 2 else xr_rest))
             nc.tensor.matmul_mx(
                 out=accs[u][:, 0:hi - lo], lhsT=codes.bitcast(E4M3), lhsT_scale=scales,
                 rhs=g_q[h][0][:, lo:hi].bitcast(E5M2), rhs_scale=g_q[h][1][:, lo:hi],
@@ -325,7 +331,7 @@ def tile_attend_gheads_sg_pl_kernel(
             if hi == SLOTS:
                 nc.sync.dma_start(out=out_rows[:, j, :], in_=windows[j][:])
 
-        woven = keep.tile([P, TOKENS, PACK], BF16, name="woven", tag="g_r1", align_bytes=64)
+        woven = keep.tile([P, TOKENS, PACK], BF16, name="woven", tag="table2", align_bytes=64)
 
         def cast(copy, j, lo, hi):
             if j >= 2:

@@ -50,6 +50,7 @@ def tile_attend_gheads_sg_pl_kernel(
 
     with ExitStack() as ctx:
         keep = ctx.enter_context(tc.tile_pool(name="keep", bufs=1))
+        placed = ctx.enter_context(tc.tile_pool(name="placed", bufs=1))
         ring = ctx.enter_context(tc.tile_pool(name="ring", bufs=2))
         psum = ctx.enter_context(tc.psum_pool(name="psum", bufs=1))
 
@@ -75,14 +76,9 @@ def tile_attend_gheads_sg_pl_kernel(
         ts_pool = keep.tile([P, TOKENS], F32, name="ts_pool", tag="x_d1", align_bytes=64)
         ts_runs = keep.tile([P, TOKENS // P], F32, name="ts_runs")
 
-        windows = [keep.tile([P, TOKENS], F32, name="window%d" % j) for j in range(2)]
-        nc.gpsimd.memset(windows[0][:, 0:P], 0.0)
-        nc.gpsimd.memset(windows[0][:, P:], 0.0)
-        nc.gpsimd.memset(windows[1][:], 0.0)
-        third_window = keep.tile([P, TOKENS], F32, name="third_window")
-        for lo, hi in ((0, TOKENS // 2 - 1), (TOKENS // 2 - 1, TOKENS)):
-            nc.vector.memset(third_window[:, lo:hi], 0.0)
-        windows.append(third_window)
+        windows = [placed.tile([P, TOKENS], F32, name="window%d" % j, offset=4 * TOKENS * j) for j in range(2)]
+        for j in (1, 0):
+            nc.vector.memset(windows[j][:], 0.0)
 
         x_raw = [keep.tile([P, PACK, R], F32, name="x_raw", tag="x_raw%d" % h, align_bytes=64) for h in range(HEADS)]
         table = [keep.tile([P, TOKENS], F32, name="table", tag="table%d" % j, align_bytes=64) for j in range(PACK)]
@@ -180,15 +176,15 @@ def tile_attend_gheads_sg_pl_kernel(
         xr_rest = quantize(x_r[1].rearrange("p (c t) -> p c t", t=PACK), "rest", E4M3, place="table2")
 
         shared_out = ((0, 3), (1, 0), (1, 1), (1, 2), (1, 3))
-        first_rows = keep.tile([P, 2 * SLOTS], F32, name="first_rows", align_bytes=64)
-        last_rows = keep.tile([P, 3 * SLOTS], F32, name="last_rows", tag="x_d0", align_bytes=64)
+        first_row = keep.tile([P, SLOTS], F32, name="first_row", align_bytes=64)
+        last_rows = keep.tile([P, 4 * SLOTS], F32, name="last_rows", tag="x_d0", align_bytes=64)
         factors = []
         for n, (h, t) in enumerate(shared_out):
-            if n < 2:
-                row = first_rows[:, n * SLOTS:(n + 1) * SLOTS]
+            if n == 0:
+                row = first_row[:]
                 nc.scalar.activation(row, ts_listed[:], COPY, scale=c2[h][:, t:t + 1])
             else:
-                row = last_rows[:, (n - 2) * SLOTS:(n - 1) * SLOTS]
+                row = last_rows[:, (n - 1) * SLOTS:n * SLOTS]
                 nc.gpsimd.tensor_scalar(row, ts_listed[:], c2[h][:, t:t + 1], 0.0, MULT, ADD)
             factors.append(row)
 
@@ -251,7 +247,10 @@ def tile_attend_gheads_sg_pl_kernel(
             scaled[4 * h + b] = s
         for t in range(1, PACK - 1):
             own_target(t)
-        g_r = [keep.tile([P, SLOTS, PACK], BF16, name="g_r", tag="g_r%d" % h, align_bytes=64) for h in range(HEADS)]
+        g_r = [
+            keep.tile([P, SLOTS, PACK], BF16, name="g_first", align_bytes=64),
+            placed.tile([P, SLOTS, PACK], BF16, name="g_second", offset=12 * TOKENS - 4 * SLOTS, align_bytes=64),
+        ]
         g_q = []
         for h in range(HEADS):
             banks = [ts_bank() if (h, t) == (1, 0) else bank() for t in range(PACK)]
@@ -283,8 +282,7 @@ def tile_attend_gheads_sg_pl_kernel(
                     in_=g_r[h][:, lo:lo + HALF, :].rearrange("p c t -> p (c t)"),
                 )
             g_q.append((codes, scales))
-        late_window = keep.tile([P, TOKENS], F32, name="late_window", tag="g_r1", align_bytes=64)
-        windows.append(late_window)
+        windows += [placed.tile([P, TOKENS], F32, name="window%d" % j, offset=4 * TOKENS * j) for j in (2, 3)]
 
         chunks = len(CHUNKS)
         starts = [sum(CHUNKS[:k]) for k in range(chunks + 1)]
@@ -308,7 +306,8 @@ def tile_attend_gheads_sg_pl_kernel(
         for u in (4, 5):
             for h in range(HEADS):
                 gradient_pass(u, h, h == 0)
-        nc.gpsimd.memset(late_window[:], 0.0)
+        for j in (2, 3):
+            nc.gpsimd.memset(windows[j][:], 0.0)
         pairs = keep.tile([P, 2 * SPAN * 2], BF16, name="pairs", align_bytes=64)
         shared_first, own_first = 0, TOKENS - OWN_COLUMNS
         for u, (j, lo, hi) in enumerate(units):

@@ -216,6 +216,7 @@ def tile_attend_gheads_sg_pl_kernel(
             )
 
         warm = bank()
+        nc.tensor.transpose(warm[:, 0:P], late_planes[:, 1, 0:2].bitcast(F32).to_broadcast([P, P]), ident[:])
         for width in (SLOTS, HALF):
             nc.tensor.matmul_mx(
                 out=warm[:, 0:width], lhsT=xr_rest[0][:, 0:P].bitcast(E4M3), lhsT_scale=xr_rest[1][:, 0:P],
@@ -304,8 +305,8 @@ def tile_attend_gheads_sg_pl_kernel(
             for u in range(4):
                 gradient_pass(u, h, h == 0)
         for u in (4, 5):
-            for h in range(HEADS):
-                gradient_pass(u, h, h == 0)
+            for h in (1, 0):
+                gradient_pass(u, h, h == 1)
         for j in (2, 3):
             nc.gpsimd.memset(windows[j][:], 0.0)
         pairs = keep.tile([P, 2 * SPAN * 2], BF16, name="pairs", align_bytes=64)

@@ -27,6 +27,7 @@ OWN_COLUMNS = 896
 VECTOR_COLUMNS = 1024
 SPAN = TOKENS + OWN_COLUMNS
 VECTOR_SLOTS = 448
+PIECES = ((0, 128), (128, 256), (256, 512))
 STORE_AFTER = (0, 1, 2, 3, 5)
 FLOPS = 4 * 2 * 512 * 512 * 512
 
@@ -76,9 +77,11 @@ def tile_attend_gheads_sg_pl_kernel(
         ts_pool = keep.tile([P, TOKENS], F32, name="ts_pool", tag="x_d1", align_bytes=64)
         ts_runs = keep.tile([P, TOKENS // P], F32, name="ts_runs")
 
-        windows = [placed.tile([P, TOKENS], F32, name="window%d" % j, offset=4 * TOKENS * j) for j in range(2)]
+        windows = [placed.tile([P, TOKENS], F32, name="window%d" % j, offset=4 * TOKENS * j) for j in range(3)]
         for j in (1, 0):
             nc.vector.memset(windows[j][:], 0.0)
+        nc.gpsimd.memset(windows[2][:, 0:P], 0.0)
+        nc.gpsimd.memset(windows[2][:, P:], 0.0)
 
         x_raw = [keep.tile([P, PACK, R], F32, name="x_raw", tag="x_raw%d" % h, align_bytes=64) for h in range(HEADS)]
         table = [keep.tile([P, TOKENS], F32, name="table", tag="table%d" % j, align_bytes=64) for j in range(PACK)]
@@ -110,21 +113,24 @@ def tile_attend_gheads_sg_pl_kernel(
         nc.vector.tensor_copy(*deal(x_d[0][:], x_raw[0][:]))
 
         half_r = HEADS * D * PACK // 2
-        shared = keep.tile([P, 2 * half_r], BF16, name="shared", tag="shared", align_bytes=64)
-        x_r = [shared[:, jj * half_r:(jj + 1) * half_r] for jj in range(2)]
-        late_planes = shared[:].rearrange("p (j i) -> p j i", j=2)[:, :, 0:SLOTS]
+        shared = keep.tile([P, (PACK - 1) * SLOTS + half_r], BF16, name="shared", tag="x_raw1", align_bytes=64)
+        w_listed = shared[:, 0:PACK * SLOTS].rearrange("p (j i) -> p j i", j=PACK)
+        x_r = [
+            shared[:, (PACK - 1) * SLOTS:],
+            placed.tile([P, half_r], BF16, name="x_r1", offset=12 * TOKENS, align_bytes=64)[:],
+        ]
 
         def lay_along_r(h):
             words = x_d[h][:].rearrange("p r j -> p (r j)").bitcast(F32)
-            for jj in range(2):
+            for jj in (1 - h, h):
                 turned = ts_bank() if (h, jj) == (1, 1) else bank()
                 for t in range(PACK):
                     nc.tensor.transpose(
                         turned[:, t * P:(t + 1) * P], words[:, 2 * t * P + jj:2 * (t + 1) * P:2], ident[:]
                     )
                 nc.scalar.copy(
-                    out=x_r[jj].rearrange("s (e h p t) -> s e h p t", e=2, h=HEADS, t=PACK)[:, :, h, :, :],
-                    in_=turned[:].bitcast(BF16).rearrange("s (t p e) -> s e p t", t=PACK, e=2),
+                    out=x_r[jj].rearrange("s (e h c i t) -> s h c t i e", e=2, h=HEADS, i=4, t=PACK)[:, h],
+                    in_=turned[:].bitcast(BF16).rearrange("s (t c i e) -> s c t i e", t=PACK, i=4, e=2),
                 )
 
         lay_along_r(0)
@@ -168,12 +174,9 @@ def tile_attend_gheads_sg_pl_kernel(
                 ts_spread[:, b * P:(b + 1) * P], ts_col[:, b:b + 1].to_broadcast([P, P]), ident[:]
             )
 
-        early_planes = keep.tile([P, 2, SLOTS], BF16, name="early_planes", tag="x_raw1", align_bytes=64)
-        for j in range(2):
-            nc.vector.tensor_copy(early_planes[:, j, :], table[j][:].indirect(offsets[:]))
+        for j in range(PACK - 1):
+            nc.vector.tensor_copy(w_listed[:, j, :], table[j][:].indirect(offsets[:]))
         xr_first = quantize(x_r[0].rearrange("p (c t) -> p c t", t=PACK), "xr", E4M3)
-        nc.vector.tensor_copy(late_planes[:, 0, :], table[2][:].indirect(offsets[:]))
-        xr_rest = quantize(x_r[1].rearrange("p (c t) -> p c t", t=PACK), "rest", E4M3, place="table2")
 
         shared_out = ((0, 3), (1, 0), (1, 1), (1, 2), (1, 3))
         first_row = keep.tile([P, SLOTS], F32, name="first_row", align_bytes=64)
@@ -188,25 +191,23 @@ def tile_attend_gheads_sg_pl_kernel(
                 nc.gpsimd.tensor_scalar(row, ts_listed[:], c2[h][:, t:t + 1], 0.0, MULT, ADD)
             factors.append(row)
 
-        w_d = keep.tile([P, SLOTS, PACK], BF16, name="w_d", tag="x_d1", align_bytes=64)
-        weave(nc.scalar.copy, w_d[:, :, 0:2], early_planes[:])
-        for lo in range(0, SLOTS, P):
-            hi = lo + P
+        for lo, hi in PIECES:
             listed = table[3][:].indirect(offsets[:, lo // 16:hi // 16])
-            if lo == 0:
-                nc.vector.tensor_copy(late_planes[:, 1, lo:hi], listed)
+            if lo < HALF:
+                nc.vector.tensor_copy(w_listed[:, 3, lo:hi], listed)
             else:
-                nc.scalar.activation(late_planes[:, 1, lo:hi], listed, COPY)
+                nc.scalar.activation(w_listed[:, 3, lo:hi], listed, COPY)
         w_q = {}
-        for step in range(5):
-            if step < 4:
-                cols = slice(step * P, (step + 1) * P)
-                weave(nc.vector.tensor_copy, w_d[:, cols, 2:4], late_planes[:, :, cols])
-            if step > 0:
-                b = step - 1
-                w_q[b] = quantize(w_d[:, b * P:(b + 1) * P, :], "w%d" % b, E4M3)
+        w_d = {}
+        for b in range(4):
+            w_d[b] = keep.tile([P, P, PACK], BF16, name="w_d", tag="w_d%d" % (b if b % 2 else 0), align_bytes=64)
+            weave(nc.scalar.copy if b % 2 else nc.vector.tensor_copy, w_d[b][:], w_listed[:, :, b * P:(b + 1) * P])
+            if b == 0:
+                w_q[0] = quantize(w_d[0][:], "w0", E4M3)
+        for b in (1, 2, 3):
+            w_q[b] = quantize(w_d[b][:], "w%d" % b, E4M3)
 
-        held = keep.tile([P, HEADS * PACK * SLOTS], F32, name="held", tag="x_d1", align_bytes=64)
+        held = keep.tile([P, HEADS * PACK * SLOTS], F32, name="held", tag="w_d3", align_bytes=64)
         targets = {
             (h, t): held[:, (h * PACK + t) * SLOTS:(h * PACK + t + 1) * SLOTS] for h in range(HEADS) for t in range(PACK)
         }
@@ -216,10 +217,10 @@ def tile_attend_gheads_sg_pl_kernel(
             )
 
         warm = bank()
-        nc.tensor.transpose(warm[:, 0:P], late_planes[:, 1, 0:2].bitcast(F32).to_broadcast([P, P]), ident[:])
+        nc.tensor.transpose(warm[:, 0:P], w_listed[:, 3, 0:2].bitcast(F32).to_broadcast([P, P]), ident[:])
         for width in (SLOTS, HALF):
             nc.tensor.matmul_mx(
-                out=warm[:, 0:width], lhsT=xr_rest[0][:, 0:P].bitcast(E4M3), lhsT_scale=xr_rest[1][:, 0:P],
+                out=warm[:, 0:width], lhsT=xd_q[0][0][:, 0:P].bitcast(E4M3), lhsT_scale=xd_q[0][1][:, 0:P],
                 rhs=xd_q[1][0][:, 0:width].bitcast(E4M3), rhs_scale=xd_q[1][1][:, 0:width], start=True, stop=True,
             )
 
@@ -227,8 +228,6 @@ def tile_attend_gheads_sg_pl_kernel(
             nc.vector.scalar_tensor_tensor(
                 targets[0, t], y_sb[0, t // 2][:, t % 2, :], c2[0][:, t:t + 1], ts_spread[:], MULT, MULT
             )
-
-        own_target(0)
 
         scaled = {}
         for h, b in ((h, b) for h in range(HEADS) for b in range(4)):
@@ -246,11 +245,10 @@ def tile_attend_gheads_sg_pl_kernel(
                     s[:], a[:].rearrange("i (t m) -> i t m", t=PACK), COPY, scale=ts2_col[:, b:b + 1]
                 )
             scaled[4 * h + b] = s
-        for t in range(1, PACK - 1):
+        for t in range(PACK - 1):
             own_target(t)
         g_r = [
-            keep.tile([P, SLOTS, PACK], BF16, name="g_first", align_bytes=64),
-            placed.tile([P, SLOTS, PACK], BF16, name="g_second", offset=12 * TOKENS - 4 * SLOTS, align_bytes=64),
+            keep.tile([P, SLOTS, PACK], BF16, name="g_r", tag="g_r%d" % h, align_bytes=64) for h in range(HEADS)
         ]
         g_q = []
         for h in range(HEADS):
@@ -283,7 +281,11 @@ def tile_attend_gheads_sg_pl_kernel(
                     in_=g_r[h][:, lo:lo + HALF, :].rearrange("p c t -> p (c t)"),
                 )
             g_q.append((codes, scales))
-        windows += [placed.tile([P, TOKENS], F32, name="window%d" % j, offset=4 * TOKENS * j) for j in (2, 3)]
+        rest_codes = keep.tile([P, D], U32, name="rest_codes", tag="g_r1", align_bytes=64)
+        rest_scales = keep.tile([P, D], U8, name="rest_scales", align_bytes=64)
+        nc.vector.quantize_mx(out=rest_codes[:].bitcast(E4M3), scales=rest_scales[:], in_=x_r[1])
+        xr_rest = (rest_codes, rest_scales)
+        windows += [placed.tile([P, TOKENS], F32, name="window%d" % j, offset=4 * TOKENS * j) for j in (3,)]
 
         chunks = len(CHUNKS)
         starts = [sum(CHUNKS[:k]) for k in range(chunks + 1)]
@@ -305,10 +307,9 @@ def tile_attend_gheads_sg_pl_kernel(
             for u in range(4):
                 gradient_pass(u, h, h == 0)
         for u in (4, 5):
-            for h in (1, 0):
-                gradient_pass(u, h, h == 1)
-        for j in (2, 3):
-            nc.gpsimd.memset(windows[j][:], 0.0)
+            for h in range(HEADS):
+                gradient_pass(u, h, h == 0)
+        nc.gpsimd.memset(windows[3][:], 0.0)
         pairs = keep.tile([P, 2 * SPAN * 2], BF16, name="pairs", align_bytes=64)
         shared_first, own_first = 0, TOKENS - OWN_COLUMNS
         for u, (j, lo, hi) in enumerate(units):
@@ -331,7 +332,7 @@ def tile_attend_gheads_sg_pl_kernel(
             if hi == SLOTS:
                 nc.sync.dma_start(out=out_rows[:, j, :], in_=windows[j][:])
 
-        woven = keep.tile([P, TOKENS, PACK], BF16, name="woven", tag="table2", align_bytes=64)
+        woven = keep.tile([P, TOKENS, PACK], BF16, name="woven", tag="g_r1", align_bytes=64)
 
         def cast(copy, j, lo, hi):
             if j >= 2:

@@ -24,7 +24,7 @@ HEADS = 2
 HALF = SLOTS // 2
 CHUNKS = (512, 512, 512, 256, 128, 128)
 OWN_COLUMNS = 896
-VECTOR_COLUMNS = 1024
+VECTOR_COLUMNS = 992
 SPAN = TOKENS + OWN_COLUMNS
 VECTOR_SLOTS = 448
 PIECES = ((0, 128), (128, 256), (256, 512))
@@ -93,8 +93,8 @@ def tile_attend_gheads_sg_pl_kernel(
         nc.sync.dma_start(out=x_raw[0][:], in_=xs[0].rearrange("(p j) r -> p j r", j=PACK))
         nc.sync.dma_start(out=x_raw[1][:], in_=xs[1].rearrange("(p j) r -> p j r", j=PACK))
         for h in range(HEADS):
-            nc.sync.dma_start(out=u_col[h][:], in_=us[h].rearrange("(m t) o -> m (t o)", t=PACK))
-            nc.sync.dma_start(out=w_col[h][:], in_=ws[h].rearrange("(m t) o -> m (t o)", t=PACK))
+            nc.scalar.dma_start(out=u_col[h][:], in_=us[h].rearrange("(m t) o -> m (t o)", t=PACK))
+            nc.scalar.dma_start(out=w_col[h][:], in_=ws[h].rearrange("(m t) o -> m (t o)", t=PACK))
         for j in range(PACK):
             nc.sync.dma_start(out=table[j][:], in_=w_planes[:, j, :])
 

@@ -28,6 +28,7 @@ VECTOR_COLUMNS = 992
 SPAN = TOKENS + OWN_COLUMNS
 VECTOR_SLOTS = 448
 PIECES = ((0, 128), (128, 256), (256, 512))
+PITCH = 768
 STORE_AFTER = (0, 1, 2, 3, 5)
 FLOPS = 4 * 2 * 512 * 512 * 512
 
@@ -113,10 +114,10 @@ def tile_attend_gheads_sg_pl_kernel(
         nc.vector.tensor_copy(*deal(x_d[0][:], x_raw[0][:]))
 
         half_r = HEADS * D * PACK // 2
-        shared = keep.tile([P, (PACK - 1) * SLOTS + half_r], BF16, name="shared", tag="x_raw1", align_bytes=64)
-        w_listed = shared[:, 0:PACK * SLOTS].rearrange("p (j i) -> p j i", j=PACK)
+        shared = keep.tile([P, (PACK - 1) * PITCH + half_r], BF16, name="shared", tag="x_d1", align_bytes=64)
+        w_listed = shared[:, 0:PACK * PITCH].rearrange("p (j i) -> p j i", j=PACK)[:, :, 0:SLOTS]
         x_r = [
-            shared[:, (PACK - 1) * SLOTS:],
+            shared[:, (PACK - 1) * PITCH:],
             placed.tile([P, half_r], BF16, name="x_r1", offset=12 * TOKENS, align_bytes=64)[:],
         ]
 
@@ -145,7 +146,7 @@ def tile_attend_gheads_sg_pl_kernel(
         nc.scalar.copy(ts_col[:], ts_turned[:, 0:512:P])
         nc.scalar.activation(ts2_col[:], ts_turned[:, 0:512:P], SQUARE)
 
-        x_d.append(keep.tile([P, R, PACK], BF16, name="x_d", tag="x_d1", align_bytes=64))
+        x_d.append(shared[:, 0:R * PACK].rearrange("p (r j) -> p r j", j=PACK))
         nc.vector.tensor_copy(*deal(x_d[1][:], x_raw[1][:]))
         xd_q = [quantize(x_d[h][:], "xd%d" % h, E4M3) for h in range(HEADS)]
         lay_along_r(1)
@@ -174,18 +175,19 @@ def tile_attend_gheads_sg_pl_kernel(
                 ts_spread[:, b * P:(b + 1) * P], ts_col[:, b:b + 1].to_broadcast([P, P]), ident[:]
             )
 
-        for j in range(PACK - 1):
+        for j in range(2):
             nc.vector.tensor_copy(w_listed[:, j, :], table[j][:].indirect(offsets[:]))
+        nc.scalar.activation(w_listed[:, 2, :], table[2][:].indirect(offsets[:]), COPY)
         xr_first = quantize(x_r[0].rearrange("p (c t) -> p c t", t=PACK), "xr", E4M3)
 
         shared_out = ((0, 3), (1, 0), (1, 1), (1, 2), (1, 3))
-        first_row = keep.tile([P, SLOTS], F32, name="first_row", align_bytes=64)
+        first_row = shared[:, PACK * PITCH:PACK * PITCH + 2 * SLOTS].bitcast(F32)
         last_rows = keep.tile([P, 4 * SLOTS], F32, name="last_rows", tag="x_d0", align_bytes=64)
         factors = []
         for n, (h, t) in enumerate(shared_out):
             if n == 0:
-                row = first_row[:]
-                nc.scalar.activation(row, ts_listed[:], COPY, scale=c2[h][:, t:t + 1])
+                row = first_row
+                nc.vector.tensor_scalar_mul(row, ts_listed[:], c2[h][:, t:t + 1])
             else:
                 row = last_rows[:, (n - 1) * SLOTS:n * SLOTS]
                 nc.gpsimd.tensor_scalar(row, ts_listed[:], c2[h][:, t:t + 1], 0.0, MULT, ADD)

from contextlib import ExitStack

import concourse.mybir as mybir
from concourse.masks import make_identity

F32 = mybir.dt.float32
BF16 = mybir.dt.bfloat16
I32 = mybir.dt.int32
U32 = mybir.dt.uint32
U16 = mybir.dt.uint16
U8 = mybir.dt.uint8
E4M3 = mybir.dt.float8_e4m3fn_x4
E5M2 = mybir.dt.float8_e5m2_x4
MULT = mybir.AluOpType.mult
ADD = mybir.AluOpType.add
SUB = mybir.AluOpType.subtract
COPY = mybir.ActivationFunctionType.Copy
SQUARE = mybir.ActivationFunctionType.Square

P = 128
PACK = 4
D, R, SLOTS, TOKENS = 512, 512, 512, 2048
HEADS = 2
HALF = SLOTS // 2
CHUNKS = (512, 512, 512, 256, 128, 128)
OWN_COLUMNS = 896
VECTOR_COLUMNS = 992
SPAN = TOKENS + OWN_COLUMNS
VECTOR_SLOTS = 448
PIECES = ((0, 128), (128, 256), (256, 512))
PITCH = 768
STORE_AFTER = (0, 1, 2, 3, 5)
FLOPS = 4 * 2 * 512 * 512 * 512


def weave(engine_copy, out, in_):
    engine_copy(
        out=out.rearrange("p (c i) t -> p c t i", i=4),
        in_=in_.rearrange("p t (c i) -> p c t i", i=4),
    )


def deal(out, in_):
    return out.rearrange("p (t s) j -> p s j t", t=4), in_.rearrange("p j (s t) -> p s j t", t=4)


def tile_attend_gheads_sg_pl_kernel(
    tc, x1, x2, wT, y1, u1, w1, y2, u2, w2, ts, offs, out_0, out_1, out_2
):
    nc = tc.nc
    xs, ys, us, ws = (x1, x2), (y1, y2), (u1, u2), (w1, w2)

    with ExitStack() as ctx:
        keep = ctx.enter_context(tc.tile_pool(name="keep", bufs=1))
        placed = ctx.enter_context(tc.tile_pool(name="placed", bufs=1))
        ring = ctx.enter_context(tc.tile_pool(name="ring", bufs=2))
        psum = ctx.enter_context(tc.psum_pool(name="psum", bufs=1))

        def quantize(src, name, fmt, place=None):
            width = src.shape[1]
            codes = keep.tile([P, width], U32, name=name + "_codes", tag=place or name + "_codes", align_bytes=64)
            scales = keep.tile([P, width], U8, name=name + "_scales", tag=name + "_scales", align_bytes=64)
            nc.vector.quantize_mx(
                out=codes[:].bitcast(fmt), scales=scales[:], in_=src.rearrange("p c t -> p (c t)")
            )
            return codes, scales

        def bank():
            return psum.tile([P, 512], F32, name="bank", tag="bank", bufs=7)

        def ts_bank():
            return psum.tile([P, 512], F32, name="ts_bank", tag="ts_bank", bufs=1)

        offsets = keep.tile([P, SLOTS // 16], U16, name="offsets")
        ident = keep.tile([P, P], F32, name="ident")
        make_identity(nc, ident[:])

        ts_pool = keep.tile([P, TOKENS], F32, name="ts_pool", tag="x_d1", align_bytes=64)
        ts_runs = keep.tile([P, TOKENS // P], F32, name="ts_runs")

        windows = [placed.tile([P, TOKENS], F32, name="window%d" % j, offset=4 * TOKENS * j) for j in range(3)]
        for j in (1, 0):
            nc.vector.memset(windows[j][:], 0.0)
        nc.gpsimd.memset(windows[2][:, 0:P], 0.0)
        nc.gpsimd.memset(windows[2][:, P:], 0.0)

        x_raw = [keep.tile([P, PACK, R], F32, name="x_raw", tag="x_raw%d" % h, align_bytes=64) for h in range(HEADS)]
        table = [keep.tile([P, TOKENS], F32, name="table", tag="table%d" % j, align_bytes=64) for j in range(PACK)]
        w_planes = wT.rearrange("(p j) c -> p j c", j=PACK)
        u_col = [keep.tile([P, PACK], F32, name="u_col%d" % h) for h in range(HEADS)]
        w_col = [keep.tile([P, PACK], F32, name="w_col%d" % h) for h in range(HEADS)]
        nc.sync.dma_start(out=ts_runs[:], in_=ts[0:1, :].rearrange("o (p k) -> (o p) k", p=P))
        nc.sync.dma_start(offsets[:], offs)
        nc.sync.dma_start(out=x_raw[0][:], in_=xs[0].rearrange("(p j) r -> p j r", j=PACK))
        nc.sync.dma_start(out=x_raw[1][:], in_=xs[1].rearrange("(p j) r -> p j r", j=PACK))
        for h in range(HEADS):
            nc.scalar.dma_start(out=u_col[h][:], in_=us[h].rearrange("(m t) o -> m (t o)", t=PACK))
            nc.scalar.dma_start(out=w_col[h][:], in_=ws[h].rearrange("(m t) o -> m (t o)", t=PACK))
        for j in range(PACK):
            nc.sync.dma_start(out=table[j][:], in_=w_planes[:, j, :])

        for b in range(4):
            spread = bank()
            for k in range(4):
                nc.tensor.transpose(
                    spread[:, k * P:(k + 1) * P], ts_runs[:, 4 * b + k:4 * b + k + 1].to_broadcast([P, P]), ident[:]
                )
            nc.scalar.copy(
                out=ts_pool[:].rearrange("q (p b k) -> q p b k", b=4, k=4)[:, :, b, :],
                in_=spread[:].rearrange("q (k p) -> q p k", k=4),
            )

        x_d = [keep.tile([P, R, PACK], BF16, name="x_d", tag="x_d0", align_bytes=64)]
        nc.vector.tensor_copy(*deal(x_d[0][:], x_raw[0][:]))

        half_r = HEADS * D * PACK // 2
        shared = keep.tile([P, (PACK - 1) * PITCH + half_r], BF16, name="shared", tag="x_d1", align_bytes=64)
        w_listed = shared[:, 0:PACK * PITCH].rearrange("p (j i) -> p j i", j=PACK)[:, :, 0:SLOTS]
        x_r = [
            shared[:, (PACK - 1) * PITCH:],
            placed.tile([P, half_r], BF16, name="x_r1", offset=12 * TOKENS, align_bytes=64)[:],
        ]

        def lay_along_r(h):
            words = x_d[h][:].rearrange("p r j -> p (r j)").bitcast(F32)
            for jj in (1 - h, h):
                turned = ts_bank() if (h, jj) == (1, 1) else bank()
                for t in range(PACK):
                    nc.tensor.transpose(
                        turned[:, t * P:(t + 1) * P], words[:, 2 * t * P + jj:2 * (t + 1) * P:2], ident[:]
                    )
                nc.scalar.copy(
                    out=x_r[jj].rearrange("s (e h c i t) -> s h c t i e", e=2, h=HEADS, i=4, t=PACK)[:, h],
                    in_=turned[:].bitcast(BF16).rearrange("s (t c i e) -> s c t i e", t=PACK, i=4, e=2),
                )

        lay_along_r(0)

        ts_listed = keep.tile([P, SLOTS], F32, name="ts_listed")
        nc.vector.tensor_copy(ts_listed[:], ts_pool[:].indirect(offsets[:]))
        ts_turned = bank()
        for b in range(4):
            nc.tensor.transpose(ts_turned[:, b * P:(b + 1) * P], ts_listed[:, b * P:(b + 1) * P], ident[:])
        ts_col = keep.tile([P, 4], F32, name="ts_col")
        ts2_col = keep.tile([P, 4], F32, name="ts2_col")
        nc.scalar.copy(ts_col[:], ts_turned[:, 0:512:P])
        nc.scalar.activation(ts2_col[:], ts_turned[:, 0:512:P], SQUARE)

        x_d.append(shared[:, 0:R * PACK].rearrange("p (r j) -> p r j", j=PACK))
        nc.vector.tensor_copy(*deal(x_d[1][:], x_raw[1][:]))
        xd_q = [quantize(x_d[h][:], "xd%d" % h, E4M3) for h in range(HEADS)]
        lay_along_r(1)

        y_sb = {}
        y_all = keep.tile([P, HEADS * PACK * SLOTS], F32, name="y_all", tag="x_raw0", align_bytes=64)
        for h in range(HEADS):
            y_rows = ys[h].rearrange("(m t) i -> m t i", t=PACK)
            for tp in range(2):
                first = (h * PACK + 2 * tp) * SLOTS
                y_sb[h, tp] = y_all[:, first:first + 2 * SLOTS].rearrange("p (t i) -> p t i", t=2)
                nc.sync.dma_start(out=y_sb[h, tp], in_=y_rows[:, 2 * tp:2 * tp + 2, :])

        c1, c2 = [], []
        for h in range(HEADS):
            wu = keep.tile([P, PACK], F32, name="wu%d" % h)
            wuu = keep.tile([P, PACK], F32, name="wuu%d" % h)
            nc.gpsimd.tensor_tensor(wu[:], w_col[h][:], u_col[h][:], MULT)
            nc.gpsimd.tensor_tensor(wuu[:], wu[:], u_col[h][:], MULT)
            c2.append(wu)
            c1.append(wuu)

        ts_spread = ts_bank()
        for b in range(4):
            nc.tensor.transpose(
                ts_spread[:, b * P:(b + 1) * P], ts_col[:, b:b + 1].to_broadcast([P, P]), ident[:]
            )

        for j in range(2):
            nc.vector.tensor_copy(w_listed[:, j, :], table[j][:].indirect(offsets[:]))
        nc.scalar.activation(w_listed[:, 2, :], table[2][:].indirect(offsets[:]), COPY)
        xr_first = quantize(x_r[0].rearrange("p (c t) -> p c t", t=PACK), "xr", E4M3)

        shared_out = ((0, 3), (1, 0), (1, 1), (1, 2), (1, 3))
        first_row = shared[:, PACK * PITCH:PACK * PITCH + 2 * SLOTS].bitcast(F32)
        last_rows = keep.tile([P, 4 * SLOTS], F32, name="last_rows", tag="x_d0", align_bytes=64)
        factors = []
        for n, (h, t) in enumerate(shared_out):
            if n == 0:
                row = first_row
                nc.vector.tensor_scalar_mul(row, ts_listed[:], c2[h][:, t:t + 1])
            else:
                row = last_rows[:, (n - 1) * SLOTS:n * SLOTS]
                nc.gpsimd.tensor_scalar(row, ts_listed[:], c2[h][:, t:t + 1], 0.0, MULT, ADD)
            factors.append(row)

        for lo, hi in PIECES:
            listed = table[3][:].indirect(offsets[:, lo // 16:hi // 16])
            if lo < HALF:
                nc.vector.tensor_copy(w_listed[:, 3, lo:hi], listed)
            else:
                nc.scalar.activation(w_listed[:, 3, lo:hi], listed, COPY)
        w_q = {}
        w_d = {}
        for b in range(4):
            w_d[b] = keep.tile([P, P, PACK], BF16, name="w_d", tag="w_d%d" % (b if b % 2 else 0), align_bytes=64)
            weave(nc.scalar.copy if b % 2 else nc.vector.tensor_copy, w_d[b][:], w_listed[:, :, b * P:(b + 1) * P])
            if b == 0:
                w_q[0] = quantize(w_d[0][:], "w0", E4M3)
        for b in (1, 2, 3):
            w_q[b] = quantize(w_d[b][:], "w%d" % b, E4M3)

        held = keep.tile([P, HEADS * PACK * SLOTS], F32, name="held", tag="w_d3", align_bytes=64)
        targets = {
            (h, t): held[:, (h * PACK + t) * SLOTS:(h * PACK + t + 1) * SLOTS] for h in range(HEADS) for t in range(PACK)
        }
        for n, (h, t) in enumerate(shared_out):
            nc.gpsimd.tensor_tensor(
                targets[h, t], y_sb[h, t // 2][:, t % 2, :], factors[n], MULT
            )

        warm = bank()
        nc.tensor.transpose(warm[:, 0:P], w_listed[:, 3, 0:2].bitcast(F32).to_broadcast([P, P]), ident[:])
        for width in (SLOTS, HALF):
            nc.tensor.matmul_mx(
                out=warm[:, 0:width], lhsT=xd_q[0][0][:, 0:P].bitcast(E4M3), lhsT_scale=xd_q[0][1][:, 0:P],
                rhs=xd_q[1][0][:, 0:width].bitcast(E4M3), rhs_scale=xd_q[1][1][:, 0:width], start=True, stop=True,
            )

        def own_target(t):
            nc.vector.scalar_tensor_tensor(
                targets[0, t], y_sb[0, t // 2][:, t % 2, :], c2[0][:, t:t + 1], ts_spread[:], MULT, MULT
            )

        scaled = {}
        for h, b in ((h, b) for h in range(HEADS) for b in range(4)):
            a = bank()
            w_codes, w_scales = w_q[b]
            nc.tensor.matmul_mx(
                out=a[:], lhsT=w_codes[:].bitcast(E4M3), lhsT_scale=w_scales[:],
                rhs=xd_q[h][0][:].bitcast(E4M3), rhs_scale=xd_q[h][1][:], start=True, stop=True,
            )
            s = ring.tile([P, PACK, P], F32, name="stage", tag="stage", bufs=8)
            if (h, b) == (0, 2):
                nc.vector.tensor_scalar_mul(s[:], a[:].rearrange("i (t m) -> i t m", t=PACK), ts2_col[:, b:b + 1])
            else:
                nc.scalar.activation(
                    s[:], a[:].rearrange("i (t m) -> i t m", t=PACK), COPY, scale=ts2_col[:, b:b + 1]
                )
            scaled[4 * h + b] = s
        for t in range(PACK - 1):
            own_target(t)
        g_r = [
            keep.tile([P, SLOTS, PACK], BF16, name="g_r", tag="g_r%d" % h, align_bytes=64) for h in range(HEADS)
        ]
        g_q = []
        for h in range(HEADS):
            banks = [ts_bank() if (h, t) == (1, 0) else bank() for t in range(PACK)]
            for t in range(PACK):
                for b in range(4):
                    nc.tensor.transpose(banks[t][:, b * P:(b + 1) * P], scaled[4 * h + b][:, t, :], ident[:])
            planes = keep.tile([P, PACK, SLOTS], BF16, name="g_planes", tag="g_planes%d" % h, align_bytes=64)
            for t in range(PACK):
                for lo, hi in ((0, HALF), (HALF, SLOTS)) if (h, t) == (1, 3) else ((0, SLOTS),):
                    nc.vector.scalar_tensor_tensor(
                        planes[:, t, lo:hi], banks[t][:, lo:hi], c1[h][:, t:t + 1], targets[h, t][:, lo:hi], MULT, SUB
                    )
            if h == 0:
                shares = ((nc.scalar.copy, 0, HALF), (nc.scalar.copy, HALF, SLOTS))
            else:
                shares = (
                    (nc.scalar.copy, 0, P),
                    (nc.vector.tensor_copy, P, HALF),
                    (nc.vector.tensor_copy, HALF, VECTOR_SLOTS),
                    (nc.scalar.copy, VECTOR_SLOTS, SLOTS),
                )
            for copy, lo, hi in shares:
                weave(copy, g_r[h][:, lo:hi, :], planes[:, :, lo:hi])
            codes = keep.tile([P, SLOTS], U32, name="g_codes%d" % h, align_bytes=64)
            scales = keep.tile([P, SLOTS], U8, name="g_scales%d" % h, align_bytes=64)
            for lo in (0, HALF):
                nc.vector.quantize_mx(
                    out=codes[:, lo:lo + HALF].bitcast(E5M2), scales=scales[:, lo:lo + HALF],
                    in_=g_r[h][:, lo:lo + HALF, :].rearrange("p c t -> p (c t)"),
                )
            g_q.append((codes, scales))
        rest_codes = keep.tile([P, D], U32, name="rest_codes", tag="g_r1", align_bytes=64)
        rest_scales = keep.tile([P, D], U8, name="rest_scales", align_bytes=64)
        nc.vector.quantize_mx(out=rest_codes[:].bitcast(E4M3), scales=rest_scales[:], in_=x_r[1])
        xr_rest = (rest_codes, rest_scales)
        windows += [placed.tile([P, TOKENS], F32, name="window%d" % j, offset=4 * TOKENS * j) for j in (3,)]

        chunks = len(CHUNKS)
        starts = [sum(CHUNKS[:k]) for k in range(chunks + 1)]
        out_rows = out_0.rearrange("(p j) c -> p j c", j=PACK)
        units = ((1, 0, HALF), (0, 0, HALF), (1, HALF, SLOTS), (0, HALF, SLOTS), (2, 0, SLOTS), (3, 0, SLOTS))
        accs = [bank() for unit in units]

        def gradient_pass(u, h, start):
            j, lo, hi = units[u]
            first = (j % 2 * HEADS + h) * P
            codes, scales = (t[:, first:first + P] for t in (xr_first if j < 2 else xr_rest))
            nc.tensor.matmul_mx(
                out=accs[u][:, 0:hi - lo], lhsT=codes.bitcast(E4M3), lhsT_scale=scales,
                rhs=g_q[h][0][:, lo:hi].bitcast(E5M2), rhs_scale=g_q[h][1][:, lo:hi],
                start=start, stop=not start,
            )

        for h in range(HEADS):
            for u in range(4):
                gradient_pass(u, h, h == 0)
        for u in (4, 5):
            for h in range(HEADS):
                gradient_pass(u, h, h == 0)
        nc.gpsimd.memset(windows[3][:], 0.0)
        pairs = keep.tile([P, 2 * SPAN * 2], BF16, name="pairs", align_bytes=64)
        shared_first, own_first = 0, TOKENS - OWN_COLUMNS
        for u, (j, lo, hi) in enumerate(units):
            if j == 2:
                dw = pairs[:].bitcast(F32)[:, TOKENS - HALF:TOKENS + HALF]
            elif j == 3:
                dw = pairs[:].bitcast(F32)[:, 2 * TOKENS - 3 * HALF:2 * TOKENS - HALF]
            else:
                dw = ring.tile([P, hi - lo], F32, name="dw", tag="stage", bufs=8)
            if j % 2 == 0:
                nc.vector.tensor_copy(dw[:], accs[u][:, 0:hi - lo])
                nc.vector.tensor_copy(windows[j][:].indirect(offsets[:, lo // 16:hi // 16]), dw[:])
            else:
                nc.scalar.copy(dw[:], accs[u][:, 0:hi - lo])
                for at in range(lo, hi, HALF):
                    nc.scalar.activation(
                        windows[j][:].indirect(offsets[:, at // 16:(at + HALF) // 16]),
                        dw[:, at - lo:at - lo + HALF], COPY,
                    )
            if hi == SLOTS:
                nc.sync.dma_start(out=out_rows[:, j, :], in_=windows[j][:])

        woven = keep.tile([P, TOKENS, PACK], BF16, name="woven", tag="g_r1", align_bytes=64)

        def cast(copy, j, lo, hi):
            if j >= 2:
                first = TOKENS + lo
            elif lo < OWN_COLUMNS:
                first = own_first + lo
            else:
                first = shared_first + lo - OWN_COLUMNS
            copy(pairs[:].rearrange("p (w e) -> p w e", e=2)[:, first:first + hi - lo, j % 2], windows[j][:, lo:hi])

        def weave_words(copy, dtype, lo, hi):
            words = pairs[:].bitcast(dtype)
            if lo < OWN_COLUMNS:
                both = words[:, own_first:own_first + 2 * OWN_COLUMNS].rearrange("p (u c) -> p c u", u=2)[:, lo:hi, :]
            else:
                both = words.rearrange("p (u c) -> p c u", u=2)[:, lo - OWN_COLUMNS:hi - OWN_COLUMNS, :]
            copy(
                woven[:].rearrange("p c t -> p (c t)").bitcast(dtype).rearrange("p (c u) -> p c u", u=2)[:, lo:hi, :],
                both,
            )

        for j in (1, 0):
            cast(nc.gpsimd.tensor_copy, j, OWN_COLUMNS, TOKENS)
        for j in range(PACK):
            cast(nc.vector.tensor_copy, j, 0, OWN_COLUMNS if j < 2 else VECTOR_COLUMNS)
        for lo, hi in ((0, starts[1]), (starts[1], OWN_COLUMNS), (OWN_COLUMNS, VECTOR_COLUMNS)):
            weave_words(nc.vector.tensor_copy, I32, lo, hi)
        for j in (3, 2):
            cast(nc.scalar.copy, j, VECTOR_COLUMNS, starts[3])
        weave_words(nc.scalar.copy, U32, VECTOR_COLUMNS, starts[3])
        for j in (3, 2):
            cast(nc.scalar.copy, j, starts[3], TOKENS)
        for k in range(3, chunks):
            weave_words(nc.scalar.copy, U32, starts[k], starts[k + 1])

        out_words = out_1.rearrange("a p c l -> p (a c l)").bitcast(I32)
        scale_rows = out_2.rearrange("a f c -> (a f) c").bitcast(I32)
        out_scales = keep.tile([P, TOKENS // 2], U8, name="out_scales", align_bytes=64)
        out_codes = keep.tile([P, TOKENS], U32, name="out_codes", align_bytes=64)
        stored = 0
        for k in range(chunks):
            cols = slice(starts[k], starts[k + 1])
            side, at = divmod(starts[k], TOKENS // 2)
            nc.vector.quantize_mx(
                out=out_codes[:, cols].bitcast(E4M3), scales=out_scales[4 * side:, at:at + CHUNKS[k]],
                in_=woven[:, cols, :].rearrange("p c t -> p (c t)"),
            )
            if k in STORE_AFTER:
                cols = slice(stored, starts[k + 1])
                nc.sync.dma_start(out=out_words[:, cols], in_=out_codes[:, cols].bitcast(I32))
                stored = starts[k + 1]
        for quad in range(4):
            nc.sync.dma_start(
                out=scale_rows[4 * quad:4 * quad + 4, :].rearrange("f (a c) -> a f c", a=2),
                in_=out_scales[32 * quad:32 * quad + 8, :].bitcast(I32),
            )
